import numpy as np
import ml_dtypes


def mxq(x, axis, fmt="e4m3"):
    dtype, down = {"e4m3": (ml_dtypes.float8_e4m3fn, 7), "e5m2": (ml_dtypes.float8_e5m2, 14)}[fmt]
    v = np.moveaxis(np.asarray(x, np.float32).astype(ml_dtypes.bfloat16).astype(np.float64), axis, -1)
    blocks = v.reshape(v.shape[:-1] + (-1, 32))
    amax = np.abs(blocks).max(-1, keepdims=True)
    byte = np.maximum(np.where(amax > 0, np.frexp(amax)[1] - 1 + 127, 0) - down, 1)
    scale = np.exp2(byte - 127.0)
    codes = (blocks / scale).astype(np.float32).astype(dtype).astype(np.float64)
    return np.moveaxis((codes * scale).reshape(v.shape), -1, axis)


WIDE = False


def mx_kscale(k):
    if not WIDE:
        return np.ones(k)
    levels = np.array([18, -18])
    if k % 512:
        return np.exp2(np.random.permutation(np.resize(levels, k // 32))).repeat(32)
    a = np.empty((k // 512, 16))
    for p in range(k // 512):
        a[p, :8] = np.random.permutation(np.resize(levels, 8))
        for g in range(8):
            far = levels[np.abs(levels - a[p, g]) >= 10]
            a[p, g + 8] = far[np.random.randint(len(far))]
    return np.exp2(a.ravel()).repeat(32)


def f64(x):
    return np.asarray(x).astype(np.float64)


def striped(idx):
    return np.tile(np.asarray(idx).reshape(-1, 16).T, (8, 1)).astype(np.uint16)


def unstriped(offs):
    return offs[:16].T.reshape(-1).astype(np.int64)


B, N, T, D, R = 1, 512, 2048, 512, 1024


def setup_inputs():
    n = np.random.standard_normal
    idx = np.random.permutation(T)[:B * N]
    s = mx_kscale(D)[:, None]
    z = mx_kscale(R)[:, None]
    x = n((B, D, R))
    teach = np.exp(n((B, R, N)))
    teach = teach / teach.sum(-1, keepdims=True)
    return {
        "xT": (x * s).astype(np.float32),
        "wT": (n((D, T)) * (0.50 / np.sqrt(D)) / s).astype(np.float32),
        "y": teach.astype(np.float32),
        "wt": (np.random.uniform(0.5, 1.5, (B, R, 1)) * N / np.sqrt(R) * z).astype(np.float32),
        "kb": np.tile(0.5 * n(T), (128, 1)).astype(np.float32),
        "xm": (x.transpose(0, 2, 1) / z).astype(np.float32),
        "offs": striped(idx),
    }


def reference(xT, wT, y, wt, kb, xm, offs):
    idx = unstriped(offs)
    pick = lambda x: x[:, idx].reshape(x.shape[0], B, N).transpose(1, 0, 2)
    a = mxq(f64(xT), 1, "e4m3").transpose(0, 2, 1) @ mxq(pick(f64(wT)), 1, "e4m3")
    a = a + pick(f64(kb))[:, :1, :]
    e = np.exp(a - a.max(-1, keepdims=True))
    g = f64(wt) * (e / e.sum(-1, keepdims=True) - f64(y))
    dw = mxq(f64(xm), 1, "e4m3").transpose(0, 2, 1) @ mxq(g, 1, "e5m2")
    gw = np.zeros((D, T))
    gw[:, idx] = dw.transpose(1, 0, 2).reshape(D, B * N)
    return gw

@@ -1,0 +1,229 @@
+from contextlib import ExitStack
+
+import concourse.mybir as mybir
+from concourse.masks import make_identity
+
+N, T, D, R = 512, 2048, 512, 1024
+FLOPS = 2 * 2 * N * D * R
+
+F32 = mybir.dt.float32
+BF16 = mybir.dt.bfloat16
+U32 = mybir.dt.uint32
+U16 = mybir.dt.uint16
+U8 = mybir.dt.uint8
+E4 = mybir.dt.float8_e4m3fn_x4
+E5 = mybir.dt.float8_e5m2_x4
+ALU = mybir.AluOpType
+ACT = mybir.ActivationFunctionType
+
+P = 128
+PACK = 4
+PASS = P * PACK
+HALVES = R // PASS
+BLOCKS = N // P
+OUT_TILES = 3
+
+
+def interleave(engine_copy, dst, src):
+    engine_copy(
+        out=dst.rearrange("p (c i) j -> p c j i", i=4),
+        in_=src.rearrange("p j (c i) -> p c j i", i=4),
+    )
+
+
+def tile_attend_gkl_w_kb_kernel(tc, xT, wT, y, wt, kb, xm, offs, out):
+    nc = tc.nc
+    with ExitStack() as ctx:
+        keep = ctx.enter_context(tc.tile_pool(name="keep", bufs=1))
+        ring = ctx.enter_context(tc.tile_pool(name="ring", bufs=2))
+        psum = ctx.enter_context(tc.psum_pool(name="psum", bufs=1))
+
+        offsets = keep.tile([P, N // 16], U16, name="offsets")
+        nc.sync.dma_start(offsets[:], offs)
+
+        x_raw = [keep.tile([P, PACK, PASS], F32, name=f"x_raw{g}") for g in range(HALVES)]
+        w_raw = [keep.tile([P, T], F32, name=f"w_raw{j}") for j in range(PACK)]
+        y_raw = [keep.tile([P, 2, N], F32, name=f"y_raw{h}") for h in range(2 * HALVES)]
+        m_raw = [keep.tile([P, PACK, D], F32, name=f"m_raw{g}") for g in range(HALVES)]
+        x_rows = xT[0].rearrange("(p j) r -> p j r", j=PACK)
+        w_rows = wT.rearrange("(p j) c -> p j c", j=PACK)
+        nc.sync.dma_start(out=x_raw[0][:], in_=x_rows[:, :, 0:PASS])
+        kb_row = keep.tile([P, T], F32, name="kb_row")
+        nc.vector.memset(kb_row[:], 0.0)
+        weights = keep.tile([P, HALVES, PACK], F32, name="weights")
+        nc.sync.dma_start(out=weights[:], in_=wt[0].rearrange("(g p t) o -> p g (t o)", g=HALVES, t=PACK))
+        nc.sync.dma_start(out=kb_row[0:1, :], in_=kb[0:1, :])
+        for j in range(PACK):
+            nc.sync.dma_start(out=w_raw[j][:], in_=w_rows[:, j, :])
+        nc.sync.dma_start(out=x_raw[1][:], in_=x_rows[:, :, PASS:R])
+        for h in range(2 * HALVES):
+            g, u = divmod(h, 2)
+            y_rows = y[0][g * PASS : (g + 1) * PASS, :].rearrange("(p t) i -> p t i", t=PACK)
+            nc.sync.dma_start(out=y_raw[h][:], in_=y_rows[:, 2 * u : 2 * u + 2, :])
+        for g in range(HALVES):
+            nc.sync.dma_start(
+                out=m_raw[g][:],
+                in_=xm[0][g * PASS : (g + 1) * PASS, :].rearrange("(p t) d -> p t d", t=PACK),
+            )
+
+        ident = keep.tile([P, P], F32, name="ident")
+        make_identity(nc, ident[:])
+        warm = keep.tile([P, 1], F32, name="warm")
+        nc.scalar.activation(out=warm[:], in_=ident[:, 0:1], func=ACT.Exp)
+        windows = [keep.tile([P, T], F32, name=f"window{k}") for k in range(OUT_TILES)]
+        for k in range(OUT_TILES):
+            nc.vector.memset(windows[k][:], 0.0)
+
+        x_bf = [keep.tile([P, PASS, PACK], BF16, name=f"x_bf{g}", align_bytes=64) for g in range(HALVES)]
+        x_codes = [keep.tile([P, PASS], U32, name=f"x_codes{g}", align_bytes=64) for g in range(HALVES)]
+        x_scales = [keep.tile([P, PASS], U8, name=f"x_scales{g}", align_bytes=64) for g in range(HALVES)]
+
+        def quantize(codes, scales, grouped, fmt):
+            nc.vector.quantize_mx(out=codes.bitcast(fmt), scales=scales, in_=grouped.rearrange("p c j -> p (c j)"))
+
+        interleave(nc.scalar.copy, x_bf[0][:], x_raw[0][:])
+        quantize(x_codes[0][:], x_scales[0][:], x_bf[0][:], E4)
+
+        w_bf = keep.tile([P, N, PACK], BF16, name="w_bf", align_bytes=64)
+        w_codes = keep.tile([P, N], U32, name="w_codes", align_bytes=64)
+        w_scales = keep.tile([P, N], U8, name="w_scales", align_bytes=64)
+        nc.vector.tensor_copy(w_bf[:, :, 0], w_raw[0][:].indirect(offsets[:]))
+
+        kb_picked = keep.tile([P, N], F32, name="kb_picked")
+        nc.vector.tensor_copy(kb_picked[:], kb_row[:].indirect(offsets[:]))
+        kb_turned = psum.tile([P, BLOCKS, P], F32, name="kb_turned", tag="scores", bufs=3)
+        for b in range(BLOCKS):
+            nc.tensor.transpose(kb_turned[:, b, :], kb_picked[:, b * P : (b + 1) * P], ident[:])
+        neg_kb = keep.tile([P, BLOCKS], F32, name="neg_kb")
+        nc.scalar.activation(out=neg_kb[:], in_=kb_turned[:, :, 0], func=ACT.Copy, scale=-1.0)
+
+        for j in range(1, PACK - 1):
+            nc.vector.tensor_copy(w_bf[:, :, j], w_raw[j][:].indirect(offsets[:]))
+        for u in range(2):
+            slots = slice(u * N // 2, (u + 1) * N // 2)
+            nc.vector.tensor_copy(w_bf[:, slots, PACK - 1], w_raw[PACK - 1][:].indirect(offsets[:, u * 16 : (u + 1) * 16]))
+            quantize(w_codes[:, slots], w_scales[:, slots], w_bf[:, slots, :], E4)
+
+        neg_at = [
+            [keep.tile([P, PACK, P], F32, name=f"neg_at{g}_{b}") for b in range(BLOCKS)] for g in range(HALVES)
+        ]
+
+        def scores_by_slot(g, b, on_vector):
+            st = psum.tile([P, PASS], F32, name="st", tag="st", bufs=3)
+            slots = slice(b * P, (b + 1) * P)
+            nc.tensor.matmul_mx(
+                out=st[:],
+                lhsT=w_codes[:, slots].bitcast(E4),
+                lhsT_scale=w_scales[:, slots],
+                rhs=x_codes[g][:].bitcast(E4),
+                rhs_scale=x_scales[g][:],
+                start=True,
+                stop=True,
+            )
+            by_place = st[:].rearrange("p (m t) -> p t m", t=PACK)
+            if on_vector:
+                nc.vector.tensor_scalar(
+                    out=neg_at[g][b][:], in0=by_place, scalar1=-1.0, scalar2=neg_kb[:, b : b + 1], op0=ALU.mult, op1=ALU.add
+                )
+            else:
+                nc.scalar.activation(
+                    out=neg_at[g][b][:], in_=by_place, func=ACT.Identity, bias=neg_kb[:, b : b + 1], scale=-1.0
+                )
+
+        neg_max = keep.tile([P, HALVES * PACK], F32, name="neg_max")
+        sums = keep.tile([P, HALVES * PACK], F32, name="sums")
+        inv = keep.tile([P, HALVES * PACK], F32, name="inv")
+        factor = keep.tile([P, HALVES * PACK], F32, name="factor")
+        g_bf = [keep.tile([P, PACK, N], BF16, name=f"g_bf{g}") for g in range(HALVES)]
+        g_grouped = [keep.tile([P, N, PACK], BF16, name=f"g_grouped{g}", align_bytes=64) for g in range(HALVES)]
+        g_codes = [keep.tile([P, N], U32, name=f"g_codes{g}", align_bytes=64) for g in range(HALVES)]
+        g_scales = [keep.tile([P, N], U8, name=f"g_scales{g}", align_bytes=64) for g in range(HALVES)]
+        neg_a = {}
+        e = {}
+
+        def turn_and_max(k):
+            g, t = divmod(k, PACK)
+            neg_a[k] = psum.tile([P, N], F32, name="neg_a", tag="scores", bufs=3)
+            for b in range(BLOCKS):
+                nc.tensor.transpose(neg_a[k][:, b * P : (b + 1) * P], neg_at[g][b][:, t, :], ident[:])
+            nc.vector.tensor_reduce(out=neg_max[:, k : k + 1], in_=neg_a[k][:], axis=mybir.AxisListType.X, op=ALU.min)
+
+        def exponent(k):
+            g, t = divmod(k, PACK)
+            e[k] = ring.tile([P, N], F32, name="e", tag="e", bufs=3)
+            col = slice(k, k + 1)
+            nc.scalar.activation(
+                out=e[k][:], in_=neg_a[k][:], func=ACT.Exp, bias=neg_max[:, col], scale=-1.0, accum_out=sums[:, col]
+            )
+            nc.vector.reciprocal(out=inv[:, col], in_=sums[:, col])
+            nc.vector.tensor_tensor(out=factor[:, col], in0=inv[:, col], in1=weights[:, g, t : t + 1], op=ALU.mult)
+
+        def gradient(k):
+            g, t = divmod(k, PACK)
+            wy = ring.tile([P, N], F32, name="wy", tag="wy")
+            nc.gpsimd.tensor_scalar(
+                out=wy[:], in0=y_raw[k // 2][:, k % 2, :], scalar1=weights[:, g, t : t + 1], scalar2=0.0, op0=ALU.mult, op1=ALU.add
+            )
+            nc.vector.scalar_tensor_tensor(
+                out=g_bf[g][:, t, :], in0=e[k][:], scalar=factor[:, k : k + 1], in1=wy[:], op0=ALU.mult, op1=ALU.subtract
+            )
+
+        def group_g(g, scalar_cols):
+            interleave(nc.scalar.copy, g_grouped[g][:, 0:scalar_cols, :], g_bf[g][:, :, 0:scalar_cols])
+            if scalar_cols < N:
+                interleave(nc.vector.tensor_copy, g_grouped[g][:, scalar_cols:N, :], g_bf[g][:, :, scalar_cols:N])
+            quantize(g_codes[g][:], g_scales[g][:], g_grouped[g][:], E5)
+
+        m_bf = [keep.tile([P, HALVES * P, PACK], BF16, name=f"m_bf{b}", align_bytes=64) for b in range(D // P)]
+        m_codes = [keep.tile([P, HALVES * P], U32, name=f"m_codes{b}", align_bytes=64) for b in range(D // P)]
+        m_scales = [keep.tile([P, HALVES * P], U8, name=f"m_scales{b}", align_bytes=64) for b in range(D // P)]
+
+        def prepare_xm(b):
+            for g in range(HALVES):
+                interleave(nc.scalar.copy, m_bf[b][:, g * P : (g + 1) * P, :], m_raw[g][:, :, b * P : (b + 1) * P])
+            quantize(m_codes[b][:], m_scales[b][:], m_bf[b][:], E4)
+
+        for b in range(BLOCKS):
+            scores_by_slot(0, b, on_vector=(b == 2))
+        interleave(nc.scalar.copy, x_bf[1][:, 0:256, :], x_raw[1][:, :, 0:256])
+        turn_and_max(0)
+        interleave(nc.vector.tensor_copy, x_bf[1][:, 256:PASS, :], x_raw[1][:, :, 256:PASS])
+        tiles = HALVES * PACK
+        for k in range(1, tiles + 2):
+            if k < tiles:
+                turn_and_max(k)
+            if k == 1:
+                quantize(x_codes[1][:], x_scales[1][:], x_bf[1][:], E4)
+            if k <= tiles:
+                exponent(k - 1)
+            if k in (2, 3):
+                scores_by_slot(1, 2 * k - 4, on_vector=False)
+                scores_by_slot(1, 2 * k - 3, on_vector=False)
+            if k >= 2:
+                gradient(k - 2)
+            if k == 6:
+                group_g(0, N)
+            if k == 7:
+                prepare_xm(0)
+        group_g(1, 176)
+
+        for b in range(D // P):
+            dw = psum.tile([P, N], F32, name="dw", tag="dw", bufs=2)
+            for g in range(HALVES):
+                cols = slice(g * P, (g + 1) * P)
+                nc.tensor.matmul_mx(
+                    out=dw[:],
+                    lhsT=m_codes[b][:, cols].bitcast(E4),
+                    lhsT_scale=m_scales[b][:, cols],
+                    rhs=g_codes[g][:].bitcast(E5),
+                    rhs_scale=g_scales[g][:],
+                    start=(g == 0),
+                    stop=(g == HALVES - 1),
+                )
+            dw_sb = ring.tile([P, N], F32, name="dw_sb", tag="dw_sb")
+            nc.scalar.copy(out=dw_sb[:], in_=dw[:])
+            if b + 1 < D // P:
+                prepare_xm(b + 1)
+            window = windows[b % OUT_TILES]
+            nc.vector.tensor_copy(window[:].indirect(offsets[:]), dw_sb[:])
+            nc.sync.dma_start(out=out[b * P : (b + 1) * P, :], in_=window[:])

@@ -19,211 +19,271 @@ ACT = mybir.ActivationFunctionType
 P = 128
 PACK = 4
 PASS = P * PACK
-HALVES = R // PASS
+PASSES = R // PASS
+TILES = PASSES * PACK
 BLOCKS = N // P
-OUT_TILES = 3
+HALF = N // 2
+WINDOWS = 3
+TURNED = (6, 7)
 
 
-def interleave(engine_copy, dst, src):
-    engine_copy(
-        out=dst.rearrange("p (c i) j -> p c j i", i=4),
-        in_=src.rearrange("p j (c i) -> p c j i", i=4),
-    )
+def interleave(copy, dst, src):
+    copy(out=dst.rearrange("p (c i) j -> p c j i", i=4), in_=src.rearrange("p j (c i) -> p c j i", i=4))
 
 
 def tile_attend_gkl_w_kb_kernel(tc, xT, wT, y, wt, kb, xm, offs, out):
     nc = tc.nc
+    on_scalar, on_vector = nc.scalar.copy, nc.vector.tensor_copy
     with ExitStack() as ctx:
         keep = ctx.enter_context(tc.tile_pool(name="keep", bufs=1))
         ring = ctx.enter_context(tc.tile_pool(name="ring", bufs=2))
-        psum = ctx.enter_context(tc.psum_pool(name="psum", bufs=1))
+        psum = ctx.enter_context(tc.psum_pool(name="psum", bufs=4))
 
         offsets = keep.tile([P, N // 16], U16, name="offsets")
         nc.sync.dma_start(offsets[:], offs)
 
-        x_raw = [keep.tile([P, PACK, PASS], F32, name=f"x_raw{g}") for g in range(HALVES)]
         w_raw = [keep.tile([P, T], F32, name=f"w_raw{j}") for j in range(PACK)]
-        y_raw = [keep.tile([P, 2, N], F32, name=f"y_raw{h}") for h in range(2 * HALVES)]
-        m_raw = [keep.tile([P, PACK, D], F32, name=f"m_raw{g}") for g in range(HALVES)]
-        x_rows = xT[0].rearrange("(p j) r -> p j r", j=PACK)
-        w_rows = wT.rearrange("(p j) c -> p j c", j=PACK)
-        nc.sync.dma_start(out=x_raw[0][:], in_=x_rows[:, :, 0:PASS])
+        x_first = [keep.tile([P, PACK, PASS // 2], F32, name=f"x_first{u}") for u in range(2)]
+        x_second = keep.tile([P, PACK, PASS], F32, name="x_second")
+        y_raw = [keep.tile([P, 2, N], F32, name=f"y_raw{h}") for h in range(TILES // 2)]
+        m_raw = [keep.tile([P, PACK, D], F32, name=f"m_raw{g}") for g in range(PASSES)]
         kb_row = keep.tile([P, T], F32, name="kb_row")
+        weights = keep.tile([P, PASSES, PACK], F32, name="weights")
+        w_rows = wT.rearrange("(p j) c -> p j c", j=PACK)
+        x_rows = xT[0].rearrange("(p j) r -> p j r", j=PACK)
+
         nc.vector.memset(kb_row[:], 0.0)
-        weights = keep.tile([P, HALVES, PACK], F32, name="weights")
-        nc.sync.dma_start(out=weights[:], in_=wt[0].rearrange("(g p t) o -> p g (t o)", g=HALVES, t=PACK))
-        nc.sync.dma_start(out=kb_row[0:1, :], in_=kb[0:1, :])
-        for j in range(PACK):
+        nc.sync.dma_start(out=w_raw[0][:], in_=w_rows[:, 0, :])
+        nc.scalar.dma_start(out=kb_row[0:1, :], in_=kb[0:1, :])
+        nc.sync.dma_start(out=weights[:], in_=wt[0].rearrange("(g p t) o -> p g (t o)", g=PASSES, t=PACK))
+        for j in range(1, PACK):
             nc.sync.dma_start(out=w_raw[j][:], in_=w_rows[:, j, :])
-        nc.sync.dma_start(out=x_raw[1][:], in_=x_rows[:, :, PASS:R])
-        for h in range(2 * HALVES):
+        for u in range(2):
+            nc.sync.dma_start(out=x_first[u][:], in_=x_rows[:, :, u * PASS // 2 : (u + 1) * PASS // 2])
+        nc.sync.dma_start(out=x_second[:], in_=x_rows[:, :, PASS:R])
+        for h in range(TILES // 2):
             g, u = divmod(h, 2)
             y_rows = y[0][g * PASS : (g + 1) * PASS, :].rearrange("(p t) i -> p t i", t=PACK)
             nc.sync.dma_start(out=y_raw[h][:], in_=y_rows[:, 2 * u : 2 * u + 2, :])
-        for g in range(HALVES):
-            nc.sync.dma_start(
-                out=m_raw[g][:],
-                in_=xm[0][g * PASS : (g + 1) * PASS, :].rearrange("(p t) d -> p t d", t=PACK),
-            )
+        for g in range(PASSES):
+            m_rows = xm[0][g * PASS : (g + 1) * PASS, :].rearrange("(p t) d -> p t d", t=PACK)
+            nc.sync.dma_start(out=m_raw[g][:], in_=m_rows)
 
         ident = keep.tile([P, P], F32, name="ident")
         make_identity(nc, ident[:])
         warm = keep.tile([P, 1], F32, name="warm")
         nc.scalar.activation(out=warm[:], in_=ident[:, 0:1], func=ACT.Exp)
-        windows = [keep.tile([P, T], F32, name=f"window{k}") for k in range(OUT_TILES)]
-        for k in range(OUT_TILES):
-            nc.vector.memset(windows[k][:], 0.0)
-
-        x_bf = [keep.tile([P, PASS, PACK], BF16, name=f"x_bf{g}", align_bytes=64) for g in range(HALVES)]
-        x_codes = [keep.tile([P, PASS], U32, name=f"x_codes{g}", align_bytes=64) for g in range(HALVES)]
-        x_scales = [keep.tile([P, PASS], U8, name=f"x_scales{g}", align_bytes=64) for g in range(HALVES)]
+        windows = [keep.tile([P, T], F32, name=f"window{k}") for k in range(WINDOWS)]
+        for window in windows[:-1]:
+            nc.vector.memset(window[:], 0.0)
+        nc.gpsimd.memset(windows[-1][:], 0.0)
+        g_codes = [keep.tile([P, N], U32, name=f"g_codes{g}", align_bytes=64) for g in range(PASSES)]
+        g_scales = [keep.tile([P, N], U8, name=f"g_scales{g}", align_bytes=64) for g in range(PASSES)]
+        nc.gpsimd.memset(g_codes[1][:, HALF:N], 0)
+        nc.gpsimd.memset(g_scales[1][:, HALF:N].bitcast(U32), 0)
 
         def quantize(codes, scales, grouped, fmt):
             nc.vector.quantize_mx(out=codes.bitcast(fmt), scales=scales, in_=grouped.rearrange("p c j -> p (c j)"))
 
-        interleave(nc.scalar.copy, x_bf[0][:], x_raw[0][:])
-        quantize(x_codes[0][:], x_scales[0][:], x_bf[0][:], E4)
+        def matmul(acc, lhs_codes, lhs_scales, rhs_codes, rhs_scales, rhs_fmt, start, stop):
+            nc.tensor.matmul_mx(
+                out=acc,
+                lhsT=lhs_codes.bitcast(E4),
+                lhsT_scale=lhs_scales,
+                rhs=rhs_codes.bitcast(rhs_fmt),
+                rhs_scale=rhs_scales,
+                start=start,
+                stop=stop,
+            )
 
         w_bf = keep.tile([P, N, PACK], BF16, name="w_bf", align_bytes=64)
         w_codes = keep.tile([P, N], U32, name="w_codes", align_bytes=64)
         w_scales = keep.tile([P, N], U8, name="w_scales", align_bytes=64)
-        nc.vector.tensor_copy(w_bf[:, :, 0], w_raw[0][:].indirect(offsets[:]))
+        w_pair = keep.tile([P, 2, N], F32, name="w_pair")
+        nc.vector.tensor_copy(w_pair[:, 0, :], w_raw[0][:].indirect(offsets[:]))
 
         kb_picked = keep.tile([P, N], F32, name="kb_picked")
         nc.vector.tensor_copy(kb_picked[:], kb_row[:].indirect(offsets[:]))
-        kb_turned = psum.tile([P, BLOCKS, P], F32, name="kb_turned", tag="scores", bufs=3)
+        kb_turned = psum.tile([P, BLOCKS, P], F32, name="kb_turned", tag="side")
         for b in range(BLOCKS):
             nc.tensor.transpose(kb_turned[:, b, :], kb_picked[:, b * P : (b + 1) * P], ident[:])
-        neg_kb = keep.tile([P, BLOCKS], F32, name="neg_kb")
-        nc.scalar.activation(out=neg_kb[:], in_=kb_turned[:, :, 0], func=ACT.Copy, scale=-1.0)
+        neg_kb_col = keep.tile([P, BLOCKS], F32, name="neg_kb_col")
+        nc.scalar.activation(out=neg_kb_col[:], in_=kb_turned[:, :, 0], func=ACT.Copy, scale=-1.0)
+        kb_spread = psum.tile([P, N], F32, name="kb_spread", tag="side")
+        for b in range(BLOCKS):
+            nc.tensor.transpose(kb_spread[:, b * P : (b + 1) * P], neg_kb_col[:, b : b + 1].to_broadcast([P, P]), ident[:])
+        neg_kb = keep.tile([P, N], F32, name="neg_kb")
+        nc.scalar.copy(out=neg_kb[:], in_=kb_spread[:])
 
-        for j in range(1, PACK - 1):
+        nc.vector.tensor_copy(w_pair[:, 1, :], w_raw[1][:].indirect(offsets[:]))
+        nc.scalar.copy(out=w_bf[:, :, 0:2], in_=w_pair[:].rearrange("p j c -> p c j"))
+        for j in range(2, PACK):
             nc.vector.tensor_copy(w_bf[:, :, j], w_raw[j][:].indirect(offsets[:]))
-        for u in range(2):
-            slots = slice(u * N // 2, (u + 1) * N // 2)
-            nc.vector.tensor_copy(w_bf[:, slots, PACK - 1], w_raw[PACK - 1][:].indirect(offsets[:, u * 16 : (u + 1) * 16]))
-            quantize(w_codes[:, slots], w_scales[:, slots], w_bf[:, slots, :], E4)
+        quantize(w_codes[:], w_scales[:], w_bf[:], E4)
 
-        neg_at = [
-            [keep.tile([P, PACK, P], F32, name=f"neg_at{g}_{b}") for b in range(BLOCKS)] for g in range(HALVES)
-        ]
+        x_bf = [keep.tile([P, PACK, P, PACK], BF16, name=f"x_bf{g}", align_bytes=64) for g in range(PASSES)]
+        x_codes = [keep.tile([P, PASS], U32, name=f"x_codes{g}", align_bytes=64) for g in range(PASSES)]
+        x_scales = [keep.tile([P, PASS], U8, name=f"x_scales{g}", align_bytes=64) for g in range(PASSES)]
 
-        def scores_by_slot(g, b, on_vector):
-            st = psum.tile([P, PASS], F32, name="st", tag="st", bufs=3)
-            slots = slice(b * P, (b + 1) * P)
-            nc.tensor.matmul_mx(
-                out=st[:],
-                lhsT=w_codes[:, slots].bitcast(E4),
-                lhsT_scale=w_scales[:, slots],
-                rhs=x_codes[g][:].bitcast(E4),
-                rhs_scale=x_scales[g][:],
-                start=True,
-                stop=True,
+        def cast_x(copy, g, m0, m1, raw, raw_m0):
+            copy(
+                out=x_bf[g][:, :, m0:m1, :].rearrange("p t m j -> p m t j"),
+                in_=raw[:, :, PACK * (m0 - raw_m0) : PACK * (m1 - raw_m0)].rearrange("p j (m t) -> p m t j", t=PACK),
             )
-            by_place = st[:].rearrange("p (m t) -> p t m", t=PACK)
-            if on_vector:
-                nc.vector.tensor_scalar(
-                    out=neg_at[g][b][:], in0=by_place, scalar1=-1.0, scalar2=neg_kb[:, b : b + 1], op0=ALU.mult, op1=ALU.add
-                )
-            else:
-                nc.scalar.activation(
-                    out=neg_at[g][b][:], in_=by_place, func=ACT.Identity, bias=neg_kb[:, b : b + 1], scale=-1.0
-                )
 
-        neg_max = keep.tile([P, HALVES * PACK], F32, name="neg_max")
-        sums = keep.tile([P, HALVES * PACK], F32, name="sums")
-        inv = keep.tile([P, HALVES * PACK], F32, name="inv")
-        factor = keep.tile([P, HALVES * PACK], F32, name="factor")
-        g_bf = [keep.tile([P, PACK, N], BF16, name=f"g_bf{g}") for g in range(HALVES)]
-        g_grouped = [keep.tile([P, N, PACK], BF16, name=f"g_grouped{g}", align_bytes=64) for g in range(HALVES)]
-        g_codes = [keep.tile([P, N], U32, name=f"g_codes{g}", align_bytes=64) for g in range(HALVES)]
-        g_scales = [keep.tile([P, N], U8, name=f"g_scales{g}", align_bytes=64) for g in range(HALVES)]
+        def quantize_x(g, t0, t1):
+            cols = slice(t0 * P, t1 * P)
+            quantize(x_codes[g][:, cols], x_scales[g][:, cols], x_bf[g][:, t0:t1].rearrange("p t m j -> p (t m) j"), E4)
+
+        cast_x(on_scalar, 0, 0, 64, x_first[0], 0)
+        cast_x(on_scalar, 0, 64, 76, x_first[1], 64)
+        cast_x(on_vector, 0, 76, P, x_first[1], 64)
+        for t in range(PACK):
+            quantize_x(0, t, t + 1)
+        for m0 in range(0, 96, 32):
+            cast_x(on_scalar, 1, m0, m0 + 32, x_second, 0)
+        cast_x(on_vector, 1, 96, P, x_second, 0)
+        quantize_x(1, 2, 4)
+        quantize_x(1, 0, 2)
+
+        wy = [keep.tile([P, N], F32, name=f"wy{k}") for k in range(TILES)]
+
+        def weigh_targets():
+            for k in range(TILES):
+                g, t = divmod(k, PACK)
+                targets, weight = y_raw[k // 2][:, k % 2, :], weights[:, g, t : t + 1]
+                if k in TURNED:
+                    nc.vector.tensor_scalar(out=wy[k][:], in0=targets, scalar1=weight, scalar2=None, op0=ALU.mult)
+                else:
+                    nc.scalar.activation(out=wy[k][:], in_=targets, func=ACT.Copy, scale=weight)
+
+        neg_max = keep.tile([P, TILES], F32, name="neg_max")
+        sums = keep.tile([P, TILES], F32, name="sums")
+        inv = keep.tile([P, TILES], F32, name="inv")
+        factor = keep.tile([P, TILES], F32, name="factor")
+        e = [keep.tile([P, N], F32, name=f"e{k}") for k in range(TILES)]
         neg_a = {}
-        e = {}
 
-        def turn_and_max(k):
+        def scores(k):
             g, t = divmod(k, PACK)
-            neg_a[k] = psum.tile([P, N], F32, name="neg_a", tag="scores", bufs=3)
+            rows = slice(t * P, (t + 1) * P)
+            raw = psum.tile([P, N], F32, name="raw", tag="scores")
+            matmul(raw[:], x_codes[g][:, rows], x_scales[g][:, rows], w_codes[:], w_scales[:], E4, True, True)
+            neg_a[k] = keep.tile([P, N], F32, name=f"neg_a{k}")
+            nc.vector.scalar_tensor_tensor(out=neg_a[k][:], in0=raw[:], scalar=-1.0, in1=neg_kb[:], op0=ALU.mult, op1=ALU.add)
+
+        neg_at = keep.tile([P, BLOCKS, 2 * P], F32, name="neg_at")
+
+        def scores_by_slot():
+            rows = slice(2 * P, 4 * P)
+            for u in range(2):
+                raw = psum.tile([P, 2, 2 * P], F32, name="raw_t", tag="side")
+                for v in range(2):
+                    slots = slice((2 * u + v) * P, (2 * u + v + 1) * P)
+                    matmul(raw[:, v, :], w_codes[:, slots], w_scales[:, slots], x_codes[1][:, rows], x_scales[1][:, rows], E4, True, True)
+                for v in range(2):
+                    b = 2 * u + v
+                    nc.scalar.activation(
+                        out=neg_at[:, b, :], in_=raw[:, v, :], func=ACT.Identity, bias=neg_kb_col[:, b : b + 1], scale=-1.0
+                    )
+
+        def turn(k):
+            rows = slice((k - TURNED[0]) * P, (k - TURNED[0] + 1) * P)
+            neg_a[k] = psum.tile([P, N], F32, name="turned", tag="scores")
             for b in range(BLOCKS):
-                nc.tensor.transpose(neg_a[k][:, b * P : (b + 1) * P], neg_at[g][b][:, t, :], ident[:])
-            nc.vector.tensor_reduce(out=neg_max[:, k : k + 1], in_=neg_a[k][:], axis=mybir.AxisListType.X, op=ALU.min)
+                nc.tensor.transpose(neg_a[k][:, b * P : (b + 1) * P], neg_at[:, b, rows], ident[:])
 
         def exponent(k):
-            g, t = divmod(k, PACK)
-            e[k] = ring.tile([P, N], F32, name="e", tag="e", bufs=3)
             col = slice(k, k + 1)
+            nc.vector.tensor_reduce(out=neg_max[:, col], in_=neg_a[k][:], axis=mybir.AxisListType.X, op=ALU.min)
             nc.scalar.activation(
                 out=e[k][:], in_=neg_a[k][:], func=ACT.Exp, bias=neg_max[:, col], scale=-1.0, accum_out=sums[:, col]
             )
-            nc.vector.reciprocal(out=inv[:, col], in_=sums[:, col])
-            nc.vector.tensor_tensor(out=factor[:, col], in0=inv[:, col], in1=weights[:, g, t : t + 1], op=ALU.mult)
 
-        def gradient(k):
-            g, t = divmod(k, PACK)
-            wy = ring.tile([P, N], F32, name="wy", tag="wy")
-            nc.gpsimd.tensor_scalar(
-                out=wy[:], in0=y_raw[k // 2][:, k % 2, :], scalar1=weights[:, g, t : t + 1], scalar2=0.0, op0=ALU.mult, op1=ALU.add
-            )
-            nc.vector.scalar_tensor_tensor(
-                out=g_bf[g][:, t, :], in0=e[k][:], scalar=factor[:, k : k + 1], in1=wy[:], op0=ALU.mult, op1=ALU.subtract
-            )
+        def factors(g):
+            cols = slice(g * PACK, (g + 1) * PACK)
+            nc.vector.reciprocal(out=inv[:, cols], in_=sums[:, cols])
+            nc.vector.tensor_tensor(out=factor[:, cols], in0=inv[:, cols], in1=weights[:, g, :], op=ALU.mult)
 
-        def group_g(g, scalar_cols):
-            interleave(nc.scalar.copy, g_grouped[g][:, 0:scalar_cols, :], g_bf[g][:, :, 0:scalar_cols])
-            if scalar_cols < N:
-                interleave(nc.vector.tensor_copy, g_grouped[g][:, scalar_cols:N, :], g_bf[g][:, :, scalar_cols:N])
-            quantize(g_codes[g][:], g_scales[g][:], g_grouped[g][:], E5)
+        g_bf = [keep.tile([P, PACK, N], BF16, name=f"g_bf{g}") for g in range(PASSES)]
+        g_grouped = [keep.tile([P, N, PACK], BF16, name=f"g_grouped{g}", align_bytes=64) for g in range(PASSES)]
 
-        m_bf = [keep.tile([P, HALVES * P, PACK], BF16, name=f"m_bf{b}", align_bytes=64) for b in range(D // P)]
-        m_codes = [keep.tile([P, HALVES * P], U32, name=f"m_codes{b}", align_bytes=64) for b in range(D // P)]
-        m_scales = [keep.tile([P, HALVES * P], U8, name=f"m_scales{b}", align_bytes=64) for b in range(D // P)]
-
-        def prepare_xm(b):
-            for g in range(HALVES):
-                interleave(nc.scalar.copy, m_bf[b][:, g * P : (g + 1) * P, :], m_raw[g][:, :, b * P : (b + 1) * P])
-            quantize(m_codes[b][:], m_scales[b][:], m_bf[b][:], E4)
-
-        for b in range(BLOCKS):
-            scores_by_slot(0, b, on_vector=(b == 2))
-        interleave(nc.scalar.copy, x_bf[1][:, 0:256, :], x_raw[1][:, :, 0:256])
-        turn_and_max(0)
-        interleave(nc.vector.tensor_copy, x_bf[1][:, 256:PASS, :], x_raw[1][:, :, 256:PASS])
-        tiles = HALVES * PACK
-        for k in range(1, tiles + 2):
-            if k < tiles:
-                turn_and_max(k)
-            if k == 1:
-                quantize(x_codes[1][:], x_scales[1][:], x_bf[1][:], E4)
-            if k <= tiles:
-                exponent(k - 1)
-            if k in (2, 3):
-                scores_by_slot(1, 2 * k - 4, on_vector=False)
-                scores_by_slot(1, 2 * k - 3, on_vector=False)
-            if k >= 2:
-                gradient(k - 2)
-            if k == 6:
-                group_g(0, N)
-            if k == 7:
-                prepare_xm(0)
-        group_g(1, 176)
-
-        for b in range(D // P):
-            dw = psum.tile([P, N], F32, name="dw", tag="dw", bufs=2)
-            for g in range(HALVES):
-                cols = slice(g * P, (g + 1) * P)
-                nc.tensor.matmul_mx(
-                    out=dw[:],
-                    lhsT=m_codes[b][:, cols].bitcast(E4),
-                    lhsT_scale=m_scales[b][:, cols],
-                    rhs=g_codes[g][:].bitcast(E5),
-                    rhs_scale=g_scales[g][:],
-                    start=(g == 0),
-                    stop=(g == HALVES - 1),
+        def gradient(g, s0, s1, copies):
+            for t in range(PACK):
+                k = g * PACK + t
+                nc.vector.scalar_tensor_tensor(
+                    out=g_bf[g][:, t, s0:s1],
+                    in0=e[k][:, s0:s1],
+                    scalar=factor[:, k : k + 1],
+                    in1=wy[k][:, s0:s1],
+                    op0=ALU.mult,
+                    op1=ALU.subtract,
                 )
-            dw_sb = ring.tile([P, N], F32, name="dw_sb", tag="dw_sb")
-            nc.scalar.copy(out=dw_sb[:], in_=dw[:])
-            if b + 1 < D // P:
-                prepare_xm(b + 1)
-            window = windows[b % OUT_TILES]
-            nc.vector.tensor_copy(window[:].indirect(offsets[:]), dw_sb[:])
-            nc.sync.dma_start(out=out[b * P : (b + 1) * P, :], in_=window[:])
+            for n, copy in enumerate(copies):
+                slots = slice(s0 + n * P, s0 + (n + 1) * P)
+                interleave(copy, g_grouped[g][:, slots, :], g_bf[g][:, :, slots])
+
+        def quantize_g(g, s0, s1):
+            quantize(g_codes[g][:, s0:s1], g_scales[g][:, s0:s1], g_grouped[g][:, s0:s1, :], E5)
+
+        m_codes = [keep.tile([P, PASSES * P], U32, name=f"m_codes{b}", align_bytes=64) for b in range(D // P)]
+        m_scales = [keep.tile([P, PASSES * P], U8, name=f"m_scales{b}", align_bytes=64) for b in range(D // P)]
+
+        def prepare_xm(b, copies):
+            m_bf = ring.tile([P, PASSES * P, PACK], BF16, name="m_bf", align_bytes=64)
+            for g, copy in enumerate(copies):
+                interleave(copy, m_bf[:, g * P : (g + 1) * P, :], m_raw[g][:, :, b * P : (b + 1) * P])
+            quantize(m_codes[b][:], m_scales[b][:], m_bf[:], E4)
+
+        dw_sb = {}
+
+        def product(b, s0, s1):
+            dw = psum.tile([P, N], F32, name="dw", tag="side")
+            for g in range(PASSES):
+                cols = slice(g * P, (g + 1) * P)
+                matmul(dw[:], m_codes[b][:, cols], m_scales[b][:, cols], g_codes[g][:], g_scales[g][:], E5, g == 0, g == PASSES - 1)
+            dw_sb[b, s0] = keep.tile([P, s1 - s0], F32, name=f"dw_sb{b}_{s0}")
+            nc.scalar.copy(out=dw_sb[b, s0][:], in_=dw[:, s0:s1])
+
+        def scatter(b, s0, s1):
+            window = windows[b % WINDOWS]
+            nc.vector.tensor_copy(window[:].indirect(offsets[:, s0 // 16 : s1 // 16]), dw_sb[b, s0][:])
+            if s1 == N:
+                nc.sync.dma_start(out=out[b * P : (b + 1) * P, :], in_=window[:])
+
+        for pair in range(TILES // 2):
+            if pair == 2:
+                scores_by_slot()
+                weigh_targets()
+            if pair == 3:
+                factors(0)
+            for k in (2 * pair, 2 * pair + 1):
+                if k in TURNED:
+                    turn(k)
+                else:
+                    scores(k)
+            for k in (2 * pair, 2 * pair + 1):
+                exponent(k)
+        factors(1)
+        gradient(0, 0, N, (on_scalar, on_scalar, on_scalar, on_vector))
+        gradient(1, 0, HALF, (on_scalar, on_vector))
+        quantize_g(0, 0, N)
+        prepare_xm(0, (on_scalar, on_vector))
+        prepare_xm(1, (on_scalar, on_vector))
+        quantize_g(1, 0, HALF)
+        product(0, 0, HALF)
+        product(1, 0, HALF)
+        gradient(1, HALF, N, (on_scalar, on_scalar))
+        quantize_g(1, HALF, N)
+        scatter(0, 0, HALF)
+        prepare_xm(2, (on_scalar, on_scalar))
+        prepare_xm(3, (on_scalar, on_scalar))
+        product(0, HALF, N)
+        product(1, HALF, N)
+        scatter(1, 0, HALF)
+        scatter(0, HALF, N)
+        scatter(1, HALF, N)
+        for b in range(2, D // P):
+            product(b, 0, N)
+        for b in range(2, D // P):
+            scatter(b, 0, N)

@@ -53,10 +53,11 @@ def tile_attend_gkl_w_kb_kernel(tc, xT, wT, y, wt, kb, xm, offs, out):
         x_rows = xT[0].rearrange("(p j) r -> p j r", j=PACK)
 
         nc.vector.memset(kb_row[:], 0.0)
-        nc.sync.dma_start(out=w_raw[0][:], in_=w_rows[:, 0, :])
-        nc.scalar.dma_start(out=kb_row[0:1, :], in_=kb[0:1, :])
+        for j in range(2):
+            nc.sync.dma_start(out=w_raw[j][:], in_=w_rows[:, j, :])
+        nc.sync.dma_start(out=kb_row[0:1, :], in_=kb[0:1, :])
         nc.sync.dma_start(out=weights[:], in_=wt[0].rearrange("(g p t) o -> p g (t o)", g=PASSES, t=PACK))
-        for j in range(1, PACK):
+        for j in range(2, PACK):
             nc.sync.dma_start(out=w_raw[j][:], in_=w_rows[:, j, :])
         for u in range(2):
             nc.sync.dma_start(out=x_first[u][:], in_=x_rows[:, :, u * PASS // 2 : (u + 1) * PASS // 2])
@@ -76,11 +77,11 @@ def tile_attend_gkl_w_kb_kernel(tc, xT, wT, y, wt, kb, xm, offs, out):
         windows = [keep.tile([P, T], F32, name=f"window{k}") for k in range(WINDOWS)]
         for window in windows[:-1]:
             nc.vector.memset(window[:], 0.0)
-        nc.gpsimd.memset(windows[-1][:], 0.0)
         g_codes = [keep.tile([P, N], U32, name=f"g_codes{g}", align_bytes=64) for g in range(PASSES)]
         g_scales = [keep.tile([P, N], U8, name=f"g_scales{g}", align_bytes=64) for g in range(PASSES)]
         nc.gpsimd.memset(g_codes[1][:, HALF:N], 0)
         nc.gpsimd.memset(g_scales[1][:, HALF:N].bitcast(U32), 0)
+        nc.gpsimd.memset(windows[-1][:], 0.0)
 
         def quantize(codes, scales, grouped, fmt):
             nc.vector.quantize_mx(out=codes.bitcast(fmt), scales=scales, in_=grouped.rearrange("p c j -> p (c j)"))
@@ -101,6 +102,8 @@ def tile_attend_gkl_w_kb_kernel(tc, xT, wT, y, wt, kb, xm, offs, out):
         w_scales = keep.tile([P, N], U8, name="w_scales", align_bytes=64)
         w_pair = keep.tile([P, 2, N], F32, name="w_pair")
         nc.vector.tensor_copy(w_pair[:, 0, :], w_raw[0][:].indirect(offsets[:]))
+        nc.vector.tensor_copy(w_pair[:, 1, :], w_raw[1][:].indirect(offsets[:]))
+        nc.scalar.copy(out=w_bf[:, :, 0:2], in_=w_pair[:].rearrange("p j c -> p c j"))
 
         kb_picked = keep.tile([P, N], F32, name="kb_picked")
         nc.vector.tensor_copy(kb_picked[:], kb_row[:].indirect(offsets[:]))
@@ -112,11 +115,7 @@ def tile_attend_gkl_w_kb_kernel(tc, xT, wT, y, wt, kb, xm, offs, out):
         kb_spread = psum.tile([P, N], F32, name="kb_spread", tag="side")
         for b in range(BLOCKS):
             nc.tensor.transpose(kb_spread[:, b * P : (b + 1) * P], neg_kb_col[:, b : b + 1].to_broadcast([P, P]), ident[:])
-        neg_kb = keep.tile([P, N], F32, name="neg_kb")
-        nc.scalar.copy(out=neg_kb[:], in_=kb_spread[:])
 
-        nc.vector.tensor_copy(w_pair[:, 1, :], w_raw[1][:].indirect(offsets[:]))
-        nc.scalar.copy(out=w_bf[:, :, 0:2], in_=w_pair[:].rearrange("p j c -> p c j"))
         for j in range(2, PACK):
             nc.vector.tensor_copy(w_bf[:, :, j], w_raw[j][:].indirect(offsets[:]))
         quantize(w_codes[:], w_scales[:], w_bf[:], E4)
@@ -140,6 +139,8 @@ def tile_attend_gkl_w_kb_kernel(tc, xT, wT, y, wt, kb, xm, offs, out):
         cast_x(on_vector, 0, 76, P, x_first[1], 64)
         for t in range(PACK):
             quantize_x(0, t, t + 1)
+        neg_kb = keep.tile([P, N], F32, name="neg_kb")
+        nc.scalar.copy(out=neg_kb[:], in_=kb_spread[:])
         for m0 in range(0, 96, 32):
             cast_x(on_scalar, 1, m0, m0 + 32, x_second, 0)
         cast_x(on_vector, 1, 96, P, x_second, 0)

@@ -9,6 +9,7 @@ FLOPS = 2 * 2 * N * D * R
 F32 = mybir.dt.float32
 BF16 = mybir.dt.bfloat16
 U32 = mybir.dt.uint32
+I32 = mybir.dt.int32
 U16 = mybir.dt.uint16
 U8 = mybir.dt.uint8
 E4 = mybir.dt.float8_e4m3fn_x4
@@ -24,7 +25,6 @@ TILES = PASSES * PACK
 BLOCKS = N // P
 HALF = N // 2
 WINDOWS = 3
-TURNED = (6, 7)
 
 
 def interleave(copy, dst, src):
@@ -43,8 +43,7 @@ def tile_attend_gkl_w_kb_kernel(tc, xT, wT, y, wt, kb, xm, offs, out):
         nc.sync.dma_start(offsets[:], offs)
 
         w_raw = [keep.tile([P, T], F32, name=f"w_raw{j}") for j in range(PACK)]
-        x_first = [keep.tile([P, PACK, PASS // 2], F32, name=f"x_first{u}") for u in range(2)]
-        x_second = keep.tile([P, PACK, PASS], F32, name="x_second")
+        x_raw = [keep.tile([P, PACK, PASS], F32, name=f"x_raw{g}") for g in range(PASSES)]
         y_raw = [keep.tile([P, 2, N], F32, name=f"y_raw{h}") for h in range(TILES // 2)]
         m_raw = [keep.tile([P, PACK, D], F32, name=f"m_raw{g}") for g in range(PASSES)]
         kb_row = keep.tile([P, T], F32, name="kb_row")
@@ -52,16 +51,15 @@ def tile_attend_gkl_w_kb_kernel(tc, xT, wT, y, wt, kb, xm, offs, out):
         w_rows = wT.rearrange("(p j) c -> p j c", j=PACK)
         x_rows = xT[0].rearrange("(p j) r -> p j r", j=PACK)
 
-        nc.vector.memset(kb_row[:], 0.0)
+        nc.vector.memset(kb_row[:].bitcast(I32), 0)
         for j in range(2):
             nc.sync.dma_start(out=w_raw[j][:], in_=w_rows[:, j, :])
         nc.sync.dma_start(out=kb_row[0:1, :], in_=kb[0:1, :])
         nc.sync.dma_start(out=weights[:], in_=wt[0].rearrange("(g p t) o -> p g (t o)", g=PASSES, t=PACK))
         for j in range(2, PACK):
             nc.sync.dma_start(out=w_raw[j][:], in_=w_rows[:, j, :])
-        for u in range(2):
-            nc.sync.dma_start(out=x_first[u][:], in_=x_rows[:, :, u * PASS // 2 : (u + 1) * PASS // 2])
-        nc.sync.dma_start(out=x_second[:], in_=x_rows[:, :, PASS:R])
+        for g in range(PASSES):
+            nc.sync.dma_start(out=x_raw[g][:], in_=x_rows[:, :, g * PASS : (g + 1) * PASS])
         for h in range(TILES // 2):
             g, u = divmod(h, 2)
             y_rows = y[0][g * PASS : (g + 1) * PASS, :].rearrange("(p t) i -> p t i", t=PACK)
@@ -76,12 +74,12 @@ def tile_attend_gkl_w_kb_kernel(tc, xT, wT, y, wt, kb, xm, offs, out):
         nc.scalar.activation(out=warm[:], in_=ident[:, 0:1], func=ACT.Exp)
         windows = [keep.tile([P, T], F32, name=f"window{k}") for k in range(WINDOWS)]
         for window in windows[:-1]:
-            nc.vector.memset(window[:], 0.0)
+            nc.vector.memset(window[:].bitcast(I32), 0)
         g_codes = [keep.tile([P, N], U32, name=f"g_codes{g}", align_bytes=64) for g in range(PASSES)]
         g_scales = [keep.tile([P, N], U8, name=f"g_scales{g}", align_bytes=64) for g in range(PASSES)]
         nc.gpsimd.memset(g_codes[1][:, HALF:N], 0)
         nc.gpsimd.memset(g_scales[1][:, HALF:N].bitcast(U32), 0)
-        nc.gpsimd.memset(windows[-1][:], 0.0)
+        nc.gpsimd.memset(windows[-1][:].bitcast(I32), 0)
 
         def quantize(codes, scales, grouped, fmt):
             nc.vector.quantize_mx(out=codes.bitcast(fmt), scales=scales, in_=grouped.rearrange("p c j -> p (c j)"))
@@ -120,40 +118,29 @@ def tile_attend_gkl_w_kb_kernel(tc, xT, wT, y, wt, kb, xm, offs, out):
             nc.vector.tensor_copy(w_bf[:, :, j], w_raw[j][:].indirect(offsets[:]))
         quantize(w_codes[:], w_scales[:], w_bf[:], E4)
 
-        x_bf = [keep.tile([P, PACK, P, PACK], BF16, name=f"x_bf{g}", align_bytes=64) for g in range(PASSES)]
+        x_bf = [keep.tile([P, PASS, PACK], BF16, name=f"x_bf{g}", align_bytes=64) for g in range(PASSES)]
         x_codes = [keep.tile([P, PASS], U32, name=f"x_codes{g}", align_bytes=64) for g in range(PASSES)]
         x_scales = [keep.tile([P, PASS], U8, name=f"x_scales{g}", align_bytes=64) for g in range(PASSES)]
 
-        def cast_x(copy, g, m0, m1, raw, raw_m0):
-            copy(
-                out=x_bf[g][:, :, m0:m1, :].rearrange("p t m j -> p m t j"),
-                in_=raw[:, :, PACK * (m0 - raw_m0) : PACK * (m1 - raw_m0)].rearrange("p j (m t) -> p m t j", t=PACK),
-            )
-
-        def quantize_x(g, t0, t1):
-            cols = slice(t0 * P, t1 * P)
-            quantize(x_codes[g][:, cols], x_scales[g][:, cols], x_bf[g][:, t0:t1].rearrange("p t m j -> p (t m) j"), E4)
-
-        cast_x(on_scalar, 0, 0, 64, x_first[0], 0)
-        cast_x(on_scalar, 0, 64, 76, x_first[1], 64)
-        cast_x(on_vector, 0, 76, P, x_first[1], 64)
-        for t in range(PACK):
-            quantize_x(0, t, t + 1)
+        x_by_place = x_raw[0][:].rearrange("p j (m t) -> p t m j", t=PACK)
+        for t, copy in enumerate((on_vector, on_scalar, on_scalar, on_vector)):
+            cols = slice(t * P, (t + 1) * P)
+            copy(out=x_bf[0][:, cols, :], in_=x_by_place[:, t])
+            quantize(x_codes[0][:, cols], x_scales[0][:, cols], x_bf[0][:, cols, :], E4)
         neg_kb = keep.tile([P, N], F32, name="neg_kb")
         nc.scalar.copy(out=neg_kb[:], in_=kb_spread[:])
-        for m0 in range(0, 96, 32):
-            cast_x(on_scalar, 1, m0, m0 + 32, x_second, 0)
-        cast_x(on_vector, 1, 96, P, x_second, 0)
-        quantize_x(1, 2, 4)
-        quantize_x(1, 0, 2)
+        for n, copy in enumerate((on_scalar, on_scalar, on_vector, on_vector)):
+            cols = slice(n * P, (n + 1) * P)
+            interleave(copy, x_bf[1][:, cols, :], x_raw[1][:, :, cols])
+        quantize(x_codes[1][:], x_scales[1][:], x_bf[1][:], E4)
 
         wy = [keep.tile([P, N], F32, name=f"wy{k}") for k in range(TILES)]
 
-        def weigh_targets():
-            for k in range(TILES):
-                g, t = divmod(k, PACK)
+        def weigh_targets(g):
+            for t in range(PACK):
+                k = g * PACK + t
                 targets, weight = y_raw[k // 2][:, k % 2, :], weights[:, g, t : t + 1]
-                if k in TURNED:
+                if t >= 2:
                     nc.vector.tensor_scalar(out=wy[k][:], in0=targets, scalar1=weight, scalar2=None, op0=ALU.mult)
                 else:
                     nc.scalar.activation(out=wy[k][:], in_=targets, func=ACT.Copy, scale=weight)
@@ -173,26 +160,25 @@ def tile_attend_gkl_w_kb_kernel(tc, xT, wT, y, wt, kb, xm, offs, out):
             neg_a[k] = keep.tile([P, N], F32, name=f"neg_a{k}")
             nc.vector.scalar_tensor_tensor(out=neg_a[k][:], in0=raw[:], scalar=-1.0, in1=neg_kb[:], op0=ALU.mult, op1=ALU.add)
 
-        neg_at = keep.tile([P, BLOCKS, 2 * P], F32, name="neg_at")
+        neg_at = [keep.tile([P, PACK, P], F32, name=f"neg_at{b}") for b in range(BLOCKS)]
 
         def scores_by_slot():
-            rows = slice(2 * P, 4 * P)
-            for u in range(2):
-                raw = psum.tile([P, 2, 2 * P], F32, name="raw_t", tag="side")
-                for v in range(2):
-                    slots = slice((2 * u + v) * P, (2 * u + v + 1) * P)
-                    matmul(raw[:, v, :], w_codes[:, slots], w_scales[:, slots], x_codes[1][:, rows], x_scales[1][:, rows], E4, True, True)
-                for v in range(2):
-                    b = 2 * u + v
-                    nc.scalar.activation(
-                        out=neg_at[:, b, :], in_=raw[:, v, :], func=ACT.Identity, bias=neg_kb_col[:, b : b + 1], scale=-1.0
-                    )
+            for b in range(BLOCKS):
+                slots = slice(b * P, (b + 1) * P)
+                raw = psum.tile([P, PASS], F32, name="raw_t", tag="side")
+                matmul(raw[:], w_codes[:, slots], w_scales[:, slots], x_codes[1][:], x_scales[1][:], E4, True, True)
+                nc.scalar.activation(
+                    out=neg_at[b][:],
+                    in_=raw[:].rearrange("p (m t) -> p t m", t=PACK),
+                    func=ACT.Identity,
+                    bias=neg_kb_col[:, b : b + 1],
+                    scale=-1.0,
+                )
 
         def turn(k):
-            rows = slice((k - TURNED[0]) * P, (k - TURNED[0] + 1) * P)
             neg_a[k] = psum.tile([P, N], F32, name="turned", tag="scores")
             for b in range(BLOCKS):
-                nc.tensor.transpose(neg_a[k][:, b * P : (b + 1) * P], neg_at[:, b, rows], ident[:])
+                nc.tensor.transpose(neg_a[k][:, b * P : (b + 1) * P], neg_at[b][:, k % PACK, :], ident[:])
 
         def exponent(k):
             col = slice(k, k + 1)
@@ -252,36 +238,37 @@ def tile_attend_gkl_w_kb_kernel(tc, xT, wT, y, wt, kb, xm, offs, out):
             if s1 == N:
                 nc.sync.dma_start(out=out[b * P : (b + 1) * P, :], in_=window[:])
 
-        for pair in range(TILES // 2):
-            if pair == 2:
-                scores_by_slot()
-                weigh_targets()
-            if pair == 3:
-                factors(0)
-            for k in (2 * pair, 2 * pair + 1):
-                if k in TURNED:
-                    turn(k)
-                else:
-                    scores(k)
-            for k in (2 * pair, 2 * pair + 1):
-                exponent(k)
+        def softmax_tiles(g, make_scores):
+            for pair in range(2):
+                ks = (g * PACK + 2 * pair, g * PACK + 2 * pair + 1)
+                for k in ks:
+                    make_scores(k)
+                for k in ks:
+                    exponent(k)
+
+        scores_by_slot()
+        softmax_tiles(0, scores)
+        weigh_targets(0)
+        factors(0)
+        gradient(0, 0, N, (on_scalar, on_scalar, on_vector, on_vector))
+        softmax_tiles(1, turn)
+        weigh_targets(1)
         factors(1)
-        gradient(0, 0, N, (on_scalar, on_scalar, on_scalar, on_vector))
         gradient(1, 0, HALF, (on_scalar, on_vector))
-        quantize_g(0, 0, N)
         prepare_xm(0, (on_scalar, on_vector))
-        prepare_xm(1, (on_scalar, on_vector))
+        quantize_g(0, 0, N)
         quantize_g(1, 0, HALF)
+        prepare_xm(1, (on_scalar, on_vector))
         product(0, 0, HALF)
         product(1, 0, HALF)
-        gradient(1, HALF, N, (on_scalar, on_scalar))
-        quantize_g(1, HALF, N)
         scatter(0, 0, HALF)
+        gradient(1, HALF, N, (on_scalar, on_scalar))
         prepare_xm(2, (on_scalar, on_scalar))
-        prepare_xm(3, (on_scalar, on_scalar))
+        quantize_g(1, HALF, N)
         product(0, HALF, N)
         product(1, HALF, N)
         scatter(1, 0, HALF)
+        prepare_xm(3, (on_scalar, on_scalar))
         scatter(0, HALF, N)
         scatter(1, HALF, N)
         for b in range(2, D // P):

@@ -24,7 +24,6 @@ PASSES = R // PASS
 TILES = PASSES * PACK
 BLOCKS = N // P
 HALF = N // 2
-WINDOWS = 3
 
 
 def interleave(copy, dst, src):
@@ -36,7 +35,6 @@ def tile_attend_gkl_w_kb_kernel(tc, xT, wT, y, wt, kb, xm, offs, out):
     on_scalar, on_vector = nc.scalar.copy, nc.vector.tensor_copy
     with ExitStack() as ctx:
         keep = ctx.enter_context(tc.tile_pool(name="keep", bufs=1))
-        ring = ctx.enter_context(tc.tile_pool(name="ring", bufs=2))
         psum = ctx.enter_context(tc.psum_pool(name="psum", bufs=4))
 
         offsets = keep.tile([P, N // 16], U16, name="offsets")
@@ -44,8 +42,8 @@ def tile_attend_gkl_w_kb_kernel(tc, xT, wT, y, wt, kb, xm, offs, out):
 
         w_raw = [keep.tile([P, T], F32, name=f"w_raw{j}") for j in range(PACK)]
         x_raw = [keep.tile([P, PACK, PASS], F32, name=f"x_raw{g}") for g in range(PASSES)]
-        y_raw = [keep.tile([P, 2, N], F32, name=f"y_raw{h}") for h in range(TILES // 2)]
-        m_raw = [keep.tile([P, PACK, D], F32, name=f"m_raw{g}") for g in range(PASSES)]
+        y_raw = [keep.tile([P, PACK, N], F32, name=f"y_raw{g}") for g in range(PASSES)]
+        m_raw = [keep.tile([P, PACK, D], F32, name=f"m_raw{g}", tag=f"w_raw{g}") for g in range(PASSES)]
         kb_row = keep.tile([P, T], F32, name="kb_row")
         weights = keep.tile([P, PASSES, PACK], F32, name="weights")
         w_rows = wT.rearrange("(p j) c -> p j c", j=PACK)
@@ -55,31 +53,29 @@ def tile_attend_gkl_w_kb_kernel(tc, xT, wT, y, wt, kb, xm, offs, out):
         for j in range(2):
             nc.sync.dma_start(out=w_raw[j][:], in_=w_rows[:, j, :])
         nc.sync.dma_start(out=kb_row[0:1, :], in_=kb[0:1, :])
-        nc.sync.dma_start(out=weights[:], in_=wt[0].rearrange("(g p t) o -> p g (t o)", g=PASSES, t=PACK))
         for j in range(2, PACK):
             nc.sync.dma_start(out=w_raw[j][:], in_=w_rows[:, j, :])
         for g in range(PASSES):
             nc.sync.dma_start(out=x_raw[g][:], in_=x_rows[:, :, g * PASS : (g + 1) * PASS])
-        for h in range(TILES // 2):
-            g, u = divmod(h, 2)
-            y_rows = y[0][g * PASS : (g + 1) * PASS, :].rearrange("(p t) i -> p t i", t=PACK)
-            nc.sync.dma_start(out=y_raw[h][:], in_=y_rows[:, 2 * u : 2 * u + 2, :])
+        nc.sync.dma_start(out=weights[:], in_=wt[0].rearrange("(g p t) o -> p g (t o)", g=PASSES, t=PACK))
         for g in range(PASSES):
-            m_rows = xm[0][g * PASS : (g + 1) * PASS, :].rearrange("(p t) d -> p t d", t=PACK)
-            nc.sync.dma_start(out=m_raw[g][:], in_=m_rows)
+            nc.sync.dma_start(out=y_raw[g][:], in_=y[0][g * PASS : (g + 1) * PASS, :].rearrange("(p t) i -> p t i", t=PACK))
+        for g in range(PASSES):
+            nc.sync.dma_start(out=m_raw[g][:], in_=xm[0][g * PASS : (g + 1) * PASS, :].rearrange("(p t) d -> p t d", t=PACK))
 
         ident = keep.tile([P, P], F32, name="ident")
         make_identity(nc, ident[:])
         warm = keep.tile([P, 1], F32, name="warm")
         nc.scalar.activation(out=warm[:], in_=ident[:, 0:1], func=ACT.Exp)
-        windows = [keep.tile([P, T], F32, name=f"window{k}") for k in range(WINDOWS)]
-        for window in windows[:-1]:
-            nc.vector.memset(window[:].bitcast(I32), 0)
-        g_codes = [keep.tile([P, N], U32, name=f"g_codes{g}", align_bytes=64) for g in range(PASSES)]
-        g_scales = [keep.tile([P, N], U8, name=f"g_scales{g}", align_bytes=64) for g in range(PASSES)]
-        nc.gpsimd.memset(g_codes[1][:, HALF:N], 0)
-        nc.gpsimd.memset(g_scales[1][:, HALF:N].bitcast(U32), 0)
-        nc.gpsimd.memset(windows[-1][:].bitcast(I32), 0)
+        windows = [keep.tile([P, T], F32, name=f"window{k}") for k in range(D // P)]
+        nc.vector.memset(windows[0][:].bitcast(I32), 0)
+        g_codes = [keep.tile([P, HALF + N], U32, name=f"g_codes{g}", align_bytes=64) for g in range(PASSES)]
+        g_scales = [keep.tile([P, HALF + N], U8, name=f"g_scales{g}", align_bytes=64) for g in range(PASSES)]
+        for g in range(PASSES):
+            nc.gpsimd.memset(g_codes[g][:, 0:HALF], 0)
+            nc.gpsimd.memset(g_scales[g][:, 0:HALF].bitcast(U32), 0)
+        for window in windows[1:]:
+            nc.gpsimd.memset(window[:].bitcast(I32), 0)
 
         def quantize(codes, scales, grouped, fmt):
             nc.vector.quantize_mx(out=codes.bitcast(fmt), scales=scales, in_=grouped.rearrange("p c j -> p (c j)"))
@@ -108,11 +104,14 @@ def tile_attend_gkl_w_kb_kernel(tc, xT, wT, y, wt, kb, xm, offs, out):
         kb_turned = psum.tile([P, BLOCKS, P], F32, name="kb_turned", tag="side")
         for b in range(BLOCKS):
             nc.tensor.transpose(kb_turned[:, b, :], kb_picked[:, b * P : (b + 1) * P], ident[:])
-        neg_kb_col = keep.tile([P, BLOCKS], F32, name="neg_kb_col")
-        nc.scalar.activation(out=neg_kb_col[:], in_=kb_turned[:, :, 0], func=ACT.Copy, scale=-1.0)
+        kb_col = keep.tile([P, BLOCKS], F32, name="kb_col")
+        nc.scalar.copy(out=kb_col[:], in_=kb_turned[:, :, 0])
+
         kb_spread = psum.tile([P, N], F32, name="kb_spread", tag="side")
         for b in range(BLOCKS):
-            nc.tensor.transpose(kb_spread[:, b * P : (b + 1) * P], neg_kb_col[:, b : b + 1].to_broadcast([P, P]), ident[:])
+            nc.tensor.transpose(kb_spread[:, b * P : (b + 1) * P], kb_col[:, b : b + 1].to_broadcast([P, P]), ident[:])
+        kb_all = keep.tile([P, N], F32, name="kb_all")
+        nc.scalar.copy(out=kb_all[:], in_=kb_spread[:])
 
         for j in range(2, PACK):
             nc.vector.tensor_copy(w_bf[:, :, j], w_raw[j][:].indirect(offsets[:]))
@@ -122,152 +121,194 @@ def tile_attend_gkl_w_kb_kernel(tc, xT, wT, y, wt, kb, xm, offs, out):
         x_codes = [keep.tile([P, PASS], U32, name=f"x_codes{g}", align_bytes=64) for g in range(PASSES)]
         x_scales = [keep.tile([P, PASS], U8, name=f"x_scales{g}", align_bytes=64) for g in range(PASSES)]
 
-        x_by_place = x_raw[0][:].rearrange("p j (m t) -> p t m j", t=PACK)
-        for t, copy in enumerate((on_vector, on_scalar, on_scalar, on_vector)):
-            cols = slice(t * P, (t + 1) * P)
-            copy(out=x_bf[0][:, cols, :], in_=x_by_place[:, t])
-            quantize(x_codes[0][:, cols], x_scales[0][:, cols], x_bf[0][:, cols, :], E4)
-        neg_kb = keep.tile([P, N], F32, name="neg_kb")
-        nc.scalar.copy(out=neg_kb[:], in_=kb_spread[:])
-        for n, copy in enumerate((on_scalar, on_scalar, on_vector, on_vector)):
-            cols = slice(n * P, (n + 1) * P)
-            interleave(copy, x_bf[1][:, cols, :], x_raw[1][:, :, cols])
-        quantize(x_codes[1][:], x_scales[1][:], x_bf[1][:], E4)
+        def prepare_x(g, shares):
+            c0 = 0
+            for copy, width in shares:
+                interleave(copy, x_bf[g][:, c0 : c0 + width, :], x_raw[g][:, :, c0 : c0 + width])
+                c0 = c0 + width
+            quantize(x_codes[g][:], x_scales[g][:], x_bf[g][:], E4)
 
         wy = [keep.tile([P, N], F32, name=f"wy{k}") for k in range(TILES)]
 
-        def weigh_targets(g):
+        def weigh_targets(g, s0, s1, on_vector_from):
             for t in range(PACK):
                 k = g * PACK + t
-                targets, weight = y_raw[k // 2][:, k % 2, :], weights[:, g, t : t + 1]
-                if t >= 2:
-                    nc.vector.tensor_scalar(out=wy[k][:], in0=targets, scalar1=weight, scalar2=None, op0=ALU.mult)
+                targets, weight = y_raw[g][:, t, s0:s1], weights[:, g, t : t + 1]
+                if on_vector_from < 0:
+                    nc.gpsimd.tensor_scalar(out=wy[k][:, s0:s1], in0=targets, scalar1=weight, scalar2=0.0, op0=ALU.mult, op1=ALU.add)
+                elif t >= on_vector_from:
+                    nc.vector.tensor_scalar(out=wy[k][:, s0:s1], in0=targets, scalar1=weight, scalar2=None, op0=ALU.mult)
                 else:
-                    nc.scalar.activation(out=wy[k][:], in_=targets, func=ACT.Copy, scale=weight)
+                    nc.scalar.activation(out=wy[k][:, s0:s1], in_=targets, func=ACT.Copy, scale=weight)
 
         neg_max = keep.tile([P, TILES], F32, name="neg_max")
         sums = keep.tile([P, TILES], F32, name="sums")
         inv = keep.tile([P, TILES], F32, name="inv")
         factor = keep.tile([P, TILES], F32, name="factor")
         e = [keep.tile([P, N], F32, name=f"e{k}") for k in range(TILES)]
-        neg_a = {}
+        by_slot = [[keep.tile([P, PACK, P], F32, name=f"by_slot{g}_{b}") for b in range(BLOCKS)] for g in range(PASSES)]
 
-        def scores(k):
-            g, t = divmod(k, PACK)
-            rows = slice(t * P, (t + 1) * P)
-            raw = psum.tile([P, N], F32, name="raw", tag="scores")
-            matmul(raw[:], x_codes[g][:, rows], x_scales[g][:, rows], w_codes[:], w_scales[:], E4, True, True)
-            neg_a[k] = keep.tile([P, N], F32, name=f"neg_a{k}")
-            nc.vector.scalar_tensor_tensor(out=neg_a[k][:], in0=raw[:], scalar=-1.0, in1=neg_kb[:], op0=ALU.mult, op1=ALU.add)
-
-        neg_at = [keep.tile([P, PACK, P], F32, name=f"neg_at{b}") for b in range(BLOCKS)]
-
-        def scores_by_slot():
+        def scores(g, pieces):
+            raw = []
             for b in range(BLOCKS):
                 slots = slice(b * P, (b + 1) * P)
-                raw = psum.tile([P, PASS], F32, name="raw_t", tag="side")
-                matmul(raw[:], w_codes[:, slots], w_scales[:, slots], x_codes[1][:], x_scales[1][:], E4, True, True)
-                nc.scalar.activation(
-                    out=neg_at[b][:],
-                    in_=raw[:].rearrange("p (m t) -> p t m", t=PACK),
-                    func=ACT.Identity,
-                    bias=neg_kb_col[:, b : b + 1],
-                    scale=-1.0,
-                )
+                raw.append(psum.tile([P, PASS], F32, name="raw", tag="side"))
+                matmul(raw[b][:], w_codes[:, slots], w_scales[:, slots], x_codes[g][:], x_scales[g][:], E4, True, True)
+            width = PACK // pieces
+            for u in range(pieces):
+                places = slice(u * width, (u + 1) * width)
+                for b in range(BLOCKS):
+                    nc.scalar.activation(
+                        out=by_slot[g][b][:, places, :],
+                        in_=raw[b][:].rearrange("p (m t) -> p t m", t=PACK)[:, places, :],
+                        func=ACT.Identity,
+                        bias=kb_col[:, b : b + 1],
+                        scale=1.0,
+                    )
 
-        def turn(k):
-            neg_a[k] = psum.tile([P, N], F32, name="turned", tag="scores")
+        turned = {}
+
+        def row_max(k):
+            g, t = divmod(k, PACK)
+            col = slice(k, k + 1)
+            a = psum.tile([P, N], F32, name="turned", tag=("scores", "side")[g])
+            turned[k] = a
             for b in range(BLOCKS):
-                nc.tensor.transpose(neg_a[k][:, b * P : (b + 1) * P], neg_at[b][:, k % PACK, :], ident[:])
+                nc.tensor.transpose(a[:, b * P : (b + 1) * P], by_slot[g][b][:, t, :], ident[:])
+            nc.vector.tensor_reduce(out=neg_max[:, col], in_=a[:], axis=mybir.AxisListType.X, op=ALU.max, negate=True)
+
+        def prepare_pair(g, u, copy, by_row):
+            cols = slice(u * HALF, (u + 1) * HALF)
+            pair = x_raw[g][:].rearrange("p j (m u e) -> p u m j e", u=2, e=2)[:, u]
+            copy(out=x_bf[g][:, cols, :].rearrange("p (e m) j -> p m j e" if by_row else "p (m e) j -> p m j e", e=2), in_=pair)
+            quantize(x_codes[g][:, cols], x_scales[g][:, cols], x_bf[g][:, cols, :], E4)
+
+        def scores_by_row(k):
+            g, t = divmod(k, PACK)
+            rows = slice(t * P, (t + 1) * P)
+            raw = psum.tile([P, N], F32, name="raw_rows", tag="scores")
+            matmul(raw[:], x_codes[g][:, rows], x_scales[g][:, rows], w_codes[:], w_scales[:], E4, True, True)
+            turned[k] = keep.tile([P, N], F32, name=f"a{k}")
+            nc.vector.tensor_tensor(out=turned[k][:], in0=raw[:], in1=kb_all[:], op=ALU.add)
+
+        def max_by_row(k):
+            nc.vector.tensor_reduce(out=neg_max[:, k : k + 1], in_=turned[k][:], axis=mybir.AxisListType.X, op=ALU.max, negate=True)
+
+        def half_scores(g):
+            for b in range(BLOCKS):
+                slots = slice(b * P, (b + 1) * P)
+                raw = psum.tile([P, HALF], F32, name="raw_half", tag="side")
+                matmul(raw[:], w_codes[:, slots], w_scales[:, slots], x_codes[g][:, HALF:N], x_scales[g][:, HALF:N], E4, True, True)
+                nc.scalar.activation(
+                    out=by_slot[g][b][:, 2:PACK, :],
+                    in_=raw[:].rearrange("p (m e) -> p e m", e=2),
+                    func=ACT.Identity,
+                    bias=kb_col[:, b : b + 1],
+                    scale=1.0,
+                )
 
         def exponent(k):
             col = slice(k, k + 1)
-            nc.vector.tensor_reduce(out=neg_max[:, col], in_=neg_a[k][:], axis=mybir.AxisListType.X, op=ALU.min)
-            nc.scalar.activation(
-                out=e[k][:], in_=neg_a[k][:], func=ACT.Exp, bias=neg_max[:, col], scale=-1.0, accum_out=sums[:, col]
-            )
+            nc.scalar.activation(out=e[k][:], in_=turned[k][:], func=ACT.Exp, bias=neg_max[:, col], scale=1.0, accum_out=sums[:, col])
 
-        def factors(g):
-            cols = slice(g * PACK, (g + 1) * PACK)
+        def factors(k0, k1):
+            cols = slice(k0, k1)
             nc.vector.reciprocal(out=inv[:, cols], in_=sums[:, cols])
-            nc.vector.tensor_tensor(out=factor[:, cols], in0=inv[:, cols], in1=weights[:, g, :], op=ALU.mult)
+            nc.vector.tensor_tensor(out=factor[:, cols], in0=inv[:, cols], in1=weights[:].rearrange("p g t -> p (g t)")[:, cols], op=ALU.mult)
 
-        g_bf = [keep.tile([P, PACK, N], BF16, name=f"g_bf{g}") for g in range(PASSES)]
+        g_bf = {(g, s0): keep.tile([P, PACK, HALF], BF16, name=f"g_bf{g}_{s0}") for g in range(PASSES) for s0 in (0, HALF)}
         g_grouped = [keep.tile([P, N, PACK], BF16, name=f"g_grouped{g}", align_bytes=64) for g in range(PASSES)]
 
-        def gradient(g, s0, s1, copies):
-            for t in range(PACK):
-                k = g * PACK + t
+        def gradient(ks, s0, s1):
+            for k in ks:
+                g, t = divmod(k, PACK)
                 nc.vector.scalar_tensor_tensor(
-                    out=g_bf[g][:, t, s0:s1],
+                    out=g_bf[g, s0][:, t, :],
                     in0=e[k][:, s0:s1],
                     scalar=factor[:, k : k + 1],
                     in1=wy[k][:, s0:s1],
                     op0=ALU.mult,
                     op1=ALU.subtract,
                 )
-            for n, copy in enumerate(copies):
-                slots = slice(s0 + n * P, s0 + (n + 1) * P)
-                interleave(copy, g_grouped[g][:, slots, :], g_bf[g][:, :, slots])
+
+        def group_g(g, s0, shares):
+            c0 = 0
+            for copy, width in shares:
+                interleave(copy, g_grouped[g][:, s0 + c0 : s0 + c0 + width, :], g_bf[g, s0][:, :, c0 : c0 + width])
+                c0 = c0 + width
 
         def quantize_g(g, s0, s1):
-            quantize(g_codes[g][:, s0:s1], g_scales[g][:, s0:s1], g_grouped[g][:, s0:s1, :], E5)
+            cols = slice(HALF + s0, HALF + s1)
+            quantize(g_codes[g][:, cols], g_scales[g][:, cols], g_grouped[g][:, s0:s1, :], E5)
 
+        m_bf = [keep.tile([P, PASSES * P, PACK], BF16, name=f"m_bf{b}", align_bytes=64) for b in range(D // P)]
         m_codes = [keep.tile([P, PASSES * P], U32, name=f"m_codes{b}", align_bytes=64) for b in range(D // P)]
         m_scales = [keep.tile([P, PASSES * P], U8, name=f"m_scales{b}", align_bytes=64) for b in range(D // P)]
 
         def prepare_xm(b, copies):
-            m_bf = ring.tile([P, PASSES * P, PACK], BF16, name="m_bf", align_bytes=64)
             for g, copy in enumerate(copies):
-                interleave(copy, m_bf[:, g * P : (g + 1) * P, :], m_raw[g][:, :, b * P : (b + 1) * P])
-            quantize(m_codes[b][:], m_scales[b][:], m_bf[:], E4)
+                interleave(copy, m_bf[b][:, g * P : (g + 1) * P, :], m_raw[g][:, :, b * P : (b + 1) * P])
+            quantize(m_codes[b][:], m_scales[b][:], m_bf[b][:], E4)
 
         dw_sb = {}
 
         def product(b, s0, s1):
             dw = psum.tile([P, N], F32, name="dw", tag="side")
+            first = HALF + s1 - N
+            moving = slice(first, first + N)
             for g in range(PASSES):
                 cols = slice(g * P, (g + 1) * P)
-                matmul(dw[:], m_codes[b][:, cols], m_scales[b][:, cols], g_codes[g][:], g_scales[g][:], E5, g == 0, g == PASSES - 1)
-            dw_sb[b, s0] = keep.tile([P, s1 - s0], F32, name=f"dw_sb{b}_{s0}")
-            nc.scalar.copy(out=dw_sb[b, s0][:], in_=dw[:, s0:s1])
+                matmul(dw[:], m_codes[b][:, cols], m_scales[b][:, cols], g_codes[g][:, moving], g_scales[g][:, moving], E5, g == 0, g == PASSES - 1)
+            dw_sb[b, s0] = keep.tile([P, s1 - s0], F32, name=f"dw_sb{b}_{s0}", tag=f"g_bf1_{HALF}" if (b, s1) == (1, HALF) else f"dw_sb{b}_{s0}")
+            nc.scalar.copy(out=dw_sb[b, s0][:], in_=dw[:, N - (s1 - s0) : N])
 
         def scatter(b, s0, s1):
-            window = windows[b % WINDOWS]
-            nc.vector.tensor_copy(window[:].indirect(offsets[:, s0 // 16 : s1 // 16]), dw_sb[b, s0][:])
+            nc.vector.tensor_copy(windows[b][:].indirect(offsets[:, s0 // 16 : s1 // 16]), dw_sb[b, s0][:])
             if s1 == N:
-                nc.sync.dma_start(out=out[b * P : (b + 1) * P, :], in_=window[:])
+                nc.sync.dma_start(out=out[b * P : (b + 1) * P, :], in_=windows[b][:])
 
-        def softmax_tiles(g, make_scores):
-            for pair in range(2):
-                ks = (g * PACK + 2 * pair, g * PACK + 2 * pair + 1)
-                for k in ks:
-                    make_scores(k)
-                for k in ks:
-                    exponent(k)
-
-        scores_by_slot()
-        softmax_tiles(0, scores)
-        weigh_targets(0)
-        factors(0)
-        gradient(0, 0, N, (on_scalar, on_scalar, on_vector, on_vector))
-        softmax_tiles(1, turn)
-        weigh_targets(1)
-        factors(1)
-        gradient(1, 0, HALF, (on_scalar, on_vector))
-        prepare_xm(0, (on_scalar, on_vector))
-        quantize_g(0, 0, N)
+        prepare_pair(0, 0, on_vector, True)
+        prepare_pair(0, 1, on_scalar, False)
+        prepare_pair(1, 1, on_vector, False)
+        prepare_pair(1, 0, on_scalar, True)
+        scores_by_row(0)
+        scores_by_row(1)
+        half_scores(0)
+        half_scores(1)
+        for k in range(TILES):
+            if k == 2:
+                scores_by_row(4)
+                scores_by_row(5)
+            if k % PACK < 2:
+                max_by_row(k)
+            else:
+                row_max(k)
+        for k in range(TILES):
+            exponent(k)
+        weigh_targets(0, 0, N, -1)
+        weigh_targets(1, 0, N, -1)
+        for k in range(0, TILES, 2):
+            factors(k, k + 2)
+        gradient(range(TILES), 0, HALF)
+        group_g(0, 0, ((on_scalar, 256),))
+        group_g(1, 0, ((on_scalar, 128), (on_vector, 128)))
+        quantize_g(0, 0, HALF)
         quantize_g(1, 0, HALF)
-        prepare_xm(1, (on_scalar, on_vector))
+        prepare_xm(0, (on_scalar, on_scalar))
         product(0, 0, HALF)
+        gradient(range(PACK), HALF, N)
+        prepare_xm(1, (on_scalar, on_scalar))
+        group_g(0, HALF, ((on_scalar, HALF),))
+        gradient(range(PACK, TILES), HALF, N)
+        group_g(1, HALF, ((on_scalar, HALF),))
         product(1, 0, HALF)
         scatter(0, 0, HALF)
-        gradient(1, HALF, N, (on_scalar, on_scalar))
-        prepare_xm(2, (on_scalar, on_scalar))
+        quantize_g(0, HALF, N)
         quantize_g(1, HALF, N)
+        prepare_xm(2, (on_scalar, on_scalar))
+        scatter(1, 0, HALF)
         product(0, HALF, N)
         product(1, HALF, N)
-        scatter(1, 0, HALF)
         prepare_xm(3, (on_scalar, on_scalar))
         scatter(0, HALF, N)
         scatter(1, HALF, N)

@@ -24,6 +24,7 @@ PASSES = R // PASS
 TILES = PASSES * PACK
 BLOCKS = N // P
 HALF = N // 2
+WINDOWS = 3
 
 
 def interleave(copy, dst, src):
@@ -38,20 +39,20 @@ def tile_attend_gkl_w_kb_kernel(tc, xT, wT, y, wt, kb, xm, offs, out):
         psum = ctx.enter_context(tc.psum_pool(name="psum", bufs=4))
 
         offsets = keep.tile([P, N // 16], U16, name="offsets")
-        nc.sync.dma_start(offsets[:], offs)
 
-        w_raw = [keep.tile([P, T], F32, name=f"w_raw{j}") for j in range(PACK)]
+        w_raw = [keep.tile([P, T], F32, name=f"w_raw{j}", align_bytes=64) for j in range(PACK)]
         x_raw = [keep.tile([P, PACK, PASS], F32, name=f"x_raw{g}") for g in range(PASSES)]
         y_raw = [keep.tile([P, PACK, N], F32, name=f"y_raw{g}") for g in range(PASSES)]
-        m_raw = [keep.tile([P, PACK, D], F32, name=f"m_raw{g}", tag=f"w_raw{g}") for g in range(PASSES)]
+        m_raw = [keep.tile([P, PACK, D], F32, name=f"m_raw{g}", tag=f"w_raw{g}", align_bytes=64) for g in range(PASSES)]
         kb_row = keep.tile([P, T], F32, name="kb_row")
         weights = keep.tile([P, PASSES, PACK], F32, name="weights")
         w_rows = wT.rearrange("(p j) c -> p j c", j=PACK)
         x_rows = xT[0].rearrange("(p j) r -> p j r", j=PACK)
 
         nc.vector.memset(kb_row[:].bitcast(I32), 0)
-        for j in range(2):
-            nc.sync.dma_start(out=w_raw[j][:], in_=w_rows[:, j, :])
+        nc.sync.dma_start(out=w_raw[0][:], in_=w_rows[:, 0, :])
+        nc.sync.dma_start(offsets[:], offs)
+        nc.sync.dma_start(out=w_raw[1][:], in_=w_rows[:, 1, :])
         nc.sync.dma_start(out=kb_row[0:1, :], in_=kb[0:1, :])
         for j in range(2, PACK):
             nc.sync.dma_start(out=w_raw[j][:], in_=w_rows[:, j, :])
@@ -67,7 +68,7 @@ def tile_attend_gkl_w_kb_kernel(tc, xT, wT, y, wt, kb, xm, offs, out):
         make_identity(nc, ident[:])
         warm = keep.tile([P, 1], F32, name="warm")
         nc.scalar.activation(out=warm[:], in_=ident[:, 0:1], func=ACT.Exp)
-        windows = [keep.tile([P, T], F32, name=f"window{k}") for k in range(D // P)]
+        windows = [keep.tile([P, T], F32, name=f"window{k}") for k in range(WINDOWS)]
         nc.vector.memset(windows[0][:].bitcast(I32), 0)
         g_codes = [keep.tile([P, HALF + N], U32, name=f"g_codes{g}", align_bytes=64) for g in range(PASSES)]
         g_scales = [keep.tile([P, HALF + N], U8, name=f"g_scales{g}", align_bytes=64) for g in range(PASSES)]
@@ -128,23 +129,24 @@ def tile_attend_gkl_w_kb_kernel(tc, xT, wT, y, wt, kb, xm, offs, out):
                 c0 = c0 + width
             quantize(x_codes[g][:], x_scales[g][:], x_bf[g][:], E4)
 
-        wy = [keep.tile([P, N], F32, name=f"wy{k}") for k in range(TILES)]
+        wy = {}
 
         def weigh_targets(g, s0, s1, on_vector_from):
+            wy[g] = keep.tile([P, PACK, N], F32, name=f"wy{g}", tag=("x_bf1", "wy1")[g], align_bytes=64)
             for t in range(PACK):
                 k = g * PACK + t
                 targets, weight = y_raw[g][:, t, s0:s1], weights[:, g, t : t + 1]
                 if on_vector_from < 0:
-                    nc.gpsimd.tensor_scalar(out=wy[k][:, s0:s1], in0=targets, scalar1=weight, scalar2=0.0, op0=ALU.mult, op1=ALU.add)
+                    nc.gpsimd.tensor_scalar(out=wy[g][:, t, s0:s1], in0=targets, scalar1=weight, scalar2=0.0, op0=ALU.mult, op1=ALU.add)
                 elif t >= on_vector_from:
-                    nc.vector.tensor_scalar(out=wy[k][:, s0:s1], in0=targets, scalar1=weight, scalar2=None, op0=ALU.mult)
+                    nc.vector.tensor_scalar(out=wy[g][:, t, s0:s1], in0=targets, scalar1=weight, scalar2=None, op0=ALU.mult)
                 else:
-                    nc.scalar.activation(out=wy[k][:, s0:s1], in_=targets, func=ACT.Copy, scale=weight)
+                    nc.scalar.activation(out=wy[g][:, t, s0:s1], in_=targets, func=ACT.Copy, scale=weight)
 
         neg_max = keep.tile([P, TILES], F32, name="neg_max")
-        sums = keep.tile([P, TILES], F32, name="sums")
-        inv = keep.tile([P, TILES], F32, name="inv")
-        factor = keep.tile([P, TILES], F32, name="factor")
+        sums = [keep.tile([P, PACK], F32, name=f"sums{g}") for g in range(PASSES)]
+        inv = [keep.tile([P, PACK], F32, name=f"inv{g}") for g in range(PASSES)]
+        factor = [keep.tile([P, PACK], F32, name=f"factor{g}") for g in range(PASSES)]
         e = [keep.tile([P, N], F32, name=f"e{k}") for k in range(TILES)]
         by_slot = [[keep.tile([P, PACK, P], F32, name=f"by_slot{g}_{b}") for b in range(BLOCKS)] for g in range(PASSES)]
 
@@ -177,18 +179,27 @@ def tile_attend_gkl_w_kb_kernel(tc, xT, wT, y, wt, kb, xm, offs, out):
                 nc.tensor.transpose(a[:, b * P : (b + 1) * P], by_slot[g][b][:, t, :], ident[:])
             nc.vector.tensor_reduce(out=neg_max[:, col], in_=a[:], axis=mybir.AxisListType.X, op=ALU.max, negate=True)
 
-        def prepare_pair(g, u, copy, by_row):
+        def on_gpsimd(out, in_):
+            nc.gpsimd.tensor_scalar(out=out, in0=in_, scalar1=1.0, scalar2=0.0, op0=ALU.mult, op1=ALU.add)
+
+        def prepare_pair(g, u, shares, by_row):
             cols = slice(u * HALF, (u + 1) * HALF)
             pair = x_raw[g][:].rearrange("p j (m u e) -> p u m j e", u=2, e=2)[:, u]
-            copy(out=x_bf[g][:, cols, :].rearrange("p (e m) j -> p m j e" if by_row else "p (m e) j -> p m j e", e=2), in_=pair)
-            quantize(x_codes[g][:, cols], x_scales[g][:, cols], x_bf[g][:, cols, :], E4)
+            dealt = x_bf[g][:, cols, :].rearrange("p (e m) j -> p m j e" if by_row else "p (m e) j -> p m j e", e=2)
+            m0 = 0
+            for copy, width in shares:
+                copy(out=dealt[:, m0 : m0 + width], in_=pair[:, m0 : m0 + width])
+                m0 = m0 + width
+
+        def quantize_x(g, c0, c1):
+            quantize(x_codes[g][:, c0:c1], x_scales[g][:, c0:c1], x_bf[g][:, c0:c1, :], E4)
 
         def scores_by_row(k):
             g, t = divmod(k, PACK)
             rows = slice(t * P, (t + 1) * P)
             raw = psum.tile([P, N], F32, name="raw_rows", tag="scores")
             matmul(raw[:], x_codes[g][:, rows], x_scales[g][:, rows], w_codes[:], w_scales[:], E4, True, True)
-            turned[k] = keep.tile([P, N], F32, name=f"a{k}")
+            turned[k] = keep.tile([P, N], F32, name=f"a{k}", align_bytes=64)
             nc.vector.tensor_tensor(out=turned[k][:], in0=raw[:], in1=kb_all[:], op=ALU.add)
 
         def max_by_row(k):
@@ -209,14 +220,18 @@ def tile_attend_gkl_w_kb_kernel(tc, xT, wT, y, wt, kb, xm, offs, out):
 
         def exponent(k):
             col = slice(k, k + 1)
-            nc.scalar.activation(out=e[k][:], in_=turned[k][:], func=ACT.Exp, bias=neg_max[:, col], scale=1.0, accum_out=sums[:, col])
+            nc.scalar.activation(out=e[k][:], in_=turned[k][:], func=ACT.Exp, bias=neg_max[:, col], scale=1.0, accum_out=sums[k // PACK][:, k % PACK : k % PACK + 1])
 
-        def factors(k0, k1):
-            cols = slice(k0, k1)
-            nc.vector.reciprocal(out=inv[:, cols], in_=sums[:, cols])
-            nc.vector.tensor_tensor(out=factor[:, cols], in0=inv[:, cols], in1=weights[:].rearrange("p g t -> p (g t)")[:, cols], op=ALU.mult)
+        def factors(g, beside_gpsimd):
+            nc.vector.reciprocal(out=inv[g][:], in_=sums[g][:])
+            if beside_gpsimd:
+                for t in range(PACK):
+                    col = slice(t, t + 1)
+                    nc.scalar.activation(out=factor[g][:, col], in_=inv[g][:, col], func=ACT.Copy, scale=weights[:, g, col])
+            else:
+                nc.vector.tensor_tensor(out=factor[g][:], in0=inv[g][:], in1=weights[:, g, :], op=ALU.mult)
 
-        g_bf = {(g, s0): keep.tile([P, PACK, HALF], BF16, name=f"g_bf{g}_{s0}") for g in range(PASSES) for s0 in (0, HALF)}
+        g_bf = {(g, s0): keep.tile([P, PACK, HALF], BF16, name=f"g_bf{g}_{s0}", align_bytes=64) for g in range(PASSES) for s0 in (0, HALF)}
         g_grouped = [keep.tile([P, N, PACK], BF16, name=f"g_grouped{g}", align_bytes=64) for g in range(PASSES)]
 
         def gradient(ks, s0, s1):
@@ -225,8 +240,8 @@ def tile_attend_gkl_w_kb_kernel(tc, xT, wT, y, wt, kb, xm, offs, out):
                 nc.vector.scalar_tensor_tensor(
                     out=g_bf[g, s0][:, t, :],
                     in0=e[k][:, s0:s1],
-                    scalar=factor[:, k : k + 1],
-                    in1=wy[k][:, s0:s1],
+                    scalar=factor[g][:, t : t + 1],
+                    in1=wy[g][:, t, s0:s1],
                     op0=ALU.mult,
                     op1=ALU.subtract,
                 )
@@ -241,16 +256,18 @@ def tile_attend_gkl_w_kb_kernel(tc, xT, wT, y, wt, kb, xm, offs, out):
             cols = slice(HALF + s0, HALF + s1)
             quantize(g_codes[g][:, cols], g_scales[g][:, cols], g_grouped[g][:, s0:s1, :], E5)
 
-        m_bf = [keep.tile([P, PASSES * P, PACK], BF16, name=f"m_bf{b}", align_bytes=64) for b in range(D // P)]
+        m_bf = {}
         m_codes = [keep.tile([P, PASSES * P], U32, name=f"m_codes{b}", align_bytes=64) for b in range(D // P)]
         m_scales = [keep.tile([P, PASSES * P], U8, name=f"m_scales{b}", align_bytes=64) for b in range(D // P)]
 
         def prepare_xm(b, copies):
+            m_bf[b] = keep.tile([P, PASSES * P, PACK], BF16, name=f"m_bf{b}", tag=("a5", "g_bf1_0", "g_bf1_256", "dw_sb0_0")[b], align_bytes=64)
             for g, copy in enumerate(copies):
                 interleave(copy, m_bf[b][:, g * P : (g + 1) * P, :], m_raw[g][:, :, b * P : (b + 1) * P])
             quantize(m_codes[b][:], m_scales[b][:], m_bf[b][:], E4)
 
         dw_sb = {}
+        DW_TAGS = {(1, 0): "g_bf0_256", (2, 0): "w_raw1"}
 
         def product(b, s0, s1):
             dw = psum.tile([P, N], F32, name="dw", tag="side")
@@ -259,23 +276,27 @@ def tile_attend_gkl_w_kb_kernel(tc, xT, wT, y, wt, kb, xm, offs, out):
             for g in range(PASSES):
                 cols = slice(g * P, (g + 1) * P)
                 matmul(dw[:], m_codes[b][:, cols], m_scales[b][:, cols], g_codes[g][:, moving], g_scales[g][:, moving], E5, g == 0, g == PASSES - 1)
-            dw_sb[b, s0] = keep.tile([P, s1 - s0], F32, name=f"dw_sb{b}_{s0}", tag=f"g_bf1_{HALF}" if (b, s1) == (1, HALF) else f"dw_sb{b}_{s0}")
+            dw_sb[b, s0] = keep.tile([P, s1 - s0], F32, name=f"dw_sb{b}_{s0}", tag=DW_TAGS.get((b, s0), f"dw_sb{b}_{s0}"), align_bytes=64)
             nc.scalar.copy(out=dw_sb[b, s0][:], in_=dw[:, N - (s1 - s0) : N])
 
         def scatter(b, s0, s1):
-            nc.vector.tensor_copy(windows[b][:].indirect(offsets[:, s0 // 16 : s1 // 16]), dw_sb[b, s0][:])
+            nc.vector.tensor_copy(windows[b % WINDOWS][:].indirect(offsets[:, s0 // 16 : s1 // 16]), dw_sb[b, s0][:])
             if s1 == N:
-                nc.sync.dma_start(out=out[b * P : (b + 1) * P, :], in_=windows[b][:])
+                nc.sync.dma_start(out=out[b * P : (b + 1) * P, :], in_=windows[b % WINDOWS][:])
 
-        prepare_pair(0, 0, on_vector, True)
-        prepare_pair(0, 1, on_scalar, False)
-        prepare_pair(1, 1, on_vector, False)
-        prepare_pair(1, 0, on_scalar, True)
+        prepare_pair(0, 0, ((on_scalar, 64), (on_vector, 64)), True)
+        quantize_x(0, 0, HALF)
+        prepare_pair(0, 1, ((on_scalar, P),), False)
+        quantize_x(0, HALF, N)
+        prepare_pair(1, 1, ((on_vector, P),), False)
+        prepare_pair(1, 0, ((on_scalar, P),), True)
+        quantize_x(1, HALF, N)
+        quantize_x(1, 0, HALF)
         scores_by_row(0)
         scores_by_row(1)
         half_scores(0)
         half_scores(1)
-        for k in range(TILES):
+        for k in range(6):
             if k == 2:
                 scores_by_row(4)
                 scores_by_row(5)
@@ -283,12 +304,16 @@ def tile_attend_gkl_w_kb_kernel(tc, xT, wT, y, wt, kb, xm, offs, out):
                 max_by_row(k)
             else:
                 row_max(k)
-        for k in range(TILES):
+        for k in range(PACK):
             exponent(k)
         weigh_targets(0, 0, N, -1)
+        factors(0, True)
         weigh_targets(1, 0, N, -1)
-        for k in range(0, TILES, 2):
-            factors(k, k + 2)
+        row_max(6)
+        row_max(7)
+        for k in range(PACK, TILES):
+            exponent(k)
+        factors(1, False)
         gradient(range(TILES), 0, HALF)
         group_g(0, 0, ((on_scalar, 256),))
         group_g(1, 0, ((on_scalar, 128), (on_vector, 128)))
@@ -298,7 +323,7 @@ def tile_attend_gkl_w_kb_kernel(tc, xT, wT, y, wt, kb, xm, offs, out):
         product(0, 0, HALF)
         gradient(range(PACK), HALF, N)
         prepare_xm(1, (on_scalar, on_scalar))
-        group_g(0, HALF, ((on_scalar, HALF),))
+        group_g(0, HALF, ((on_scalar, P), (on_scalar, P)))
         gradient(range(PACK, TILES), HALF, N)
         group_g(1, HALF, ((on_scalar, HALF),))
         product(1, 0, HALF)

@@ -19,12 +19,18 @@ ACT = mybir.ActivationFunctionType
 
 P = 128
 PACK = 4
-PASS = P * PACK
-PASSES = R // PASS
-TILES = PASSES * PACK
-BLOCKS = N // P
+SPAN = P * PACK
+SPANS = R // SPAN
+TILES = SPANS * PACK
+BY_ROW = 2
+PAIR = BY_ROW * P
+SLOT_BLOCKS = N // P
+FEATURE_BLOCKS = D // P
 HALF = N // 2
+EARLY, LATE = 0, HALF
+PER_COLUMN = 16
 WINDOWS = 3
+PSUM_SLOTS = 4
 
 
 def interleave(copy, dst, src):
@@ -36,16 +42,15 @@ def tile_attend_gkl_w_kb_kernel(tc, xT, wT, y, wt, kb, xm, offs, out):
     on_scalar, on_vector = nc.scalar.copy, nc.vector.tensor_copy
     with ExitStack() as ctx:
         keep = ctx.enter_context(tc.tile_pool(name="keep", bufs=1))
-        psum = ctx.enter_context(tc.psum_pool(name="psum", bufs=4))
+        psum = ctx.enter_context(tc.psum_pool(name="psum", bufs=PSUM_SLOTS))
 
-        offsets = keep.tile([P, N // 16], U16, name="offsets")
-
+        offsets = keep.tile([P, N // PER_COLUMN], U16, name="offsets")
         w_raw = [keep.tile([P, T], F32, name=f"w_raw{j}", align_bytes=64) for j in range(PACK)]
-        x_raw = [keep.tile([P, PACK, PASS], F32, name=f"x_raw{g}") for g in range(PASSES)]
-        y_raw = [keep.tile([P, PACK, N], F32, name=f"y_raw{g}") for g in range(PASSES)]
-        m_raw = [keep.tile([P, PACK, D], F32, name=f"m_raw{g}", tag=f"w_raw{g}", align_bytes=64) for g in range(PASSES)]
+        x_raw = [keep.tile([P, PACK, SPAN], F32, name=f"x_raw{g}") for g in range(SPANS)]
+        y_raw = [keep.tile([P, PACK, N], F32, name=f"y_raw{g}") for g in range(SPANS)]
+        m_raw = [keep.tile([P, PACK, D], F32, name=f"m_raw{g}", tag=f"w_raw{g}", align_bytes=64) for g in range(SPANS)]
         kb_row = keep.tile([P, T], F32, name="kb_row")
-        weights = keep.tile([P, PASSES, PACK], F32, name="weights")
+        weights = keep.tile([P, SPANS, PACK], F32, name="weights")
         w_rows = wT.rearrange("(p j) c -> p j c", j=PACK)
         x_rows = xT[0].rearrange("(p j) r -> p j r", j=PACK)
 
@@ -56,23 +61,21 @@ def tile_attend_gkl_w_kb_kernel(tc, xT, wT, y, wt, kb, xm, offs, out):
         nc.sync.dma_start(out=kb_row[0:1, :], in_=kb[0:1, :])
         for j in range(2, PACK):
             nc.sync.dma_start(out=w_raw[j][:], in_=w_rows[:, j, :])
-        for g in range(PASSES):
-            nc.sync.dma_start(out=x_raw[g][:], in_=x_rows[:, :, g * PASS : (g + 1) * PASS])
-        nc.sync.dma_start(out=weights[:], in_=wt[0].rearrange("(g p t) o -> p g (t o)", g=PASSES, t=PACK))
-        for g in range(PASSES):
-            nc.sync.dma_start(out=y_raw[g][:], in_=y[0][g * PASS : (g + 1) * PASS, :].rearrange("(p t) i -> p t i", t=PACK))
-        for g in range(PASSES):
-            nc.sync.dma_start(out=m_raw[g][:], in_=xm[0][g * PASS : (g + 1) * PASS, :].rearrange("(p t) d -> p t d", t=PACK))
+        for g in range(SPANS):
+            nc.sync.dma_start(out=x_raw[g][:], in_=x_rows[:, :, g * SPAN : (g + 1) * SPAN])
+        nc.sync.dma_start(out=weights[:], in_=wt[0].rearrange("(g p t) o -> p g (t o)", g=SPANS, t=PACK))
+        for g in range(SPANS):
+            nc.sync.dma_start(out=y_raw[g][:], in_=y[0][g * SPAN : (g + 1) * SPAN, :].rearrange("(p t) i -> p t i", t=PACK))
+        for g in range(SPANS):
+            nc.sync.dma_start(out=m_raw[g][:], in_=xm[0][g * SPAN : (g + 1) * SPAN, :].rearrange("(p t) d -> p t d", t=PACK))
 
         ident = keep.tile([P, P], F32, name="ident")
         make_identity(nc, ident[:])
-        warm = keep.tile([P, 1], F32, name="warm")
-        nc.scalar.activation(out=warm[:], in_=ident[:, 0:1], func=ACT.Exp)
-        windows = [keep.tile([P, T], F32, name=f"window{k}") for k in range(WINDOWS)]
+        windows = [keep.tile([P, T], F32, name=f"window{w}") for w in range(WINDOWS)]
         nc.vector.memset(windows[0][:].bitcast(I32), 0)
-        g_codes = [keep.tile([P, HALF + N], U32, name=f"g_codes{g}", align_bytes=64) for g in range(PASSES)]
-        g_scales = [keep.tile([P, HALF + N], U8, name=f"g_scales{g}", align_bytes=64) for g in range(PASSES)]
-        for g in range(PASSES):
+        g_codes = [keep.tile([P, HALF + N], U32, name=f"g_codes{g}", align_bytes=64) for g in range(SPANS)]
+        g_scales = [keep.tile([P, HALF + N], U8, name=f"g_scales{g}", align_bytes=64) for g in range(SPANS)]
+        for g in range(SPANS):
             nc.gpsimd.memset(g_codes[g][:, 0:HALF], 0)
             nc.gpsimd.memset(g_scales[g][:, 0:HALF].bitcast(U32), 0)
         for window in windows[1:]:
@@ -96,20 +99,19 @@ def tile_attend_gkl_w_kb_kernel(tc, xT, wT, y, wt, kb, xm, offs, out):
         w_codes = keep.tile([P, N], U32, name="w_codes", align_bytes=64)
         w_scales = keep.tile([P, N], U8, name="w_scales", align_bytes=64)
         w_pair = keep.tile([P, 2, N], F32, name="w_pair")
-        nc.vector.tensor_copy(w_pair[:, 0, :], w_raw[0][:].indirect(offsets[:]))
-        nc.vector.tensor_copy(w_pair[:, 1, :], w_raw[1][:].indirect(offsets[:]))
+        for j in range(2):
+            nc.vector.tensor_copy(w_pair[:, j, :], w_raw[j][:].indirect(offsets[:]))
         nc.scalar.copy(out=w_bf[:, :, 0:2], in_=w_pair[:].rearrange("p j c -> p c j"))
 
         kb_picked = keep.tile([P, N], F32, name="kb_picked")
         nc.vector.tensor_copy(kb_picked[:], kb_row[:].indirect(offsets[:]))
-        kb_turned = psum.tile([P, BLOCKS, P], F32, name="kb_turned", tag="side")
-        for b in range(BLOCKS):
+        kb_turned = psum.tile([P, SLOT_BLOCKS, P], F32, name="kb_turned", tag="side")
+        for b in range(SLOT_BLOCKS):
             nc.tensor.transpose(kb_turned[:, b, :], kb_picked[:, b * P : (b + 1) * P], ident[:])
-        kb_col = keep.tile([P, BLOCKS], F32, name="kb_col")
+        kb_col = keep.tile([P, SLOT_BLOCKS], F32, name="kb_col")
         nc.scalar.copy(out=kb_col[:], in_=kb_turned[:, :, 0])
-
         kb_spread = psum.tile([P, N], F32, name="kb_spread", tag="side")
-        for b in range(BLOCKS):
+        for b in range(SLOT_BLOCKS):
             nc.tensor.transpose(kb_spread[:, b * P : (b + 1) * P], kb_col[:, b : b + 1].to_broadcast([P, P]), ident[:])
         kb_all = keep.tile([P, N], F32, name="kb_all")
         nc.scalar.copy(out=kb_all[:], in_=kb_spread[:])
@@ -118,226 +120,196 @@ def tile_attend_gkl_w_kb_kernel(tc, xT, wT, y, wt, kb, xm, offs, out):
             nc.vector.tensor_copy(w_bf[:, :, j], w_raw[j][:].indirect(offsets[:]))
         quantize(w_codes[:], w_scales[:], w_bf[:], E4)
 
-        x_bf = [keep.tile([P, PASS, PACK], BF16, name=f"x_bf{g}", align_bytes=64) for g in range(PASSES)]
-        x_codes = [keep.tile([P, PASS], U32, name=f"x_codes{g}", align_bytes=64) for g in range(PASSES)]
-        x_scales = [keep.tile([P, PASS], U8, name=f"x_scales{g}", align_bytes=64) for g in range(PASSES)]
+        x_bf = [keep.tile([P, SPAN, PACK], BF16, name=f"x_bf{g}", align_bytes=64) for g in range(SPANS)]
+        x_codes = [keep.tile([P, SPAN], U32, name=f"x_codes{g}", align_bytes=64) for g in range(SPANS)]
+        x_scales = [keep.tile([P, SPAN], U8, name=f"x_scales{g}", align_bytes=64) for g in range(SPANS)]
+        row_cols, slot_cols = slice(0, PAIR), slice(PAIR, SPAN)
 
-        def prepare_x(g, shares):
-            c0 = 0
-            for copy, width in shares:
-                interleave(copy, x_bf[g][:, c0 : c0 + width, :], x_raw[g][:, :, c0 : c0 + width])
-                c0 = c0 + width
-            quantize(x_codes[g][:], x_scales[g][:], x_bf[g][:], E4)
+        def x_pair(g, u):
+            return x_raw[g][:].rearrange("p j (m u e) -> p u m j e", u=2, e=2)[:, u]
+
+        def cast_x_by_row(g, copies):
+            dealt = x_bf[g][:, row_cols, :].rearrange("p (e m) j -> p m j e", e=2)
+            width = P // len(copies)
+            for n, copy in enumerate(copies):
+                copy(out=dealt[:, n * width : (n + 1) * width], in_=x_pair(g, 0)[:, n * width : (n + 1) * width])
+
+        def cast_x_by_slot(g):
+            nc.scalar.copy(out=x_bf[g][:, slot_cols, :].rearrange("p (m e) j -> p m j e", e=2), in_=x_pair(g, 1))
+
+        def quantize_x(g, cols):
+            quantize(x_codes[g][:, cols], x_scales[g][:, cols], x_bf[g][:, cols, :], E4)
 
         wy = {}
 
-        def weigh_targets(g, s0, s1, on_vector_from):
+        def weigh_targets(g):
             wy[g] = keep.tile([P, PACK, N], F32, name=f"wy{g}", tag=("x_bf1", "wy1")[g], align_bytes=64)
             for t in range(PACK):
-                k = g * PACK + t
-                targets, weight = y_raw[g][:, t, s0:s1], weights[:, g, t : t + 1]
-                if on_vector_from < 0:
-                    nc.gpsimd.tensor_scalar(out=wy[g][:, t, s0:s1], in0=targets, scalar1=weight, scalar2=0.0, op0=ALU.mult, op1=ALU.add)
-                elif t >= on_vector_from:
-                    nc.vector.tensor_scalar(out=wy[g][:, t, s0:s1], in0=targets, scalar1=weight, scalar2=None, op0=ALU.mult)
+                targets, weight = y_raw[g][:, t, :], weights[:, g, t : t + 1]
+                if g * PACK + t < TILES - 1:
+                    nc.gpsimd.tensor_scalar(out=wy[g][:, t, :], in0=targets, scalar1=weight, scalar2=0.0, op0=ALU.mult, op1=ALU.add)
                 else:
-                    nc.scalar.activation(out=wy[g][:, t, s0:s1], in_=targets, func=ACT.Copy, scale=weight)
+                    nc.scalar.activation(out=wy[g][:, t, :], in_=targets, func=ACT.Copy, scale=weight)
 
         neg_max = keep.tile([P, TILES], F32, name="neg_max")
-        sums = [keep.tile([P, PACK], F32, name=f"sums{g}") for g in range(PASSES)]
-        inv = [keep.tile([P, PACK], F32, name=f"inv{g}") for g in range(PASSES)]
-        factor = [keep.tile([P, PACK], F32, name=f"factor{g}") for g in range(PASSES)]
+        sums = [keep.tile([P, PACK], F32, name=f"sums{g}") for g in range(SPANS)]
+        inv = [keep.tile([P, PACK], F32, name=f"inv{g}") for g in range(SPANS)]
+        factor = [keep.tile([P, PACK], F32, name=f"factor{g}") for g in range(SPANS)]
         e = [keep.tile([P, N], F32, name=f"e{k}") for k in range(TILES)]
-        by_slot = [[keep.tile([P, PACK, P], F32, name=f"by_slot{g}_{b}") for b in range(BLOCKS)] for g in range(PASSES)]
+        by_slot = [[keep.tile([P, PACK, P], F32, name=f"by_slot{g}_{b}") for b in range(SLOT_BLOCKS)] for g in range(SPANS)]
+        a = {}
 
-        def scores(g, pieces):
-            raw = []
-            for b in range(BLOCKS):
+        def scores_by_row(g):
+            for t in range(BY_ROW):
+                k = g * PACK + t
+                rows = slice(t * P, (t + 1) * P)
+                raw = psum.tile([P, N], F32, name="raw_rows", tag="scores")
+                matmul(raw[:], x_codes[g][:, rows], x_scales[g][:, rows], w_codes[:], w_scales[:], E4, True, True)
+                a[k] = keep.tile([P, N], F32, name=f"a{k}", align_bytes=64)
+                nc.vector.tensor_tensor(out=a[k][:], in0=raw[:], in1=kb_all[:], op=ALU.add)
+
+        def scores_by_slot(g):
+            for b in range(SLOT_BLOCKS):
                 slots = slice(b * P, (b + 1) * P)
-                raw.append(psum.tile([P, PASS], F32, name="raw", tag="side"))
-                matmul(raw[b][:], w_codes[:, slots], w_scales[:, slots], x_codes[g][:], x_scales[g][:], E4, True, True)
-            width = PACK // pieces
-            for u in range(pieces):
-                places = slice(u * width, (u + 1) * width)
-                for b in range(BLOCKS):
-                    nc.scalar.activation(
-                        out=by_slot[g][b][:, places, :],
-                        in_=raw[b][:].rearrange("p (m t) -> p t m", t=PACK)[:, places, :],
-                        func=ACT.Identity,
-                        bias=kb_col[:, b : b + 1],
-                        scale=1.0,
-                    )
-
-        turned = {}
-
-        def row_max(k):
-            g, t = divmod(k, PACK)
-            col = slice(k, k + 1)
-            a = psum.tile([P, N], F32, name="turned", tag=("scores", "side")[g])
-            turned[k] = a
-            for b in range(BLOCKS):
-                nc.tensor.transpose(a[:, b * P : (b + 1) * P], by_slot[g][b][:, t, :], ident[:])
-            nc.vector.tensor_reduce(out=neg_max[:, col], in_=a[:], axis=mybir.AxisListType.X, op=ALU.max, negate=True)
-
-        def on_gpsimd(out, in_):
-            nc.gpsimd.tensor_scalar(out=out, in0=in_, scalar1=1.0, scalar2=0.0, op0=ALU.mult, op1=ALU.add)
-
-        def prepare_pair(g, u, shares, by_row):
-            cols = slice(u * HALF, (u + 1) * HALF)
-            pair = x_raw[g][:].rearrange("p j (m u e) -> p u m j e", u=2, e=2)[:, u]
-            dealt = x_bf[g][:, cols, :].rearrange("p (e m) j -> p m j e" if by_row else "p (m e) j -> p m j e", e=2)
-            m0 = 0
-            for copy, width in shares:
-                copy(out=dealt[:, m0 : m0 + width], in_=pair[:, m0 : m0 + width])
-                m0 = m0 + width
-
-        def quantize_x(g, c0, c1):
-            quantize(x_codes[g][:, c0:c1], x_scales[g][:, c0:c1], x_bf[g][:, c0:c1, :], E4)
-
-        def scores_by_row(k):
-            g, t = divmod(k, PACK)
-            rows = slice(t * P, (t + 1) * P)
-            raw = psum.tile([P, N], F32, name="raw_rows", tag="scores")
-            matmul(raw[:], x_codes[g][:, rows], x_scales[g][:, rows], w_codes[:], w_scales[:], E4, True, True)
-            turned[k] = keep.tile([P, N], F32, name=f"a{k}", align_bytes=64)
-            nc.vector.tensor_tensor(out=turned[k][:], in0=raw[:], in1=kb_all[:], op=ALU.add)
-
-        def max_by_row(k):
-            nc.vector.tensor_reduce(out=neg_max[:, k : k + 1], in_=turned[k][:], axis=mybir.AxisListType.X, op=ALU.max, negate=True)
-
-        def half_scores(g):
-            for b in range(BLOCKS):
-                slots = slice(b * P, (b + 1) * P)
-                raw = psum.tile([P, HALF], F32, name="raw_half", tag="side")
-                matmul(raw[:], w_codes[:, slots], w_scales[:, slots], x_codes[g][:, HALF:N], x_scales[g][:, HALF:N], E4, True, True)
+                raw = psum.tile([P, PAIR], F32, name="raw_slots", tag="side")
+                matmul(raw[:], w_codes[:, slots], w_scales[:, slots], x_codes[g][:, slot_cols], x_scales[g][:, slot_cols], E4, True, True)
                 nc.scalar.activation(
-                    out=by_slot[g][b][:, 2:PACK, :],
+                    out=by_slot[g][b][:, BY_ROW:PACK, :],
                     in_=raw[:].rearrange("p (m e) -> p e m", e=2),
                     func=ACT.Identity,
                     bias=kb_col[:, b : b + 1],
                     scale=1.0,
                 )
 
-        def exponent(k):
-            col = slice(k, k + 1)
-            nc.scalar.activation(out=e[k][:], in_=turned[k][:], func=ACT.Exp, bias=neg_max[:, col], scale=1.0, accum_out=sums[k // PACK][:, k % PACK : k % PACK + 1])
+        def row_max(k):
+            g, t = divmod(k, PACK)
+            if t >= BY_ROW:
+                a[k] = psum.tile([P, N], F32, name="turned", tag=("scores", "side")[g])
+                for b in range(SLOT_BLOCKS):
+                    nc.tensor.transpose(a[k][:, b * P : (b + 1) * P], by_slot[g][b][:, t, :], ident[:])
+            nc.vector.tensor_reduce(out=neg_max[:, k : k + 1], in_=a[k][:], axis=mybir.AxisListType.X, op=ALU.max, negate=True)
 
-        def factors(g, beside_gpsimd):
+        def exponents(g):
+            for t in range(PACK):
+                k = g * PACK + t
+                nc.scalar.activation(
+                    out=e[k][:], in_=a[k][:], func=ACT.Exp, bias=neg_max[:, k : k + 1], scale=1.0, accum_out=sums[g][:, t : t + 1]
+                )
+
+        def factor_on_scalar(g):
             nc.vector.reciprocal(out=inv[g][:], in_=sums[g][:])
-            if beside_gpsimd:
-                for t in range(PACK):
-                    col = slice(t, t + 1)
-                    nc.scalar.activation(out=factor[g][:, col], in_=inv[g][:, col], func=ACT.Copy, scale=weights[:, g, col])
-            else:
-                nc.vector.tensor_tensor(out=factor[g][:], in0=inv[g][:], in1=weights[:, g, :], op=ALU.mult)
+            for t in range(PACK):
+                col = slice(t, t + 1)
+                nc.scalar.activation(out=factor[g][:, col], in_=inv[g][:, col], func=ACT.Copy, scale=weights[:, g, col])
 
-        g_bf = {(g, s0): keep.tile([P, PACK, HALF], BF16, name=f"g_bf{g}_{s0}", align_bytes=64) for g in range(PASSES) for s0 in (0, HALF)}
-        g_grouped = [keep.tile([P, N, PACK], BF16, name=f"g_grouped{g}", align_bytes=64) for g in range(PASSES)]
+        def factor_on_vector(g):
+            nc.vector.reciprocal(out=inv[g][:], in_=sums[g][:])
+            nc.vector.tensor_tensor(out=factor[g][:], in0=inv[g][:], in1=weights[:, g, :], op=ALU.mult)
 
-        def gradient(ks, s0, s1):
-            for k in ks:
-                g, t = divmod(k, PACK)
+        g_bf = {
+            (g, s0): keep.tile([P, PACK, HALF], BF16, name=f"g_bf{g}_{s0}", align_bytes=64)
+            for g in range(SPANS)
+            for s0 in (EARLY, LATE)
+        }
+        g_grouped = [keep.tile([P, N, PACK], BF16, name=f"g_grouped{g}", align_bytes=64) for g in range(SPANS)]
+
+        def gradient(g, s0):
+            slots = slice(s0, s0 + HALF)
+            for t in range(PACK):
                 nc.vector.scalar_tensor_tensor(
                     out=g_bf[g, s0][:, t, :],
-                    in0=e[k][:, s0:s1],
+                    in0=e[g * PACK + t][:, slots],
                     scalar=factor[g][:, t : t + 1],
-                    in1=wy[g][:, t, s0:s1],
+                    in1=wy[g][:, t, slots],
                     op0=ALU.mult,
                     op1=ALU.subtract,
                 )
 
-        def group_g(g, s0, shares):
-            c0 = 0
-            for copy, width in shares:
+        def group_g(g, s0, copies):
+            width = HALF // len(copies)
+            for n, copy in enumerate(copies):
+                c0 = n * width
                 interleave(copy, g_grouped[g][:, s0 + c0 : s0 + c0 + width, :], g_bf[g, s0][:, :, c0 : c0 + width])
-                c0 = c0 + width
 
-        def quantize_g(g, s0, s1):
-            cols = slice(HALF + s0, HALF + s1)
-            quantize(g_codes[g][:, cols], g_scales[g][:, cols], g_grouped[g][:, s0:s1, :], E5)
+        def quantize_g(g, s0):
+            cols = slice(HALF + s0, HALF + s0 + HALF)
+            quantize(g_codes[g][:, cols], g_scales[g][:, cols], g_grouped[g][:, s0 : s0 + HALF, :], E5)
 
-        m_bf = {}
-        m_codes = [keep.tile([P, PASSES * P], U32, name=f"m_codes{b}", align_bytes=64) for b in range(D // P)]
-        m_scales = [keep.tile([P, PASSES * P], U8, name=f"m_scales{b}", align_bytes=64) for b in range(D // P)]
+        m_codes = [keep.tile([P, SPANS * P], U32, name=f"m_codes{b}", align_bytes=64) for b in range(FEATURE_BLOCKS)]
+        m_scales = [keep.tile([P, SPANS * P], U8, name=f"m_scales{b}", align_bytes=64) for b in range(FEATURE_BLOCKS)]
 
-        def prepare_xm(b, copies):
-            m_bf[b] = keep.tile([P, PASSES * P, PACK], BF16, name=f"m_bf{b}", tag=("a5", "g_bf1_0", "g_bf1_256", "dw_sb0_0")[b], align_bytes=64)
-            for g, copy in enumerate(copies):
-                interleave(copy, m_bf[b][:, g * P : (g + 1) * P, :], m_raw[g][:, :, b * P : (b + 1) * P])
-            quantize(m_codes[b][:], m_scales[b][:], m_bf[b][:], E4)
+        def prepare_xm(b, slot):
+            m_bf = keep.tile([P, SPANS * P, PACK], BF16, name=f"m_bf{b}", tag=slot, align_bytes=64)
+            for g in range(SPANS):
+                interleave(on_scalar, m_bf[:, g * P : (g + 1) * P, :], m_raw[g][:, :, b * P : (b + 1) * P])
+            quantize(m_codes[b][:], m_scales[b][:], m_bf[:], E4)
 
         dw_sb = {}
-        DW_TAGS = {(1, 0): "g_bf0_256", (2, 0): "w_raw1"}
 
-        def product(b, s0, s1):
+        def product(b, s0, s1, slot):
             dw = psum.tile([P, N], F32, name="dw", tag="side")
-            first = HALF + s1 - N
-            moving = slice(first, first + N)
-            for g in range(PASSES):
+            moving = slice(HALF + s1 - N, HALF + s1)
+            for g in range(SPANS):
                 cols = slice(g * P, (g + 1) * P)
-                matmul(dw[:], m_codes[b][:, cols], m_scales[b][:, cols], g_codes[g][:, moving], g_scales[g][:, moving], E5, g == 0, g == PASSES - 1)
-            dw_sb[b, s0] = keep.tile([P, s1 - s0], F32, name=f"dw_sb{b}_{s0}", tag=DW_TAGS.get((b, s0), f"dw_sb{b}_{s0}"), align_bytes=64)
+                matmul(dw[:], m_codes[b][:, cols], m_scales[b][:, cols], g_codes[g][:, moving], g_scales[g][:, moving], E5, g == 0, g == SPANS - 1)
+            dw_sb[b, s0] = keep.tile([P, s1 - s0], F32, name=f"dw_sb{b}_{s0}", tag=slot, align_bytes=64)
             nc.scalar.copy(out=dw_sb[b, s0][:], in_=dw[:, N - (s1 - s0) : N])
 
         def scatter(b, s0, s1):
-            nc.vector.tensor_copy(windows[b % WINDOWS][:].indirect(offsets[:, s0 // 16 : s1 // 16]), dw_sb[b, s0][:])
+            window = windows[b % WINDOWS]
+            nc.vector.tensor_copy(window[:].indirect(offsets[:, s0 // PER_COLUMN : s1 // PER_COLUMN]), dw_sb[b, s0][:])
             if s1 == N:
-                nc.sync.dma_start(out=out[b * P : (b + 1) * P, :], in_=windows[b % WINDOWS][:])
+                nc.sync.dma_start(out=out[b * P : (b + 1) * P, :], in_=window[:])
 
-        prepare_pair(0, 0, ((on_scalar, 64), (on_vector, 64)), True)
-        quantize_x(0, 0, HALF)
-        prepare_pair(0, 1, ((on_scalar, P),), False)
-        quantize_x(0, HALF, N)
-        prepare_pair(1, 1, ((on_vector, P),), False)
-        prepare_pair(1, 0, ((on_scalar, P),), True)
-        quantize_x(1, HALF, N)
-        quantize_x(1, 0, HALF)
-        scores_by_row(0)
-        scores_by_row(1)
-        half_scores(0)
-        half_scores(1)
-        for k in range(6):
-            if k == 2:
-                scores_by_row(4)
-                scores_by_row(5)
-            if k % PACK < 2:
-                max_by_row(k)
-            else:
-                row_max(k)
-        for k in range(PACK):
-            exponent(k)
-        weigh_targets(0, 0, N, -1)
-        factors(0, True)
-        weigh_targets(1, 0, N, -1)
-        row_max(6)
-        row_max(7)
-        for k in range(PACK, TILES):
-            exponent(k)
-        factors(1, False)
-        gradient(range(TILES), 0, HALF)
-        group_g(0, 0, ((on_scalar, 256),))
-        group_g(1, 0, ((on_scalar, 128), (on_vector, 128)))
-        quantize_g(0, 0, HALF)
-        quantize_g(1, 0, HALF)
-        prepare_xm(0, (on_scalar, on_scalar))
-        product(0, 0, HALF)
-        gradient(range(PACK), HALF, N)
-        prepare_xm(1, (on_scalar, on_scalar))
-        group_g(0, HALF, ((on_scalar, P), (on_scalar, P)))
-        gradient(range(PACK, TILES), HALF, N)
-        group_g(1, HALF, ((on_scalar, HALF),))
-        product(1, 0, HALF)
-        scatter(0, 0, HALF)
-        quantize_g(0, HALF, N)
-        quantize_g(1, HALF, N)
-        prepare_xm(2, (on_scalar, on_scalar))
-        scatter(1, 0, HALF)
-        product(0, HALF, N)
-        product(1, HALF, N)
-        prepare_xm(3, (on_scalar, on_scalar))
-        scatter(0, HALF, N)
-        scatter(1, HALF, N)
-        for b in range(2, D // P):
-            product(b, 0, N)
-        for b in range(2, D // P):
+        cast_x_by_row(0, (on_scalar, on_vector))
+        quantize_x(0, row_cols)
+        cast_x_by_slot(0)
+        quantize_x(0, slot_cols)
+        cast_x_by_slot(1)
+        cast_x_by_row(1, (on_vector,))
+        quantize_x(1, row_cols)
+        quantize_x(1, slot_cols)
+        for g in range(SPANS):
+            scores_by_row(g)
+            scores_by_slot(g)
+
+        for k in range(PACK + BY_ROW):
+            row_max(k)
+        exponents(0)
+        weigh_targets(0)
+        factor_on_scalar(0)
+        weigh_targets(1)
+        for k in range(PACK + BY_ROW, TILES):
+            row_max(k)
+        exponents(1)
+        factor_on_vector(1)
+
+        for g in range(SPANS):
+            gradient(g, EARLY)
+        group_g(0, EARLY, (on_scalar,))
+        group_g(1, EARLY, (on_scalar, on_vector))
+        for g in range(SPANS):
+            quantize_g(g, EARLY)
+        prepare_xm(0, "m_bf0")
+        product(0, EARLY, LATE, "dw_sb0_0")
+
+        gradient(0, LATE)
+        prepare_xm(1, f"g_bf1_{EARLY}")
+        group_g(0, LATE, (on_scalar, on_scalar))
+        gradient(1, LATE)
+        group_g(1, LATE, (on_scalar,))
+        product(1, EARLY, LATE, f"g_bf0_{LATE}")
+        scatter(0, EARLY, LATE)
+        for g in range(SPANS):
+            quantize_g(g, LATE)
+        prepare_xm(2, f"g_bf1_{LATE}")
+        scatter(1, EARLY, LATE)
+        for b in range(2):
+            product(b, LATE, N, f"dw_sb{b}_{LATE}")
+        prepare_xm(3, "dw_sb0_0")
+        for b in range(2):
+            scatter(b, LATE, N)
+        product(2, 0, N, "w_raw1")
+        product(3, 0, N, "dw_sb3_0")
+        for b in range(2, FEATURE_BLOCKS):
             scatter(b, 0, N)

@@ -22,8 +22,7 @@ PACK = 4
 SPAN = P * PACK
 SPANS = R // SPAN
 TILES = SPANS * PACK
-BY_ROW = 2
-PAIR = BY_ROW * P
+PIECE = SPAN // 2
 SLOT_BLOCKS = N // P
 FEATURE_BLOCKS = D // P
 HALF = N // 2
@@ -46,8 +45,8 @@ def tile_attend_gkl_w_kb_kernel(tc, xT, wT, y, wt, kb, xm, offs, out):
 
         offsets = keep.tile([P, N // PER_COLUMN], U16, name="offsets")
         w_raw = [keep.tile([P, T], F32, name=f"w_raw{j}", align_bytes=64) for j in range(PACK)]
-        x_raw = [keep.tile([P, PACK, SPAN], F32, name=f"x_raw{g}") for g in range(SPANS)]
-        y_raw = [keep.tile([P, PACK, N], F32, name=f"y_raw{g}") for g in range(SPANS)]
+        x_raw = [keep.tile([P, PACK, PIECE], F32, name=f"x_raw{h}") for h in range(R // PIECE)]
+        y_raw = [keep.tile([P, 2, N], F32, name=f"y_raw{u}") for u in range(TILES // 2)]
         m_raw = [keep.tile([P, PACK, D], F32, name=f"m_raw{g}", tag=f"w_raw{g}", align_bytes=64) for g in range(SPANS)]
         kb_row = keep.tile([P, T], F32, name="kb_row")
         weights = keep.tile([P, SPANS, PACK], F32, name="weights")
@@ -61,11 +60,13 @@ def tile_attend_gkl_w_kb_kernel(tc, xT, wT, y, wt, kb, xm, offs, out):
         nc.sync.dma_start(out=kb_row[0:1, :], in_=kb[0:1, :])
         for j in range(2, PACK):
             nc.sync.dma_start(out=w_raw[j][:], in_=w_rows[:, j, :])
-        for g in range(SPANS):
-            nc.sync.dma_start(out=x_raw[g][:], in_=x_rows[:, :, g * SPAN : (g + 1) * SPAN])
+        for h in range(R // PIECE):
+            nc.sync.dma_start(out=x_raw[h][:], in_=x_rows[:, :, h * PIECE : (h + 1) * PIECE])
         nc.sync.dma_start(out=weights[:], in_=wt[0].rearrange("(g p t) o -> p g (t o)", g=SPANS, t=PACK))
-        for g in range(SPANS):
-            nc.sync.dma_start(out=y_raw[g][:], in_=y[0][g * SPAN : (g + 1) * SPAN, :].rearrange("(p t) i -> p t i", t=PACK))
+        y_rows = y[0].rearrange("(g p t) i -> p g t i", g=SPANS, t=PACK)
+        for u in range(TILES // 2):
+            g, t = divmod(2 * u, PACK)
+            nc.sync.dma_start(out=y_raw[u][:], in_=y_rows[:, g, t : t + 2, :])
         for g in range(SPANS):
             nc.sync.dma_start(out=m_raw[g][:], in_=xm[0][g * SPAN : (g + 1) * SPAN, :].rearrange("(p t) d -> p t d", t=PACK))
 
@@ -110,43 +111,26 @@ def tile_attend_gkl_w_kb_kernel(tc, xT, wT, y, wt, kb, xm, offs, out):
             nc.tensor.transpose(kb_turned[:, b, :], kb_picked[:, b * P : (b + 1) * P], ident[:])
         kb_col = keep.tile([P, SLOT_BLOCKS], F32, name="kb_col")
         nc.scalar.copy(out=kb_col[:], in_=kb_turned[:, :, 0])
-        kb_spread = psum.tile([P, N], F32, name="kb_spread", tag="side")
-        for b in range(SLOT_BLOCKS):
-            nc.tensor.transpose(kb_spread[:, b * P : (b + 1) * P], kb_col[:, b : b + 1].to_broadcast([P, P]), ident[:])
-        kb_all = keep.tile([P, N], F32, name="kb_all")
-        nc.scalar.copy(out=kb_all[:], in_=kb_spread[:])
 
         for j in range(2, PACK):
             nc.vector.tensor_copy(w_bf[:, :, j], w_raw[j][:].indirect(offsets[:]))
         quantize(w_codes[:], w_scales[:], w_bf[:], E4)
 
-        x_bf = [keep.tile([P, SPAN, PACK], BF16, name=f"x_bf{g}", align_bytes=64) for g in range(SPANS)]
-        x_codes = [keep.tile([P, SPAN], U32, name=f"x_codes{g}", align_bytes=64) for g in range(SPANS)]
-        x_scales = [keep.tile([P, SPAN], U8, name=f"x_scales{g}", align_bytes=64) for g in range(SPANS)]
-        row_cols, slot_cols = slice(0, PAIR), slice(PAIR, SPAN)
+        x_bf = [keep.tile([P, PIECE, PACK], BF16, name=f"x_bf{h}", align_bytes=64) for h in range(R // PIECE)]
+        x_codes = [keep.tile([P, PIECE], U32, name=f"x_codes{h}", align_bytes=64) for h in range(R // PIECE)]
+        x_scales = [keep.tile([P, PIECE], U8, name=f"x_scales{h}", align_bytes=64) for h in range(R // PIECE)]
 
-        def x_pair(g, u):
-            return x_raw[g][:].rearrange("p j (m u e) -> p u m j e", u=2, e=2)[:, u]
-
-        def cast_x_by_row(g, copies):
-            dealt = x_bf[g][:, row_cols, :].rearrange("p (e m) j -> p m j e", e=2)
-            width = P // len(copies)
-            for n, copy in enumerate(copies):
-                copy(out=dealt[:, n * width : (n + 1) * width], in_=x_pair(g, 0)[:, n * width : (n + 1) * width])
-
-        def cast_x_by_slot(g):
-            nc.scalar.copy(out=x_bf[g][:, slot_cols, :].rearrange("p (m e) j -> p m j e", e=2), in_=x_pair(g, 1))
-
-        def quantize_x(g, cols):
-            quantize(x_codes[g][:, cols], x_scales[g][:, cols], x_bf[g][:, cols, :], E4)
+        def prepare_x(h, copy):
+            interleave(copy, x_bf[h][:], x_raw[h][:])
+            quantize(x_codes[h][:], x_scales[h][:], x_bf[h][:], E4)
 
         wy = {}
 
         def weigh_targets(g):
-            wy[g] = keep.tile([P, PACK, N], F32, name=f"wy{g}", tag=("x_bf1", "wy1")[g], align_bytes=64)
+            wy[g] = keep.tile([P, PACK, N], F32, name=f"wy{g}", tag=("x_bf3", "wy1")[g], align_bytes=64)
             for t in range(PACK):
-                targets, weight = y_raw[g][:, t, :], weights[:, g, t : t + 1]
-                if g * PACK + t < TILES - 1:
+                targets, weight = y_raw[(g * PACK + t) // 2][:, t % 2, :], weights[:, g, t : t + 1]
+                if g * PACK + t < 8:
                     nc.gpsimd.tensor_scalar(out=wy[g][:, t, :], in0=targets, scalar1=weight, scalar2=0.0, op0=ALU.mult, op1=ALU.add)
                 else:
                     nc.scalar.activation(out=wy[g][:, t, :], in_=targets, func=ACT.Copy, scale=weight)
@@ -159,34 +143,21 @@ def tile_attend_gkl_w_kb_kernel(tc, xT, wT, y, wt, kb, xm, offs, out):
         by_slot = [[keep.tile([P, PACK, P], F32, name=f"by_slot{g}_{b}") for b in range(SLOT_BLOCKS)] for g in range(SPANS)]
         a = {}
 
-        def scores_by_row(g):
-            for t in range(BY_ROW):
-                k = g * PACK + t
-                rows = slice(t * P, (t + 1) * P)
-                raw = psum.tile([P, N], F32, name="raw_rows", tag="scores")
-                matmul(raw[:], x_codes[g][:, rows], x_scales[g][:, rows], w_codes[:], w_scales[:], E4, True, True)
-                a[k] = keep.tile([P, N], F32, name=f"a{k}", align_bytes=64)
-                nc.vector.tensor_tensor(out=a[k][:], in0=raw[:], in1=kb_all[:], op=ALU.add)
-
-        def scores_by_slot(g):
+        def scores(h):
+            g, half = divmod(h, 2)
+            m = slice(half * PIECE // PACK, (half + 1) * PIECE // PACK)
             for b in range(SLOT_BLOCKS):
                 slots = slice(b * P, (b + 1) * P)
-                raw = psum.tile([P, PAIR], F32, name="raw_slots", tag="side")
-                matmul(raw[:], w_codes[:, slots], w_scales[:, slots], x_codes[g][:, slot_cols], x_scales[g][:, slot_cols], E4, True, True)
-                nc.scalar.activation(
-                    out=by_slot[g][b][:, BY_ROW:PACK, :],
-                    in_=raw[:].rearrange("p (m e) -> p e m", e=2),
-                    func=ACT.Identity,
-                    bias=kb_col[:, b : b + 1],
-                    scale=1.0,
-                )
+                raw = psum.tile([P, PIECE], F32, name="raw", tag="scores" if h == 1 else "side")
+                matmul(raw[:], w_codes[:, slots], w_scales[:, slots], x_codes[h][:], x_scales[h][:], E4, True, True)
+                dealt, sums_in, bias = by_slot[g][b][:, :, m], raw[:].rearrange("p (m t) -> p t m", t=PACK), kb_col[:, b : b + 1]
+                nc.scalar.activation(out=dealt, in_=sums_in, func=ACT.Identity, bias=bias, scale=1.0)
 
         def row_max(k):
             g, t = divmod(k, PACK)
-            if t >= BY_ROW:
-                a[k] = psum.tile([P, N], F32, name="turned", tag=("scores", "side")[g])
-                for b in range(SLOT_BLOCKS):
-                    nc.tensor.transpose(a[k][:, b * P : (b + 1) * P], by_slot[g][b][:, t, :], ident[:])
+            a[k] = psum.tile([P, N], F32, name="turned", tag=("scores", "side")[g])
+            for b in range(SLOT_BLOCKS):
+                nc.tensor.transpose(a[k][:, b * P : (b + 1) * P], by_slot[g][b][:, t, :], ident[:])
             nc.vector.tensor_reduce(out=neg_max[:, k : k + 1], in_=a[k][:], axis=mybir.AxisListType.X, op=ALU.max, negate=True)
 
         def exponents(g):
@@ -261,25 +232,18 @@ def tile_attend_gkl_w_kb_kernel(tc, xT, wT, y, wt, kb, xm, offs, out):
             if s1 == N:
                 nc.sync.dma_start(out=out[b * P : (b + 1) * P, :], in_=window[:])
 
-        cast_x_by_row(0, (on_scalar, on_vector))
-        quantize_x(0, row_cols)
-        cast_x_by_slot(0)
-        quantize_x(0, slot_cols)
-        cast_x_by_slot(1)
-        cast_x_by_row(1, (on_vector,))
-        quantize_x(1, row_cols)
-        quantize_x(1, slot_cols)
-        for g in range(SPANS):
-            scores_by_row(g)
-            scores_by_slot(g)
+        for h in range(R // PIECE):
+            prepare_x(h, on_scalar if h == 0 else on_vector)
+        for h in range(R // PIECE):
+            scores(h)
 
-        for k in range(PACK + BY_ROW):
+        for k in range(PACK + 2):
             row_max(k)
         exponents(0)
         weigh_targets(0)
-        factor_on_scalar(0)
+        factor_on_vector(0)
         weigh_targets(1)
-        for k in range(PACK + BY_ROW, TILES):
+        for k in range(PACK + 2, TILES):
             row_max(k)
         exponents(1)
         factor_on_vector(1)

@@ -28,7 +28,7 @@ FEATURE_BLOCKS = D // P
 HALF = N // 2
 EARLY, LATE = 0, HALF
 PER_COLUMN = 16
-WINDOWS = 3
+WINDOWS = 4
 PSUM_SLOTS = 4
 
 
@@ -46,7 +46,7 @@ def tile_attend_gkl_w_kb_kernel(tc, xT, wT, y, wt, kb, xm, offs, out):
         offsets = keep.tile([P, N // PER_COLUMN], U16, name="offsets")
         w_raw = [keep.tile([P, T], F32, name=f"w_raw{j}", align_bytes=64) for j in range(PACK)]
         x_raw = [keep.tile([P, PACK, PIECE], F32, name=f"x_raw{h}") for h in range(R // PIECE)]
-        y_raw = [keep.tile([P, 2, N], F32, name=f"y_raw{u}") for u in range(TILES // 2)]
+        y_raw = [keep.tile([P, 2, N], F32, name=f"y_raw{u}", align_bytes=64) for u in range(TILES // 2)]
         m_raw = [keep.tile([P, PACK, D], F32, name=f"m_raw{g}", tag=f"w_raw{g}", align_bytes=64) for g in range(SPANS)]
         kb_row = keep.tile([P, T], F32, name="kb_row")
         weights = keep.tile([P, SPANS, PACK], F32, name="weights")
@@ -55,6 +55,7 @@ def tile_attend_gkl_w_kb_kernel(tc, xT, wT, y, wt, kb, xm, offs, out):
 
         nc.vector.memset(kb_row[:].bitcast(I32), 0)
         nc.sync.dma_start(out=w_raw[0][:], in_=w_rows[:, 0, :])
+        nc.scalar.dma_start(out=weights[:], in_=wt[0].rearrange("(g p t) o -> p g (t o)", g=SPANS, t=PACK))
         nc.sync.dma_start(offsets[:], offs)
         nc.sync.dma_start(out=w_raw[1][:], in_=w_rows[:, 1, :])
         nc.sync.dma_start(out=kb_row[0:1, :], in_=kb[0:1, :])
@@ -62,7 +63,6 @@ def tile_attend_gkl_w_kb_kernel(tc, xT, wT, y, wt, kb, xm, offs, out):
             nc.sync.dma_start(out=w_raw[j][:], in_=w_rows[:, j, :])
         for h in range(R // PIECE):
             nc.sync.dma_start(out=x_raw[h][:], in_=x_rows[:, :, h * PIECE : (h + 1) * PIECE])
-        nc.sync.dma_start(out=weights[:], in_=wt[0].rearrange("(g p t) o -> p g (t o)", g=SPANS, t=PACK))
         y_rows = y[0].rearrange("(g p t) i -> p g t i", g=SPANS, t=PACK)
         for u in range(TILES // 2):
             g, t = divmod(2 * u, PACK)
@@ -126,14 +126,19 @@ def tile_attend_gkl_w_kb_kernel(tc, xT, wT, y, wt, kb, xm, offs, out):
 
         wy = {}
 
-        def weigh_targets(g):
-            wy[g] = keep.tile([P, PACK, N], F32, name=f"wy{g}", tag=("x_bf3", "wy1")[g], align_bytes=64)
-            for t in range(PACK):
-                targets, weight = y_raw[(g * PACK + t) // 2][:, t % 2, :], weights[:, g, t : t + 1]
-                if g * PACK + t < 8:
-                    nc.gpsimd.tensor_scalar(out=wy[g][:, t, :], in0=targets, scalar1=weight, scalar2=0.0, op0=ALU.mult, op1=ALU.add)
-                else:
-                    nc.scalar.activation(out=wy[g][:, t, :], in_=targets, func=ACT.Copy, scale=weight)
+        def weigh_targets_on_gpsimd(name, tiles, slot):
+            weighted = keep.tile([P, len(tiles), N], F32, name=name, tag=slot, align_bytes=64)
+            for n, k in enumerate(tiles):
+                g, t = divmod(k, PACK)
+                wy[k] = weighted[:, n, :]
+                nc.gpsimd.tensor_scalar(
+                    out=wy[k], in0=y_raw[k // 2][:, k % 2, :], scalar1=weights[:, g, t : t + 1], scalar2=0.0, op0=ALU.mult, op1=ALU.add
+                )
+
+        def weigh_targets_on_vector(k, slot):
+            g, t = divmod(k, PACK)
+            wy[k] = keep.tile([P, N], F32, name=f"wy{k}", tag=slot, align_bytes=64)[:]
+            nc.vector.tensor_scalar(out=wy[k], in0=y_raw[k // 2][:, k % 2, :], scalar1=weights[:, g, t : t + 1], scalar2=None, op0=ALU.mult)
 
         neg_max = keep.tile([P, TILES], F32, name="neg_max")
         sums = [keep.tile([P, PACK], F32, name=f"sums{g}") for g in range(SPANS)]
@@ -167,12 +172,6 @@ def tile_attend_gkl_w_kb_kernel(tc, xT, wT, y, wt, kb, xm, offs, out):
                     out=e[k][:], in_=a[k][:], func=ACT.Exp, bias=neg_max[:, k : k + 1], scale=1.0, accum_out=sums[g][:, t : t + 1]
                 )
 
-        def factor_on_scalar(g):
-            nc.vector.reciprocal(out=inv[g][:], in_=sums[g][:])
-            for t in range(PACK):
-                col = slice(t, t + 1)
-                nc.scalar.activation(out=factor[g][:, col], in_=inv[g][:, col], func=ACT.Copy, scale=weights[:, g, col])
-
         def factor_on_vector(g):
             nc.vector.reciprocal(out=inv[g][:], in_=sums[g][:])
             nc.vector.tensor_tensor(out=factor[g][:], in0=inv[g][:], in1=weights[:, g, :], op=ALU.mult)
@@ -191,7 +190,7 @@ def tile_attend_gkl_w_kb_kernel(tc, xT, wT, y, wt, kb, xm, offs, out):
                     out=g_bf[g, s0][:, t, :],
                     in0=e[g * PACK + t][:, slots],
                     scalar=factor[g][:, t : t + 1],
-                    in1=wy[g][:, t, slots],
+                    in1=wy[g * PACK + t][:, slots],
                     op0=ALU.mult,
                     op1=ALU.subtract,
                 )
@@ -240,11 +239,12 @@ def tile_attend_gkl_w_kb_kernel(tc, xT, wT, y, wt, kb, xm, offs, out):
         for k in range(PACK + 2):
             row_max(k)
         exponents(0)
-        weigh_targets(0)
+        weigh_targets_on_gpsimd("wy_first", range(PACK), "x_bf3")
         factor_on_vector(0)
-        weigh_targets(1)
+        weigh_targets_on_gpsimd("wy_last", range(PACK + 1, TILES), "wy_last")
         for k in range(PACK + 2, TILES):
             row_max(k)
+        weigh_targets_on_vector(PACK, "y_raw3")
         exponents(1)
         factor_on_vector(1)
 

@@ -232,7 +232,7 @@ def tile_attend_gkl_w_kb_kernel(tc, xT, wT, y, wt, kb, xm, offs, out):
                 nc.sync.dma_start(out=out[b * P : (b + 1) * P, :], in_=window[:])
 
         for h in range(R // PIECE):
-            prepare_x(h, on_scalar if h == 0 else on_vector)
+            prepare_x(h, on_scalar if h < 2 else on_vector)
         for h in range(R // PIECE):
             scores(h)
 
@@ -251,7 +251,7 @@ def tile_attend_gkl_w_kb_kernel(tc, xT, wT, y, wt, kb, xm, offs, out):
         for g in range(SPANS):
             gradient(g, EARLY)
         group_g(0, EARLY, (on_scalar,))
-        group_g(1, EARLY, (on_scalar, on_vector))
+        group_g(1, EARLY, (on_vector,))
         for g in range(SPANS):
             quantize_g(g, EARLY)
         prepare_xm(0, "m_bf0")

@@ -28,8 +28,7 @@ FEATURE_BLOCKS = D // P
 HALF = N // 2
 EARLY, LATE = 0, HALF
 PER_COLUMN = 16
-WINDOWS = 4
-PSUM_SLOTS = 4
+PSUM_BUFS = 4
 
 
 def interleave(copy, dst, src):
@@ -41,7 +40,7 @@ def tile_attend_gkl_w_kb_kernel(tc, xT, wT, y, wt, kb, xm, offs, out):
     on_scalar, on_vector = nc.scalar.copy, nc.vector.tensor_copy
     with ExitStack() as ctx:
         keep = ctx.enter_context(tc.tile_pool(name="keep", bufs=1))
-        psum = ctx.enter_context(tc.psum_pool(name="psum", bufs=PSUM_SLOTS))
+        psum = ctx.enter_context(tc.psum_pool(name="psum", bufs=PSUM_BUFS))
 
         offsets = keep.tile([P, N // PER_COLUMN], U16, name="offsets")
         w_raw = [keep.tile([P, T], F32, name=f"w_raw{j}", align_bytes=64) for j in range(PACK)]
@@ -49,13 +48,13 @@ def tile_attend_gkl_w_kb_kernel(tc, xT, wT, y, wt, kb, xm, offs, out):
         y_raw = [keep.tile([P, 2, N], F32, name=f"y_raw{u}", align_bytes=64) for u in range(TILES // 2)]
         m_raw = [keep.tile([P, PACK, D], F32, name=f"m_raw{g}", tag=f"w_raw{g}", align_bytes=64) for g in range(SPANS)]
         kb_row = keep.tile([P, T], F32, name="kb_row")
-        weights = keep.tile([P, SPANS, PACK], F32, name="weights")
+        weights = keep.tile([P, SPANS, 2 * PACK], F32, name="weights")[:, :, 0:PACK]
         w_rows = wT.rearrange("(p j) c -> p j c", j=PACK)
         x_rows = xT[0].rearrange("(p j) r -> p j r", j=PACK)
 
         nc.vector.memset(kb_row[:].bitcast(I32), 0)
         nc.sync.dma_start(out=w_raw[0][:], in_=w_rows[:, 0, :])
-        nc.scalar.dma_start(out=weights[:], in_=wt[0].rearrange("(g p t) o -> p g (t o)", g=SPANS, t=PACK))
+        nc.scalar.dma_start(out=weights, in_=wt[0].rearrange("(g p t) o -> p g (t o)", g=SPANS, t=PACK))
         nc.sync.dma_start(offsets[:], offs)
         nc.sync.dma_start(out=w_raw[1][:], in_=w_rows[:, 1, :])
         nc.sync.dma_start(out=kb_row[0:1, :], in_=kb[0:1, :])
@@ -72,7 +71,7 @@ def tile_attend_gkl_w_kb_kernel(tc, xT, wT, y, wt, kb, xm, offs, out):
 
         ident = keep.tile([P, P], F32, name="ident")
         make_identity(nc, ident[:])
-        windows = [keep.tile([P, T], F32, name=f"window{w}") for w in range(WINDOWS)]
+        windows = [keep.tile([P, T], F32, name=f"window{w}") for w in range(FEATURE_BLOCKS)]
         nc.vector.memset(windows[0][:].bitcast(I32), 0)
         g_codes = [keep.tile([P, HALF + N], U32, name=f"g_codes{g}", align_bytes=64) for g in range(SPANS)]
         g_scales = [keep.tile([P, HALF + N], U8, name=f"g_scales{g}", align_bytes=64) for g in range(SPANS)]
@@ -126,8 +125,8 @@ def tile_attend_gkl_w_kb_kernel(tc, xT, wT, y, wt, kb, xm, offs, out):
 
         wy = {}
 
-        def weigh_targets_on_gpsimd(name, tiles, slot):
-            weighted = keep.tile([P, len(tiles), N], F32, name=name, tag=slot, align_bytes=64)
+        def weigh_targets_on_gpsimd(name, tiles, tag):
+            weighted = keep.tile([P, len(tiles), N], F32, name=name, tag=tag, align_bytes=64)
             for n, k in enumerate(tiles):
                 g, t = divmod(k, PACK)
                 wy[k] = weighted[:, n, :]
@@ -135,9 +134,9 @@ def tile_attend_gkl_w_kb_kernel(tc, xT, wT, y, wt, kb, xm, offs, out):
                     out=wy[k], in0=y_raw[k // 2][:, k % 2, :], scalar1=weights[:, g, t : t + 1], scalar2=0.0, op0=ALU.mult, op1=ALU.add
                 )
 
-        def weigh_targets_on_vector(k, slot):
+        def weigh_targets_on_vector(k, tag):
             g, t = divmod(k, PACK)
-            wy[k] = keep.tile([P, N], F32, name=f"wy{k}", tag=slot, align_bytes=64)[:]
+            wy[k] = keep.tile([P, N], F32, name=f"wy{k}", tag=tag, align_bytes=64)[:]
             nc.vector.tensor_scalar(out=wy[k], in0=y_raw[k // 2][:, k % 2, :], scalar1=weights[:, g, t : t + 1], scalar2=None, op0=ALU.mult)
 
         neg_max = keep.tile([P, TILES], F32, name="neg_max")
@@ -149,14 +148,19 @@ def tile_attend_gkl_w_kb_kernel(tc, xT, wT, y, wt, kb, xm, offs, out):
         a = {}
 
         def scores(h):
-            g, half = divmod(h, 2)
+            g, half = divmod(h, SPAN // PIECE)
             m = slice(half * PIECE // PACK, (half + 1) * PIECE // PACK)
             for b in range(SLOT_BLOCKS):
                 slots = slice(b * P, (b + 1) * P)
                 raw = psum.tile([P, PIECE], F32, name="raw", tag="scores" if h == 1 else "side")
                 matmul(raw[:], w_codes[:, slots], w_scales[:, slots], x_codes[h][:], x_scales[h][:], E4, True, True)
-                dealt, sums_in, bias = by_slot[g][b][:, :, m], raw[:].rearrange("p (m t) -> p t m", t=PACK), kb_col[:, b : b + 1]
-                nc.scalar.activation(out=dealt, in_=sums_in, func=ACT.Identity, bias=bias, scale=1.0)
+                nc.scalar.activation(
+                    out=by_slot[g][b][:, :, m],
+                    in_=raw[:].rearrange("p (m t) -> p t m", t=PACK),
+                    func=ACT.Identity,
+                    bias=kb_col[:, b : b + 1],
+                    scale=1.0,
+                )
 
         def row_max(k):
             g, t = divmod(k, PACK)
@@ -208,41 +212,41 @@ def tile_attend_gkl_w_kb_kernel(tc, xT, wT, y, wt, kb, xm, offs, out):
         m_codes = [keep.tile([P, SPANS * P], U32, name=f"m_codes{b}", align_bytes=64) for b in range(FEATURE_BLOCKS)]
         m_scales = [keep.tile([P, SPANS * P], U8, name=f"m_scales{b}", align_bytes=64) for b in range(FEATURE_BLOCKS)]
 
-        def prepare_xm(b, slot):
-            m_bf = keep.tile([P, SPANS * P, PACK], BF16, name=f"m_bf{b}", tag=slot, align_bytes=64)
+        def prepare_xm(b, tag):
+            m_bf = keep.tile([P, SPANS * P, PACK], BF16, name=f"m_bf{b}", tag=tag, align_bytes=64)
             for g in range(SPANS):
                 interleave(on_scalar, m_bf[:, g * P : (g + 1) * P, :], m_raw[g][:, :, b * P : (b + 1) * P])
             quantize(m_codes[b][:], m_scales[b][:], m_bf[:], E4)
 
         dw_sb = {}
 
-        def product(b, s0, s1, slot):
+        def product(b, s0, s1, tag):
             dw = psum.tile([P, N], F32, name="dw", tag="side")
             moving = slice(HALF + s1 - N, HALF + s1)
             for g in range(SPANS):
                 cols = slice(g * P, (g + 1) * P)
                 matmul(dw[:], m_codes[b][:, cols], m_scales[b][:, cols], g_codes[g][:, moving], g_scales[g][:, moving], E5, g == 0, g == SPANS - 1)
-            dw_sb[b, s0] = keep.tile([P, s1 - s0], F32, name=f"dw_sb{b}_{s0}", tag=slot, align_bytes=64)
+            dw_sb[b, s0] = keep.tile([P, s1 - s0], F32, name=f"dw_sb{b}_{s0}", tag=tag, align_bytes=64)
             nc.scalar.copy(out=dw_sb[b, s0][:], in_=dw[:, N - (s1 - s0) : N])
 
         def scatter(b, s0, s1):
-            window = windows[b % WINDOWS]
+            window = windows[b]
             nc.vector.tensor_copy(window[:].indirect(offsets[:, s0 // PER_COLUMN : s1 // PER_COLUMN]), dw_sb[b, s0][:])
             if s1 == N:
                 nc.sync.dma_start(out=out[b * P : (b + 1) * P, :], in_=window[:])
 
         for h in range(R // PIECE):
-            prepare_x(h, on_scalar if h < 2 else on_vector)
+            prepare_x(h, on_scalar if h < SPAN // PIECE else on_vector)
         for h in range(R // PIECE):
             scores(h)
 
-        for k in range(PACK + 2):
+        for k in range(TILES - 2):
             row_max(k)
         exponents(0)
         weigh_targets_on_gpsimd("wy_first", range(PACK), "x_bf3")
         factor_on_vector(0)
         weigh_targets_on_gpsimd("wy_last", range(PACK + 1, TILES), "wy_last")
-        for k in range(PACK + 2, TILES):
+        for k in range(TILES - 2, TILES):
             row_max(k)
         weigh_targets_on_vector(PACK, "y_raw3")
         exponents(1)
@@ -251,7 +255,7 @@ def tile_attend_gkl_w_kb_kernel(tc, xT, wT, y, wt, kb, xm, offs, out):
         for g in range(SPANS):
             gradient(g, EARLY)
         group_g(0, EARLY, (on_scalar,))
-        group_g(1, EARLY, (on_vector,))
+        group_g(1, EARLY, (on_scalar, on_vector))
         for g in range(SPANS):
             quantize_g(g, EARLY)
         prepare_xm(0, "m_bf0")

@@ -134,11 +134,6 @@ def tile_attend_gkl_w_kb_kernel(tc, xT, wT, y, wt, kb, xm, offs, out):
                     out=wy[k], in0=y_raw[k // 2][:, k % 2, :], scalar1=weights[:, g, t : t + 1], scalar2=0.0, op0=ALU.mult, op1=ALU.add
                 )
 
-        def weigh_targets_on_vector(k, tag):
-            g, t = divmod(k, PACK)
-            wy[k] = keep.tile([P, N], F32, name=f"wy{k}", tag=tag, align_bytes=64)[:]
-            nc.vector.tensor_scalar(out=wy[k], in0=y_raw[k // 2][:, k % 2, :], scalar1=weights[:, g, t : t + 1], scalar2=None, op0=ALU.mult)
-
         neg_max = keep.tile([P, TILES], F32, name="neg_max")
         sums = [keep.tile([P, PACK], F32, name=f"sums{g}") for g in range(SPANS)]
         inv = [keep.tile([P, PACK], F32, name=f"inv{g}") for g in range(SPANS)]
@@ -185,7 +180,7 @@ def tile_attend_gkl_w_kb_kernel(tc, xT, wT, y, wt, kb, xm, offs, out):
             for g in range(SPANS)
             for s0 in (EARLY, LATE)
         }
-        g_grouped = [keep.tile([P, N, PACK], BF16, name=f"g_grouped{g}", align_bytes=64) for g in range(SPANS)]
+        g_grouped = {}
 
         def gradient(g, s0):
             slots = slice(s0, s0 + HALF)
@@ -199,24 +194,34 @@ def tile_attend_gkl_w_kb_kernel(tc, xT, wT, y, wt, kb, xm, offs, out):
                     op1=ALU.subtract,
                 )
 
-        def group_g(g, s0, copies):
+        def group_g(g, s0, copies, tag):
+            g_grouped[g, s0] = keep.tile([P, HALF, PACK], BF16, name=f"g_grouped{g}_{s0}", tag=tag, align_bytes=64)
             width = HALF // len(copies)
             for n, copy in enumerate(copies):
                 c0 = n * width
-                interleave(copy, g_grouped[g][:, s0 + c0 : s0 + c0 + width, :], g_bf[g, s0][:, :, c0 : c0 + width])
+                interleave(copy, g_grouped[g, s0][:, c0 : c0 + width, :], g_bf[g, s0][:, :, c0 : c0 + width])
+
+        def group_g_on_gpsimd(g, s0, tag):
+            g_grouped[g, s0] = keep.tile([P, HALF, PACK], BF16, name=f"g_grouped{g}_{s0}", tag=tag, align_bytes=64)
+            nc.gpsimd.tensor_scalar(
+                out=g_grouped[g, s0][:], in0=g_bf[g, s0][:].rearrange("p j c -> p c j"), scalar1=1.0, scalar2=0.0, op0=ALU.mult, op1=ALU.add
+            )
 
         def quantize_g(g, s0):
             cols = slice(HALF + s0, HALF + s0 + HALF)
-            quantize(g_codes[g][:, cols], g_scales[g][:, cols], g_grouped[g][:, s0 : s0 + HALF, :], E5)
+            quantize(g_codes[g][:, cols], g_scales[g][:, cols], g_grouped[g, s0][:], E5)
 
         m_codes = [keep.tile([P, SPANS * P], U32, name=f"m_codes{b}", align_bytes=64) for b in range(FEATURE_BLOCKS)]
         m_scales = [keep.tile([P, SPANS * P], U8, name=f"m_scales{b}", align_bytes=64) for b in range(FEATURE_BLOCKS)]
 
-        def prepare_xm(b, tag):
+        def prepare_xm(b, tag, calls=1):
             m_bf = keep.tile([P, SPANS * P, PACK], BF16, name=f"m_bf{b}", tag=tag, align_bytes=64)
             for g in range(SPANS):
                 interleave(on_scalar, m_bf[:, g * P : (g + 1) * P, :], m_raw[g][:, :, b * P : (b + 1) * P])
-            quantize(m_codes[b][:], m_scales[b][:], m_bf[:], E4)
+            width = SPANS * P // calls
+            for n in range(calls):
+                cols = slice(n * width, (n + 1) * width)
+                quantize(m_codes[b][:, cols], m_scales[b][:, cols], m_bf[:, cols, :], E4)
 
         dw_sb = {}
 
@@ -245,36 +250,35 @@ def tile_attend_gkl_w_kb_kernel(tc, xT, wT, y, wt, kb, xm, offs, out):
         exponents(0)
         weigh_targets_on_gpsimd("wy_first", range(PACK), "x_bf3")
         factor_on_vector(0)
-        weigh_targets_on_gpsimd("wy_last", range(PACK + 1, TILES), "wy_last")
+        weigh_targets_on_gpsimd("wy_last", range(PACK, TILES), "wy_last")
         for k in range(TILES - 2, TILES):
             row_max(k)
-        weigh_targets_on_vector(PACK, "y_raw3")
         exponents(1)
         factor_on_vector(1)
 
         for g in range(SPANS):
             gradient(g, EARLY)
-        group_g(0, EARLY, (on_scalar,))
-        group_g(1, EARLY, (on_scalar, on_vector))
+        group_g(0, EARLY, (on_scalar,), "g_grouped0")
+        prepare_xm(0, "m_bf0", SPANS)
+        group_g(1, EARLY, (on_scalar, on_vector), "g_grouped1")
         for g in range(SPANS):
             quantize_g(g, EARLY)
-        prepare_xm(0, "m_bf0")
         product(0, EARLY, LATE, "dw_sb0_0")
 
         gradient(0, LATE)
         prepare_xm(1, f"g_bf1_{EARLY}")
-        group_g(0, LATE, (on_scalar, on_scalar))
         gradient(1, LATE)
-        group_g(1, LATE, (on_scalar,))
+        group_g_on_gpsimd(0, LATE, "wy_last")
+        group_g(1, LATE, (on_scalar,), "g_grouped_last")
         product(1, EARLY, LATE, f"g_bf0_{LATE}")
         scatter(0, EARLY, LATE)
         for g in range(SPANS):
             quantize_g(g, LATE)
-        prepare_xm(2, f"g_bf1_{LATE}")
+        prepare_xm(2, "wy_last")
         scatter(1, EARLY, LATE)
         for b in range(2):
             product(b, LATE, N, f"dw_sb{b}_{LATE}")
-        prepare_xm(3, "dw_sb0_0")
+        prepare_xm(3, f"g_bf0_{LATE}")
         for b in range(2):
             scatter(b, LATE, N)
         product(2, 0, N, "w_raw1")

@@ -171,9 +171,9 @@ def tile_attend_gkl_w_kb_kernel(tc, xT, wT, y, wt, kb, xm, offs, out):
                     out=e[k][:], in_=a[k][:], func=ACT.Exp, bias=neg_max[:, k : k + 1], scale=1.0, accum_out=sums[g][:, t : t + 1]
                 )
 
-        def factor_on_vector(g):
-            nc.vector.reciprocal(out=inv[g][:], in_=sums[g][:])
-            nc.vector.tensor_tensor(out=factor[g][:], in0=inv[g][:], in1=weights[:, g, :], op=ALU.mult)
+        def factor_on_vector(g, places):
+            nc.vector.reciprocal(out=inv[g][:, places], in_=sums[g][:, places])
+            nc.vector.tensor_tensor(out=factor[g][:, places], in0=inv[g][:, places], in1=weights[:, g, places], op=ALU.mult)
 
         g_bf = {
             (g, s0): keep.tile([P, PACK, HALF], BF16, name=f"g_bf{g}_{s0}", align_bytes=64)
@@ -249,12 +249,13 @@ def tile_attend_gkl_w_kb_kernel(tc, xT, wT, y, wt, kb, xm, offs, out):
             row_max(k)
         exponents(0)
         weigh_targets_on_gpsimd("wy_first", range(PACK), "x_bf3")
-        factor_on_vector(0)
+        factor_on_vector(0, slice(0, PACK))
         weigh_targets_on_gpsimd("wy_last", range(PACK, TILES), "wy_last")
         for k in range(TILES - 2, TILES):
             row_max(k)
         exponents(1)
-        factor_on_vector(1)
+        factor_on_vector(1, slice(0, PACK // 2))
+        factor_on_vector(1, slice(PACK // 2, PACK))
 
         for g in range(SPANS):
             gradient(g, EARLY)

@@ -73,11 +73,8 @@ def tile_attend_gkl_w_kb_kernel(tc, xT, wT, y, wt, kb, xm, offs, out):
         make_identity(nc, ident[:])
         windows = [keep.tile([P, T], F32, name=f"window{w}") for w in range(FEATURE_BLOCKS)]
         nc.vector.memset(windows[0][:].bitcast(I32), 0)
-        g_codes = [keep.tile([P, HALF + N], U32, name=f"g_codes{g}", align_bytes=64) for g in range(SPANS)]
-        g_scales = [keep.tile([P, HALF + N], U8, name=f"g_scales{g}", align_bytes=64) for g in range(SPANS)]
-        for g in range(SPANS):
-            nc.gpsimd.memset(g_codes[g][:, 0:HALF], 0)
-            nc.gpsimd.memset(g_scales[g][:, 0:HALF].bitcast(U32), 0)
+        g_codes = [keep.tile([P, N], U32, name=f"g_codes{g}", align_bytes=64) for g in range(SPANS)]
+        g_scales = [keep.tile([P, N], U8, name=f"g_scales{g}", align_bytes=64) for g in range(SPANS)]
         for window in windows[1:]:
             nc.gpsimd.memset(window[:].bitcast(I32), 0)
 
@@ -201,42 +198,52 @@ def tile_attend_gkl_w_kb_kernel(tc, xT, wT, y, wt, kb, xm, offs, out):
                 c0 = n * width
                 interleave(copy, g_grouped[g, s0][:, c0 : c0 + width, :], g_bf[g, s0][:, :, c0 : c0 + width])
 
-        def group_g_on_gpsimd(g, s0, tag):
-            g_grouped[g, s0] = keep.tile([P, HALF, PACK], BF16, name=f"g_grouped{g}_{s0}", tag=tag, align_bytes=64)
-            nc.gpsimd.tensor_scalar(
-                out=g_grouped[g, s0][:], in0=g_bf[g, s0][:].rearrange("p j c -> p c j"), scalar1=1.0, scalar2=0.0, op0=ALU.mult, op1=ALU.add
-            )
-
         def quantize_g(g, s0):
-            cols = slice(HALF + s0, HALF + s0 + HALF)
+            cols = slice(s0, s0 + HALF)
             quantize(g_codes[g][:, cols], g_scales[g][:, cols], g_grouped[g, s0][:], E5)
 
         m_codes = [keep.tile([P, SPANS * P], U32, name=f"m_codes{b}", align_bytes=64) for b in range(FEATURE_BLOCKS)]
         m_scales = [keep.tile([P, SPANS * P], U8, name=f"m_scales{b}", align_bytes=64) for b in range(FEATURE_BLOCKS)]
 
-        def prepare_xm(b, tag, calls=1):
-            m_bf = keep.tile([P, SPANS * P, PACK], BF16, name=f"m_bf{b}", tag=tag, align_bytes=64)
+        def on_gpsimd(out, in_):
+            nc.gpsimd.tensor_scalar(out=out, in0=in_, scalar1=1.0, scalar2=0.0, op0=ALU.mult, op1=ALU.add)
+
+        m_bf = {}
+
+        def cast_xm(b, engine, tag):
+            m_bf[b] = keep.tile([P, SPANS * P, PACK], BF16, name=f"m_bf{b}", tag=tag, align_bytes=64)
             for g in range(SPANS):
-                interleave(on_scalar, m_bf[:, g * P : (g + 1) * P, :], m_raw[g][:, :, b * P : (b + 1) * P])
+                dst, src = m_bf[b][:, g * P : (g + 1) * P, :], m_raw[g][:, :, b * P : (b + 1) * P]
+                if engine is on_gpsimd:
+                    on_gpsimd(dst, src.rearrange("p j c -> p c j"))
+                else:
+                    interleave(engine, dst, src)
+
+        def quantize_xm(b, calls=1):
             width = SPANS * P // calls
             for n in range(calls):
                 cols = slice(n * width, (n + 1) * width)
-                quantize(m_codes[b][:, cols], m_scales[b][:, cols], m_bf[:, cols, :], E4)
+                quantize(m_codes[b][:, cols], m_scales[b][:, cols], m_bf[b][:, cols, :], E4)
 
         dw_sb = {}
 
-        def product(b, s0, s1, tag):
-            dw = psum.tile([P, N], F32, name="dw", tag="side")
-            moving = slice(HALF + s1 - N, HALF + s1)
+        def product(b, s0, s1, copy, tag):
+            dw = psum.tile([P, s1 - s0], F32, name="dw", tag="side")
             for g in range(SPANS):
                 cols = slice(g * P, (g + 1) * P)
-                matmul(dw[:], m_codes[b][:, cols], m_scales[b][:, cols], g_codes[g][:, moving], g_scales[g][:, moving], E5, g == 0, g == SPANS - 1)
-            dw_sb[b, s0] = keep.tile([P, s1 - s0], F32, name=f"dw_sb{b}_{s0}", tag=tag, align_bytes=64)
-            nc.scalar.copy(out=dw_sb[b, s0][:], in_=dw[:, N - (s1 - s0) : N])
+                matmul(dw[:], m_codes[b][:, cols], m_scales[b][:, cols], g_codes[g][:, s0:s1], g_scales[g][:, s0:s1], E5, g == 0, g == SPANS - 1)
+            staged = keep.tile([P, s1 - s0], F32, name=f"dw_sb{b}_{s0}", tag=tag, align_bytes=64)
+            copy(out=staged[:], in_=dw[:])
+            for s in range(s0, s1, HALF):
+                dw_sb[b, s] = staged[:, s - s0 :]
 
-        def scatter(b, s0, s1):
+        def scatter(b, s0, s1, engine):
             window = windows[b]
-            nc.vector.tensor_copy(window[:].indirect(offsets[:, s0 // PER_COLUMN : s1 // PER_COLUMN]), dw_sb[b, s0][:])
+            places = window[:].indirect(offsets[:, s0 // PER_COLUMN : s1 // PER_COLUMN])
+            if engine is nc.vector:
+                nc.vector.tensor_copy(places, dw_sb[b, s0][:, 0 : s1 - s0])
+            else:
+                nc.scalar.activation(places, dw_sb[b, s0][:, 0 : s1 - s0], ACT.Copy)
             if s1 == N:
                 nc.sync.dma_start(out=out[b * P : (b + 1) * P, :], in_=window[:])
 
@@ -260,29 +267,33 @@ def tile_attend_gkl_w_kb_kernel(tc, xT, wT, y, wt, kb, xm, offs, out):
         for g in range(SPANS):
             gradient(g, EARLY)
         group_g(0, EARLY, (on_scalar,), "g_grouped0")
-        prepare_xm(0, "m_bf0", SPANS)
+        cast_xm(0, on_scalar, "m_bf0")
+        quantize_xm(0, SPANS)
         group_g(1, EARLY, (on_scalar, on_vector), "g_grouped1")
         for g in range(SPANS):
             quantize_g(g, EARLY)
-        product(0, EARLY, LATE, "dw_sb0_0")
+        product(0, EARLY, LATE, on_scalar, "dw_sb0_0")
 
         gradient(0, LATE)
-        prepare_xm(1, f"g_bf1_{EARLY}")
+        cast_xm(1, on_scalar, f"g_bf1_{EARLY}")
         gradient(1, LATE)
-        group_g_on_gpsimd(0, LATE, "wy_last")
-        group_g(1, LATE, (on_scalar,), "g_grouped_last")
-        product(1, EARLY, LATE, f"g_bf0_{LATE}")
-        scatter(0, EARLY, LATE)
+        group_g(0, LATE, (on_scalar,), "g_grouped0_late")
+        group_g(1, LATE, (on_vector,), "g_grouped1_late")
+        scatter(0, EARLY, LATE, nc.scalar)
         for g in range(SPANS):
             quantize_g(g, LATE)
-        prepare_xm(2, "wy_last")
-        scatter(1, EARLY, LATE)
-        for b in range(2):
-            product(b, LATE, N, f"dw_sb{b}_{LATE}")
-        prepare_xm(3, f"g_bf0_{LATE}")
-        for b in range(2):
-            scatter(b, LATE, N)
-        product(2, 0, N, "w_raw1")
-        product(3, 0, N, "dw_sb3_0")
-        for b in range(2, FEATURE_BLOCKS):
-            scatter(b, 0, N)
+        product(0, LATE, N, on_vector, "dw_sb0_late")
+        quantize_xm(1)
+        scatter(0, LATE, N, nc.vector)
+        product(1, 0, N, on_scalar, "dw_sb1")
+        cast_xm(2, on_gpsimd, "g_grouped1_late")
+        cast_xm(3, on_gpsimd, "g_grouped0_late")
+        scatter(1, EARLY, LATE, nc.scalar)
+        scatter(1, LATE, N, nc.scalar)
+        quantize_xm(2)
+        quantize_xm(3)
+        product(2, 0, N, on_vector, "g_grouped0_late")
+        scatter(2, 0, N, nc.vector)
+        product(3, 0, N, on_scalar, "dw_sb3")
+        scatter(3, EARLY, LATE, nc.scalar)
+        scatter(3, LATE, N, nc.scalar)

@@ -44,7 +44,7 @@ def tile_attend_gkl_w_kb_kernel(tc, xT, wT, y, wt, kb, xm, offs, out):
 
         offsets = keep.tile([P, N // PER_COLUMN], U16, name="offsets")
         w_raw = [keep.tile([P, T], F32, name=f"w_raw{j}", align_bytes=64) for j in range(PACK)]
-        x_raw = [keep.tile([P, PACK, PIECE], F32, name=f"x_raw{h}") for h in range(R // PIECE)]
+        x_raw = [keep.tile([P, PACK, PIECE], F32, name=f"x_raw{h}", align_bytes=64) for h in range(R // PIECE)]
         y_raw = [keep.tile([P, 2, N], F32, name=f"y_raw{u}", align_bytes=64) for u in range(TILES // 2)]
         m_raw = [keep.tile([P, PACK, D], F32, name=f"m_raw{g}", tag=f"w_raw{g}", align_bytes=64) for g in range(SPANS)]
         kb_row = keep.tile([P, T], F32, name="kb_row")
@@ -136,7 +136,9 @@ def tile_attend_gkl_w_kb_kernel(tc, xT, wT, y, wt, kb, xm, offs, out):
         inv = [keep.tile([P, PACK], F32, name=f"inv{g}") for g in range(SPANS)]
         factor = [keep.tile([P, PACK], F32, name=f"factor{g}") for g in range(SPANS)]
         e = [keep.tile([P, N], F32, name=f"e{k}") for k in range(TILES)]
-        by_slot = [[keep.tile([P, PACK, P], F32, name=f"by_slot{g}_{b}") for b in range(SLOT_BLOCKS)] for g in range(SPANS)]
+        by_slot = [[keep.tile([P, PACK, P], F32, name=f"by_slot{g}_{b}") for b in range(SLOT_BLOCKS)] for g in range(SPANS - 1)]
+        late_sums = keep.tile([P, SLOT_BLOCKS, PACK, P], F32, name="late_sums", tag="x_bf3", align_bytes=64)
+        by_slot.append([late_sums[:, b] for b in range(SLOT_BLOCKS)])
         a = {}
 
         def scores(h):
@@ -146,13 +148,11 @@ def tile_attend_gkl_w_kb_kernel(tc, xT, wT, y, wt, kb, xm, offs, out):
                 slots = slice(b * P, (b + 1) * P)
                 raw = psum.tile([P, PIECE], F32, name="raw", tag="scores" if h == 1 else "side")
                 matmul(raw[:], w_codes[:, slots], w_scales[:, slots], x_codes[h][:], x_scales[h][:], E4, True, True)
-                nc.scalar.activation(
-                    out=by_slot[g][b][:, :, m],
-                    in_=raw[:].rearrange("p (m t) -> p t m", t=PACK),
-                    func=ACT.Identity,
-                    bias=kb_col[:, b : b + 1],
-                    scale=1.0,
-                )
+                sums_out, sums_in = by_slot[g][b][:, :, m], raw[:].rearrange("p (m t) -> p t m", t=PACK)
+                if h == 2 and b < 2:
+                    nc.vector.tensor_scalar(out=sums_out, in0=sums_in, scalar1=kb_col[:, b : b + 1], scalar2=None, op0=ALU.add)
+                else:
+                    nc.scalar.activation(out=sums_out, in_=sums_in, func=ACT.Identity, bias=kb_col[:, b : b + 1], scale=1.0)
 
         def row_max(k):
             g, t = divmod(k, PACK)
@@ -228,7 +228,7 @@ def tile_attend_gkl_w_kb_kernel(tc, xT, wT, y, wt, kb, xm, offs, out):
         dw_sb = {}
 
         def product(b, s0, s1, copy, tag):
-            dw = psum.tile([P, s1 - s0], F32, name="dw", tag="side")
+            dw = late_bank if s0 == LATE else psum.tile([P, s1 - s0], F32, name="dw", tag="side")
             for g in range(SPANS):
                 cols = slice(g * P, (g + 1) * P)
                 matmul(dw[:], m_codes[b][:, cols], m_scales[b][:, cols], g_codes[g][:, s0:s1], g_scales[g][:, s0:s1], E5, g == 0, g == SPANS - 1)
@@ -255,7 +255,7 @@ def tile_attend_gkl_w_kb_kernel(tc, xT, wT, y, wt, kb, xm, offs, out):
         for k in range(TILES - 2):
             row_max(k)
         exponents(0)
-        weigh_targets_on_gpsimd("wy_first", range(PACK), "x_bf3")
+        weigh_targets_on_gpsimd("wy_first", range(PACK), "x_raw3")
         factor_on_vector(0, slice(0, PACK))
         weigh_targets_on_gpsimd("wy_last", range(PACK, TILES), "wy_last")
         for k in range(TILES - 2, TILES):
@@ -264,36 +264,41 @@ def tile_attend_gkl_w_kb_kernel(tc, xT, wT, y, wt, kb, xm, offs, out):
         factor_on_vector(1, slice(0, PACK // 2))
         factor_on_vector(1, slice(PACK // 2, PACK))
 
+        late_bank = psum.tile([P, HALF], F32, name="late_bank", tag="scores")
         for g in range(SPANS):
             gradient(g, EARLY)
         group_g(0, EARLY, (on_scalar,), "g_grouped0")
         cast_xm(0, on_scalar, "m_bf0")
         quantize_xm(0, SPANS)
-        group_g(1, EARLY, (on_scalar, on_vector), "g_grouped1")
+        group_g(1, EARLY, (on_vector,), "g_grouped1")
         for g in range(SPANS):
             quantize_g(g, EARLY)
-        product(0, EARLY, LATE, on_scalar, "dw_sb0_0")
+        product(0, EARLY, LATE, on_scalar, "dw_sb0")
 
         gradient(0, LATE)
-        cast_xm(1, on_scalar, f"g_bf1_{EARLY}")
-        gradient(1, LATE)
         group_g(0, LATE, (on_scalar,), "g_grouped0_late")
+        cast_xm(1, on_scalar, "m_bf1")
+        gradient(1, LATE)
         group_g(1, LATE, (on_vector,), "g_grouped1_late")
         scatter(0, EARLY, LATE, nc.scalar)
+        quantize_xm(1)
+        product(1, EARLY, LATE, on_scalar, "dw_sb1")
         for g in range(SPANS):
             quantize_g(g, LATE)
-        product(0, LATE, N, on_vector, "dw_sb0_late")
-        quantize_xm(1)
-        scatter(0, LATE, N, nc.vector)
-        product(1, 0, N, on_scalar, "dw_sb1")
-        cast_xm(2, on_gpsimd, "g_grouped1_late")
-        cast_xm(3, on_gpsimd, "g_grouped0_late")
-        scatter(1, EARLY, LATE, nc.scalar)
-        scatter(1, LATE, N, nc.scalar)
+        cast_xm(2, on_vector, "g_grouped1_late")
         quantize_xm(2)
+        cast_xm(3, on_gpsimd, "g_grouped1_late")
+        product(0, LATE, N, on_vector, "dw_sb0_late")
+        scatter(1, EARLY, LATE, nc.scalar)
+        scatter(0, LATE, N, nc.vector)
+        product(2, EARLY, LATE, on_scalar, "dw_sb2")
         quantize_xm(3)
-        product(2, 0, N, on_vector, "g_grouped0_late")
-        scatter(2, 0, N, nc.vector)
-        product(3, 0, N, on_scalar, "dw_sb3")
+        product(1, LATE, N, on_vector, "g_grouped1_late")
+        scatter(1, LATE, N, nc.vector)
+        scatter(2, EARLY, LATE, nc.scalar)
+        product(2, LATE, N, on_scalar, "dw_sb2_late")
+        product(3, EARLY, LATE, on_scalar, "dw_sb3")
+        scatter(2, LATE, N, nc.vector)
         scatter(3, EARLY, LATE, nc.scalar)
-        scatter(3, LATE, N, nc.scalar)
+        product(3, LATE, N, on_scalar, "dw_sb3_late")
+        scatter(3, LATE, N, nc.vector)

@@ -44,9 +44,10 @@ def tile_attend_gkl_w_kb_kernel(tc, xT, wT, y, wt, kb, xm, offs, out):
 
         offsets = keep.tile([P, N // PER_COLUMN], U16, name="offsets")
         w_raw = [keep.tile([P, T], F32, name=f"w_raw{j}", align_bytes=64) for j in range(PACK)]
-        x_raw = [keep.tile([P, PACK, PIECE], F32, name=f"x_raw{h}", align_bytes=64) for h in range(R // PIECE)]
+        x_first = keep.tile([P, PACK, SPAN], F32, name="x_first")
+        x_raw = [x_first[:, :, 0:PIECE], x_first[:, :, PIECE:SPAN]] + [keep.tile([P, PACK, PIECE], F32, name=f"x_raw{h}")[:] for h in (2, 3)]
         y_raw = [keep.tile([P, 2, N], F32, name=f"y_raw{u}", align_bytes=64) for u in range(TILES // 2)]
-        m_raw = [keep.tile([P, PACK, D], F32, name=f"m_raw{g}", tag=f"w_raw{g}", align_bytes=64) for g in range(SPANS)]
+        m_raw = [keep.tile([P, SPANS, PACK, D // 2], F32, name=f"m_raw{u}", tag=f"w_raw{u}", align_bytes=64) for u in range(2)]
         kb_row = keep.tile([P, T], F32, name="kb_row")
         weights = keep.tile([P, SPANS, 2 * PACK], F32, name="weights")[:, :, 0:PACK]
         w_rows = wT.rearrange("(p j) c -> p j c", j=PACK)
@@ -54,20 +55,23 @@ def tile_attend_gkl_w_kb_kernel(tc, xT, wT, y, wt, kb, xm, offs, out):
 
         nc.vector.memset(kb_row[:].bitcast(I32), 0)
         nc.sync.dma_start(out=w_raw[0][:], in_=w_rows[:, 0, :])
-        nc.scalar.dma_start(out=weights, in_=wt[0].rearrange("(g p t) o -> p g (t o)", g=SPANS, t=PACK))
         nc.sync.dma_start(offsets[:], offs)
         nc.sync.dma_start(out=w_raw[1][:], in_=w_rows[:, 1, :])
         nc.sync.dma_start(out=kb_row[0:1, :], in_=kb[0:1, :])
         for j in range(2, PACK):
             nc.sync.dma_start(out=w_raw[j][:], in_=w_rows[:, j, :])
-        for h in range(R // PIECE):
-            nc.sync.dma_start(out=x_raw[h][:], in_=x_rows[:, :, h * PIECE : (h + 1) * PIECE])
+        nc.sync.dma_start(out=x_first[:], in_=x_rows[:, :, 0:SPAN])
+        for h in (2, 3):
+            nc.sync.dma_start(out=x_raw[h], in_=x_rows[:, :, h * PIECE : (h + 1) * PIECE])
+        nc.sync.dma_start(out=weights, in_=wt[0].rearrange("(g p t) o -> p g (t o)", g=SPANS, t=PACK))
         y_rows = y[0].rearrange("(g p t) i -> p g t i", g=SPANS, t=PACK)
         for u in range(TILES // 2):
             g, t = divmod(2 * u, PACK)
             nc.sync.dma_start(out=y_raw[u][:], in_=y_rows[:, g, t : t + 2, :])
-        for g in range(SPANS):
-            nc.sync.dma_start(out=m_raw[g][:], in_=xm[0][g * SPAN : (g + 1) * SPAN, :].rearrange("(p t) d -> p t d", t=PACK))
+        m_rows = xm[0].rearrange("(g p t) d -> p g t d", g=SPANS, t=PACK)
+        for u in range(2):
+            for g in range(SPANS):
+                nc.sync.dma_start(out=m_raw[u][:, g], in_=m_rows[:, g, :, u * D // 2 : (u + 1) * D // 2])
 
         ident = keep.tile([P, P], F32, name="ident")
         make_identity(nc, ident[:])
@@ -113,12 +117,13 @@ def tile_attend_gkl_w_kb_kernel(tc, xT, wT, y, wt, kb, xm, offs, out):
         quantize(w_codes[:], w_scales[:], w_bf[:], E4)
 
         x_bf = [keep.tile([P, PIECE, PACK], BF16, name=f"x_bf{h}", align_bytes=64) for h in range(R // PIECE)]
-        x_codes = [keep.tile([P, PIECE], U32, name=f"x_codes{h}", align_bytes=64) for h in range(R // PIECE)]
-        x_scales = [keep.tile([P, PIECE], U8, name=f"x_scales{h}", align_bytes=64) for h in range(R // PIECE)]
+        x_codes = keep.tile([P, R], U32, name="x_codes", align_bytes=64)
+        x_scales = keep.tile([P, R], U8, name="x_scales", align_bytes=64)
 
         def prepare_x(h, copy):
-            interleave(copy, x_bf[h][:], x_raw[h][:])
-            quantize(x_codes[h][:], x_scales[h][:], x_bf[h][:], E4)
+            interleave(copy, x_bf[h][:], x_raw[h])
+            rows = slice(h * PIECE, (h + 1) * PIECE)
+            quantize(x_codes[:, rows], x_scales[:, rows], x_bf[h][:], E4)
 
         wy = {}
 
@@ -136,20 +141,18 @@ def tile_attend_gkl_w_kb_kernel(tc, xT, wT, y, wt, kb, xm, offs, out):
         inv = [keep.tile([P, PACK], F32, name=f"inv{g}") for g in range(SPANS)]
         factor = [keep.tile([P, PACK], F32, name=f"factor{g}") for g in range(SPANS)]
         e = [keep.tile([P, N], F32, name=f"e{k}") for k in range(TILES)]
-        by_slot = [[keep.tile([P, PACK, P], F32, name=f"by_slot{g}_{b}") for b in range(SLOT_BLOCKS)] for g in range(SPANS - 1)]
-        late_sums = keep.tile([P, SLOT_BLOCKS, PACK, P], F32, name="late_sums", tag="x_bf3", align_bytes=64)
-        by_slot.append([late_sums[:, b] for b in range(SLOT_BLOCKS)])
+        by_slot = [[keep.tile([P, PACK, P], F32, name=f"by_slot{g}_{b}") for b in range(SLOT_BLOCKS)] for g in range(SPANS)]
         a = {}
 
-        def scores(h):
-            g, half = divmod(h, SPAN // PIECE)
-            m = slice(half * PIECE // PACK, (half + 1) * PIECE // PACK)
+        def scores(r0, r1, tag, blocks_on_vector):
+            g = r0 // SPAN
+            m = slice(r0 % SPAN // PACK, r0 % SPAN // PACK + (r1 - r0) // PACK)
             for b in range(SLOT_BLOCKS):
                 slots = slice(b * P, (b + 1) * P)
-                raw = psum.tile([P, PIECE], F32, name="raw", tag="scores" if h == 1 else "side")
-                matmul(raw[:], w_codes[:, slots], w_scales[:, slots], x_codes[h][:], x_scales[h][:], E4, True, True)
+                raw = psum.tile([P, r1 - r0], F32, name="raw", tag=tag)
+                matmul(raw[:], w_codes[:, slots], w_scales[:, slots], x_codes[:, r0:r1], x_scales[:, r0:r1], E4, True, True)
                 sums_out, sums_in = by_slot[g][b][:, :, m], raw[:].rearrange("p (m t) -> p t m", t=PACK)
-                if h == 2 and b < 2:
+                if b < blocks_on_vector:
                     nc.vector.tensor_scalar(out=sums_out, in0=sums_in, scalar1=kb_col[:, b : b + 1], scalar2=None, op0=ALU.add)
                 else:
                     nc.scalar.activation(out=sums_out, in_=sums_in, func=ACT.Identity, bias=kb_col[:, b : b + 1], scale=1.0)
@@ -210,10 +213,10 @@ def tile_attend_gkl_w_kb_kernel(tc, xT, wT, y, wt, kb, xm, offs, out):
 
         m_bf = {}
 
-        def cast_xm(b, engine, tag):
-            m_bf[b] = keep.tile([P, SPANS * P, PACK], BF16, name=f"m_bf{b}", tag=tag, align_bytes=64)
+        def cast_xm(b, engine, tag, into=None):
+            m_bf[b] = into if into is not None else keep.tile([P, SPANS * P, PACK], BF16, name=f"m_bf{b}", tag=tag, align_bytes=64)[:]
             for g in range(SPANS):
-                dst, src = m_bf[b][:, g * P : (g + 1) * P, :], m_raw[g][:, :, b * P : (b + 1) * P]
+                dst, src = m_bf[b][:, g * P : (g + 1) * P, :], m_raw[b // 2][:, g, :, b % 2 * P : (b % 2 + 1) * P]
                 if engine is on_gpsimd:
                     on_gpsimd(dst, src.rearrange("p j c -> p c j"))
                 else:
@@ -227,13 +230,13 @@ def tile_attend_gkl_w_kb_kernel(tc, xT, wT, y, wt, kb, xm, offs, out):
 
         dw_sb = {}
 
-        def product(b, s0, s1, copy, tag):
+        def product(b, s0, s1, copy, tag, into=None):
             dw = late_bank if s0 == LATE else psum.tile([P, s1 - s0], F32, name="dw", tag="side")
             for g in range(SPANS):
                 cols = slice(g * P, (g + 1) * P)
                 matmul(dw[:], m_codes[b][:, cols], m_scales[b][:, cols], g_codes[g][:, s0:s1], g_scales[g][:, s0:s1], E5, g == 0, g == SPANS - 1)
-            staged = keep.tile([P, s1 - s0], F32, name=f"dw_sb{b}_{s0}", tag=tag, align_bytes=64)
-            copy(out=staged[:], in_=dw[:])
+            staged = into if into is not None else keep.tile([P, s1 - s0], F32, name=f"dw_sb{b}_{s0}", tag=tag, align_bytes=64)[:]
+            copy(out=staged, in_=dw[:])
             for s in range(s0, s1, HALF):
                 dw_sb[b, s] = staged[:, s - s0 :]
 
@@ -248,14 +251,15 @@ def tile_attend_gkl_w_kb_kernel(tc, xT, wT, y, wt, kb, xm, offs, out):
                 nc.sync.dma_start(out=out[b * P : (b + 1) * P, :], in_=window[:])
 
         for h in range(R // PIECE):
-            prepare_x(h, on_scalar if h < SPAN // PIECE else on_vector)
-        for h in range(R // PIECE):
-            scores(h)
+            prepare_x(h, on_scalar if h == 1 else on_vector)
+        scores(0, PIECE, "side", 0)
+        scores(PIECE, SPAN, "scores", 0)
+        scores(SPAN, R, "side", 1)
 
         for k in range(TILES - 2):
             row_max(k)
         exponents(0)
-        weigh_targets_on_gpsimd("wy_first", range(PACK), "x_raw3")
+        weigh_targets_on_gpsimd("wy_first", range(PACK), "x_bf3")
         factor_on_vector(0, slice(0, PACK))
         weigh_targets_on_gpsimd("wy_last", range(PACK, TILES), "wy_last")
         for k in range(TILES - 2, TILES):

@@ -44,8 +44,7 @@ def tile_attend_gkl_w_kb_kernel(tc, xT, wT, y, wt, kb, xm, offs, out):
 
         offsets = keep.tile([P, N // PER_COLUMN], U16, name="offsets")
         w_raw = [keep.tile([P, T], F32, name=f"w_raw{j}", align_bytes=64) for j in range(PACK)]
-        x_first = keep.tile([P, PACK, SPAN], F32, name="x_first")
-        x_raw = [x_first[:, :, 0:PIECE], x_first[:, :, PIECE:SPAN]] + [keep.tile([P, PACK, PIECE], F32, name=f"x_raw{h}")[:] for h in (2, 3)]
+        x_raw = [keep.tile([P, PACK, PIECE], F32, name=f"x_raw{h}")[:] for h in range(R // PIECE)]
         y_raw = [keep.tile([P, 2, N], F32, name=f"y_raw{u}", align_bytes=64) for u in range(TILES // 2)]
         m_raw = [keep.tile([P, SPANS, PACK, D // 2], F32, name=f"m_raw{u}", tag=f"w_raw{u}", align_bytes=64) for u in range(2)]
         kb_row = keep.tile([P, T], F32, name="kb_row")
@@ -60,8 +59,7 @@ def tile_attend_gkl_w_kb_kernel(tc, xT, wT, y, wt, kb, xm, offs, out):
         nc.sync.dma_start(out=kb_row[0:1, :], in_=kb[0:1, :])
         for j in range(2, PACK):
             nc.sync.dma_start(out=w_raw[j][:], in_=w_rows[:, j, :])
-        nc.sync.dma_start(out=x_first[:], in_=x_rows[:, :, 0:SPAN])
-        for h in (2, 3):
+        for h in range(R // PIECE):
             nc.sync.dma_start(out=x_raw[h], in_=x_rows[:, :, h * PIECE : (h + 1) * PIECE])
         nc.sync.dma_start(out=weights, in_=wt[0].rearrange("(g p t) o -> p g (t o)", g=SPANS, t=PACK))
         y_rows = y[0].rearrange("(g p t) i -> p g t i", g=SPANS, t=PACK)
@@ -127,8 +125,9 @@ def tile_attend_gkl_w_kb_kernel(tc, xT, wT, y, wt, kb, xm, offs, out):
 
         wy = {}
 
-        def weigh_targets_on_gpsimd(name, tiles, tag):
-            weighted = keep.tile([P, len(tiles), N], F32, name=name, tag=tag, align_bytes=64)
+        held = keep.tile([P, PACK + 1, N], F32, name="held", tag="x_bf3", align_bytes=64)
+
+        def weigh_targets_on_gpsimd(weighted, tiles):
             for n, k in enumerate(tiles):
                 g, t = divmod(k, PACK)
                 wy[k] = weighted[:, n, :]
@@ -141,18 +140,19 @@ def tile_attend_gkl_w_kb_kernel(tc, xT, wT, y, wt, kb, xm, offs, out):
         inv = [keep.tile([P, PACK], F32, name=f"inv{g}") for g in range(SPANS)]
         factor = [keep.tile([P, PACK], F32, name=f"factor{g}") for g in range(SPANS)]
         e = [keep.tile([P, N], F32, name=f"e{k}") for k in range(TILES)]
-        by_slot = [[keep.tile([P, PACK, P], F32, name=f"by_slot{g}_{b}") for b in range(SLOT_BLOCKS)] for g in range(SPANS)]
+        by_slot = [[keep.tile([P, PACK, P], F32, name=f"by_slot{g}_{b}") if (g, b) != (0, SLOT_BLOCKS - 1) else None for b in range(SLOT_BLOCKS)] for g in range(SPANS)]
+        by_slot[0][SLOT_BLOCKS - 1] = held[:, PACK, :].rearrange("p (t m) -> p t m", t=PACK)
         a = {}
 
-        def scores(r0, r1, tag, blocks_on_vector):
+        def scores(r0, r1, tag, blocks, blocks_on_vector):
             g = r0 // SPAN
             m = slice(r0 % SPAN // PACK, r0 % SPAN // PACK + (r1 - r0) // PACK)
-            for b in range(SLOT_BLOCKS):
+            for b in blocks:
                 slots = slice(b * P, (b + 1) * P)
                 raw = psum.tile([P, r1 - r0], F32, name="raw", tag=tag)
                 matmul(raw[:], w_codes[:, slots], w_scales[:, slots], x_codes[:, r0:r1], x_scales[:, r0:r1], E4, True, True)
                 sums_out, sums_in = by_slot[g][b][:, :, m], raw[:].rearrange("p (m t) -> p t m", t=PACK)
-                if b < blocks_on_vector:
+                if b in blocks_on_vector:
                     nc.vector.tensor_scalar(out=sums_out, in0=sums_in, scalar1=kb_col[:, b : b + 1], scalar2=None, op0=ALU.add)
                 else:
                     nc.scalar.activation(out=sums_out, in_=sums_in, func=ACT.Identity, bias=kb_col[:, b : b + 1], scale=1.0)
@@ -213,9 +213,9 @@ def tile_attend_gkl_w_kb_kernel(tc, xT, wT, y, wt, kb, xm, offs, out):
 
         m_bf = {}
 
-        def cast_xm(b, engine, tag, into=None):
+        def cast_xm(b, engines, tag, into=None):
             m_bf[b] = into if into is not None else keep.tile([P, SPANS * P, PACK], BF16, name=f"m_bf{b}", tag=tag, align_bytes=64)[:]
-            for g in range(SPANS):
+            for g, engine in enumerate(engines):
                 dst, src = m_bf[b][:, g * P : (g + 1) * P, :], m_raw[b // 2][:, g, :, b % 2 * P : (b % 2 + 1) * P]
                 if engine is on_gpsimd:
                     on_gpsimd(dst, src.rearrange("p j c -> p c j"))
@@ -228,17 +228,21 @@ def tile_attend_gkl_w_kb_kernel(tc, xT, wT, y, wt, kb, xm, offs, out):
                 cols = slice(n * width, (n + 1) * width)
                 quantize(m_codes[b][:, cols], m_scales[b][:, cols], m_bf[b][:, cols, :], E4)
 
-        dw_sb = {}
+        dw_ps, dw_sb = {}, {}
 
-        def product(b, s0, s1, copy, tag, into=None):
-            dw = late_bank if s0 == LATE else psum.tile([P, s1 - s0], F32, name="dw", tag="side")
+        def product(b, s0, s1, dw):
             for g in range(SPANS):
                 cols = slice(g * P, (g + 1) * P)
-                matmul(dw[:], m_codes[b][:, cols], m_scales[b][:, cols], g_codes[g][:, s0:s1], g_scales[g][:, s0:s1], E5, g == 0, g == SPANS - 1)
-            staged = into if into is not None else keep.tile([P, s1 - s0], F32, name=f"dw_sb{b}_{s0}", tag=tag, align_bytes=64)[:]
-            copy(out=staged, in_=dw[:])
+                matmul(dw, m_codes[b][:, cols], m_scales[b][:, cols], g_codes[g][:, s0:s1], g_scales[g][:, s0:s1], E5, g == 0, g == SPANS - 1)
             for s in range(s0, s1, HALF):
-                dw_sb[b, s] = staged[:, s - s0 :]
+                dw_ps[b, s] = dw[:, s - s0 : s - s0 + HALF]
+
+        def bank(columns):
+            return psum.tile([P, columns], F32, name="dw", tag="side")[:]
+
+        def stage(b, s0, copy, tag, into=None):
+            dw_sb[b, s0] = into if into is not None else keep.tile([P, HALF], F32, name=f"dw_sb{b}_{s0}", tag=tag, align_bytes=64)[:]
+            copy(out=dw_sb[b, s0], in_=dw_ps[b, s0])
 
         def scatter(b, s0, s1, engine):
             window = windows[b]
@@ -251,58 +255,67 @@ def tile_attend_gkl_w_kb_kernel(tc, xT, wT, y, wt, kb, xm, offs, out):
                 nc.sync.dma_start(out=out[b * P : (b + 1) * P, :], in_=window[:])
 
         for h in range(R // PIECE):
-            prepare_x(h, on_scalar if h == 1 else on_vector)
-        scores(0, PIECE, "side", 0)
-        scores(PIECE, SPAN, "scores", 0)
-        scores(SPAN, R, "side", 1)
+            prepare_x(h, on_scalar if h < 2 else on_vector)
+        scores(0, PIECE, "side", (0, 1, 2), ())
+        scores(PIECE, SPAN, "scores", (0, 1, 2), ())
+        scores(0, SPAN, "scores", (3,), (3,))
+        scores(SPAN, R, "side", (0, 1, 2, 3), (0,))
 
         for k in range(TILES - 2):
             row_max(k)
         exponents(0)
-        weigh_targets_on_gpsimd("wy_first", range(PACK), "x_bf3")
+        weigh_targets_on_gpsimd(held, range(PACK))
         factor_on_vector(0, slice(0, PACK))
-        weigh_targets_on_gpsimd("wy_last", range(PACK, TILES), "wy_last")
+        weigh_targets_on_gpsimd(keep.tile([P, PACK, N], F32, name="wy_last"), range(PACK, TILES))
         for k in range(TILES - 2, TILES):
             row_max(k)
         exponents(1)
         factor_on_vector(1, slice(0, PACK // 2))
         factor_on_vector(1, slice(PACK // 2, PACK))
 
-        late_bank = psum.tile([P, HALF], F32, name="late_bank", tag="scores")
         for g in range(SPANS):
             gradient(g, EARLY)
         group_g(0, EARLY, (on_scalar,), "g_grouped0")
-        cast_xm(0, on_scalar, "m_bf0")
+        cast_xm(0, (on_gpsimd, on_gpsimd), "m_bf0")
         quantize_xm(0, SPANS)
-        group_g(1, EARLY, (on_vector,), "g_grouped1")
+        group_g(1, EARLY, (on_scalar,), "g_grouped1")
         for g in range(SPANS):
             quantize_g(g, EARLY)
-        product(0, EARLY, LATE, on_scalar, "dw_sb0")
+        product(0, EARLY, LATE, bank(HALF))
+        stage(0, EARLY, on_scalar, "dw_sb0")
 
         gradient(0, LATE)
         group_g(0, LATE, (on_scalar,), "g_grouped0_late")
-        cast_xm(1, on_scalar, "m_bf1")
+        cast_xm(1, (on_scalar, on_scalar), "m_bf1")
         gradient(1, LATE)
         group_g(1, LATE, (on_vector,), "g_grouped1_late")
         scatter(0, EARLY, LATE, nc.scalar)
         quantize_xm(1)
-        product(1, EARLY, LATE, on_scalar, "dw_sb1")
+        product(1, EARLY, LATE, bank(HALF))
+        stage(1, EARLY, on_scalar, "dw_sb1")
         for g in range(SPANS):
             quantize_g(g, LATE)
-        cast_xm(2, on_vector, "g_grouped1_late")
+        late_bank = psum.tile([P, HALF], F32, name="late_bank", tag="scores")[:]
+        cast_xm(2, (on_vector, on_vector), "g_grouped1_late")
         quantize_xm(2)
-        cast_xm(3, on_gpsimd, "g_grouped1_late")
-        product(0, LATE, N, on_vector, "dw_sb0_late")
+        cast_xm(3, (on_gpsimd, on_gpsimd), "g_grouped1_late")
+        product(0, LATE, N, late_bank)
+        stage(0, LATE, on_vector, "dw_sb0_late")
         scatter(1, EARLY, LATE, nc.scalar)
         scatter(0, LATE, N, nc.vector)
-        product(2, EARLY, LATE, on_scalar, "dw_sb2")
+        product(2, EARLY, LATE, bank(HALF))
+        stage(2, EARLY, on_scalar, "dw_sb2")
         quantize_xm(3)
-        product(1, LATE, N, on_vector, "g_grouped1_late")
+        product(1, LATE, N, late_bank)
+        stage(1, LATE, on_vector, "g_grouped1_late")
         scatter(1, LATE, N, nc.vector)
         scatter(2, EARLY, LATE, nc.scalar)
-        product(2, LATE, N, on_scalar, "dw_sb2_late")
-        product(3, EARLY, LATE, on_scalar, "dw_sb3")
+        product(2, LATE, N, late_bank)
+        stage(2, LATE, on_scalar, "dw_sb2_late")
+        product(3, EARLY, LATE, bank(HALF))
+        stage(3, EARLY, on_scalar, "dw_sb3")
         scatter(2, LATE, N, nc.vector)
         scatter(3, EARLY, LATE, nc.scalar)
-        product(3, LATE, N, on_scalar, "dw_sb3_late")
+        product(3, LATE, N, late_bank)
+        stage(3, LATE, on_scalar, "dw_sb3_late")
         scatter(3, LATE, N, nc.vector)

@@ -213,14 +213,13 @@ def tile_attend_gkl_w_kb_kernel(tc, xT, wT, y, wt, kb, xm, offs, out):
 
         m_bf = {}
 
-        def cast_xm(b, engines, tag, into=None):
-            m_bf[b] = into if into is not None else keep.tile([P, SPANS * P, PACK], BF16, name=f"m_bf{b}", tag=tag, align_bytes=64)[:]
-            for g, engine in enumerate(engines):
-                dst, src = m_bf[b][:, g * P : (g + 1) * P, :], m_raw[b // 2][:, g, :, b % 2 * P : (b % 2 + 1) * P]
-                if engine is on_gpsimd:
-                    on_gpsimd(dst, src.rearrange("p j c -> p c j"))
-                else:
-                    interleave(engine, dst, src)
+        def cast_xm(b, engine, tag):
+            m_bf[b] = keep.tile([P, SPANS * P, PACK], BF16, name=f"m_bf{b}", tag=tag, align_bytes=64)
+            dst, src = m_bf[b][:].rearrange("p (g c) j -> p g c j", g=SPANS), m_raw[b // 2][:, :, :, b % 2 * P : (b % 2 + 1) * P]
+            if engine is on_gpsimd:
+                on_gpsimd(dst, src.rearrange("p g j c -> p g c j"))
+            else:
+                engine(out=dst.rearrange("p g (c i) j -> p g c j i", i=4), in_=src.rearrange("p g j (c i) -> p g c j i", i=4))
 
         def quantize_xm(b, calls=1):
             width = SPANS * P // calls
@@ -276,9 +275,9 @@ def tile_attend_gkl_w_kb_kernel(tc, xT, wT, y, wt, kb, xm, offs, out):
         for g in range(SPANS):
             gradient(g, EARLY)
         group_g(0, EARLY, (on_scalar,), "g_grouped0")
-        cast_xm(0, (on_gpsimd, on_gpsimd), "m_bf0")
+        cast_xm(0, on_scalar, "m_bf0")
         quantize_xm(0, SPANS)
-        group_g(1, EARLY, (on_scalar,), "g_grouped1")
+        group_g(1, EARLY, (on_vector,), "g_grouped1")
         for g in range(SPANS):
             quantize_g(g, EARLY)
         product(0, EARLY, LATE, bank(HALF))
@@ -286,7 +285,7 @@ def tile_attend_gkl_w_kb_kernel(tc, xT, wT, y, wt, kb, xm, offs, out):
 
         gradient(0, LATE)
         group_g(0, LATE, (on_scalar,), "g_grouped0_late")
-        cast_xm(1, (on_scalar, on_scalar), "m_bf1")
+        cast_xm(1, on_scalar, "m_bf1")
         gradient(1, LATE)
         group_g(1, LATE, (on_vector,), "g_grouped1_late")
         scatter(0, EARLY, LATE, nc.scalar)
@@ -296,9 +295,9 @@ def tile_attend_gkl_w_kb_kernel(tc, xT, wT, y, wt, kb, xm, offs, out):
         for g in range(SPANS):
             quantize_g(g, LATE)
         late_bank = psum.tile([P, HALF], F32, name="late_bank", tag="scores")[:]
-        cast_xm(2, (on_vector, on_vector), "g_grouped1_late")
+        cast_xm(2, on_vector, "g_grouped1_late")
         quantize_xm(2)
-        cast_xm(3, (on_gpsimd, on_gpsimd), "g_grouped1_late")
+        cast_xm(3, on_gpsimd, "g_grouped1_late")
         product(0, LATE, N, late_bank)
         stage(0, LATE, on_vector, "dw_sb0_late")
         scatter(1, EARLY, LATE, nc.scalar)

@@ -23,16 +23,19 @@ SPAN = P * PACK
 SPANS = R // SPAN
 TILES = SPANS * PACK
 PIECE = SPAN // 2
+PIECES = R // PIECE
 SLOT_BLOCKS = N // P
 FEATURE_BLOCKS = D // P
+BLOCK_PAIRS = FEATURE_BLOCKS // 2
 HALF = N // 2
 EARLY, LATE = 0, HALF
 PER_COLUMN = 16
 PSUM_BUFS = 4
+RUN = 4
 
 
 def interleave(copy, dst, src):
-    copy(out=dst.rearrange("p (c i) j -> p c j i", i=4), in_=src.rearrange("p j (c i) -> p c j i", i=4))
+    copy(out=dst.rearrange("p (c i) j -> p c j i", i=RUN), in_=src.rearrange("p j (c i) -> p c j i", i=RUN))
 
 
 def tile_attend_gkl_w_kb_kernel(tc, xT, wT, y, wt, kb, xm, offs, out):
@@ -44,9 +47,9 @@ def tile_attend_gkl_w_kb_kernel(tc, xT, wT, y, wt, kb, xm, offs, out):
 
         offsets = keep.tile([P, N // PER_COLUMN], U16, name="offsets")
         w_raw = [keep.tile([P, T], F32, name=f"w_raw{j}", align_bytes=64) for j in range(PACK)]
-        x_raw = [keep.tile([P, PACK, PIECE], F32, name=f"x_raw{h}")[:] for h in range(R // PIECE)]
+        x_raw = [keep.tile([P, PACK, PIECE], F32, name=f"x_raw{h}")[:] for h in range(PIECES)]
         y_raw = [keep.tile([P, 2, N], F32, name=f"y_raw{u}", align_bytes=64) for u in range(TILES // 2)]
-        m_raw = [keep.tile([P, SPANS, PACK, D // 2], F32, name=f"m_raw{u}", tag=f"w_raw{u}", align_bytes=64) for u in range(2)]
+        m_raw = [keep.tile([P, SPANS, PACK, 2 * P], F32, name=f"m_raw{u}", tag=f"w_raw{u}", align_bytes=64) for u in range(BLOCK_PAIRS)]
         kb_row = keep.tile([P, T], F32, name="kb_row")
         weights = keep.tile([P, SPANS, 2 * PACK], F32, name="weights")[:, :, 0:PACK]
         w_rows = wT.rearrange("(p j) c -> p j c", j=PACK)
@@ -59,7 +62,7 @@ def tile_attend_gkl_w_kb_kernel(tc, xT, wT, y, wt, kb, xm, offs, out):
         nc.sync.dma_start(out=kb_row[0:1, :], in_=kb[0:1, :])
         for j in range(2, PACK):
             nc.sync.dma_start(out=w_raw[j][:], in_=w_rows[:, j, :])
-        for h in range(R // PIECE):
+        for h in range(PIECES):
             nc.sync.dma_start(out=x_raw[h], in_=x_rows[:, :, h * PIECE : (h + 1) * PIECE])
         nc.sync.dma_start(out=weights, in_=wt[0].rearrange("(g p t) o -> p g (t o)", g=SPANS, t=PACK))
         y_rows = y[0].rearrange("(g p t) i -> p g t i", g=SPANS, t=PACK)
@@ -67,9 +70,9 @@ def tile_attend_gkl_w_kb_kernel(tc, xT, wT, y, wt, kb, xm, offs, out):
             g, t = divmod(2 * u, PACK)
             nc.sync.dma_start(out=y_raw[u][:], in_=y_rows[:, g, t : t + 2, :])
         m_rows = xm[0].rearrange("(g p t) d -> p g t d", g=SPANS, t=PACK)
-        for u in range(2):
+        for u in range(BLOCK_PAIRS):
             for g in range(SPANS):
-                nc.sync.dma_start(out=m_raw[u][:, g], in_=m_rows[:, g, :, u * D // 2 : (u + 1) * D // 2])
+                nc.sync.dma_start(out=m_raw[u][:, g], in_=m_rows[:, g, :, 2 * u * P : 2 * (u + 1) * P])
 
         ident = keep.tile([P, P], F32, name="ident")
         make_identity(nc, ident[:])
@@ -114,7 +117,7 @@ def tile_attend_gkl_w_kb_kernel(tc, xT, wT, y, wt, kb, xm, offs, out):
             nc.vector.tensor_copy(w_bf[:, :, j], w_raw[j][:].indirect(offsets[:]))
         quantize(w_codes[:], w_scales[:], w_bf[:], E4)
 
-        x_bf = [keep.tile([P, PIECE, PACK], BF16, name=f"x_bf{h}", align_bytes=64) for h in range(R // PIECE)]
+        x_bf = [keep.tile([P, PIECE, PACK], BF16, name=f"x_bf{h}", align_bytes=64) for h in range(PIECES)]
         x_codes = keep.tile([P, R], U32, name="x_codes", align_bytes=64)
         x_scales = keep.tile([P, R], U8, name="x_scales", align_bytes=64)
 
@@ -124,8 +127,7 @@ def tile_attend_gkl_w_kb_kernel(tc, xT, wT, y, wt, kb, xm, offs, out):
             quantize(x_codes[:, rows], x_scales[:, rows], x_bf[h][:], E4)
 
         wy = {}
-
-        held = keep.tile([P, PACK + 1, N], F32, name="held", tag="x_bf3", align_bytes=64)
+        after_x = keep.tile([P, PACK + 1, N], F32, name="held", tag=f"x_bf{PIECES - 1}", align_bytes=64)
 
         def weigh_targets_on_gpsimd(weighted, tiles):
             for n, k in enumerate(tiles):
@@ -140,28 +142,36 @@ def tile_attend_gkl_w_kb_kernel(tc, xT, wT, y, wt, kb, xm, offs, out):
         inv = [keep.tile([P, PACK], F32, name=f"inv{g}") for g in range(SPANS)]
         factor = [keep.tile([P, PACK], F32, name=f"factor{g}") for g in range(SPANS)]
         e = [keep.tile([P, N], F32, name=f"e{k}") for k in range(TILES)]
-        by_slot = [[keep.tile([P, PACK, P], F32, name=f"by_slot{g}_{b}") if (g, b) != (0, SLOT_BLOCKS - 1) else None for b in range(SLOT_BLOCKS)] for g in range(SPANS)]
-        by_slot[0][SLOT_BLOCKS - 1] = held[:, PACK, :].rearrange("p (t m) -> p t m", t=PACK)
+        last_block = SLOT_BLOCKS - 1
+        by_slot = {
+            (g, b): keep.tile([P, PACK, P], F32, name=f"by_slot{g}_{b}")
+            for g in range(SPANS)
+            for b in range(SLOT_BLOCKS)
+            if (g, b) != (0, last_block)
+        }
+        by_slot[0, last_block] = after_x[:, PACK, :].rearrange("p (t m) -> p t m", t=PACK)
         a = {}
 
-        def scores(r0, r1, tag, blocks, blocks_on_vector):
+        def add_on_scalar(sums_out, raw, bias):
+            nc.scalar.activation(out=sums_out, in_=raw, func=ACT.Identity, bias=bias, scale=1.0)
+
+        def add_on_vector(sums_out, raw, bias):
+            nc.vector.tensor_scalar(out=sums_out, in0=raw, scalar1=bias, scalar2=None, op0=ALU.add)
+
+        def scores(r0, r1, blocks, add, tag):
             g = r0 // SPAN
-            m = slice(r0 % SPAN // PACK, r0 % SPAN // PACK + (r1 - r0) // PACK)
+            m = slice((r0 - g * SPAN) // PACK, (r1 - g * SPAN) // PACK)
             for b in blocks:
                 slots = slice(b * P, (b + 1) * P)
                 raw = psum.tile([P, r1 - r0], F32, name="raw", tag=tag)
                 matmul(raw[:], w_codes[:, slots], w_scales[:, slots], x_codes[:, r0:r1], x_scales[:, r0:r1], E4, True, True)
-                sums_out, sums_in = by_slot[g][b][:, :, m], raw[:].rearrange("p (m t) -> p t m", t=PACK)
-                if b in blocks_on_vector:
-                    nc.vector.tensor_scalar(out=sums_out, in0=sums_in, scalar1=kb_col[:, b : b + 1], scalar2=None, op0=ALU.add)
-                else:
-                    nc.scalar.activation(out=sums_out, in_=sums_in, func=ACT.Identity, bias=kb_col[:, b : b + 1], scale=1.0)
+                add(by_slot[g, b][:, :, m], raw[:].rearrange("p (m t) -> p t m", t=PACK), kb_col[:, b : b + 1])
 
         def row_max(k):
             g, t = divmod(k, PACK)
             a[k] = psum.tile([P, N], F32, name="turned", tag=("scores", "side")[g])
             for b in range(SLOT_BLOCKS):
-                nc.tensor.transpose(a[k][:, b * P : (b + 1) * P], by_slot[g][b][:, t, :], ident[:])
+                nc.tensor.transpose(a[k][:, b * P : (b + 1) * P], by_slot[g, b][:, t, :], ident[:])
             nc.vector.tensor_reduce(out=neg_max[:, k : k + 1], in_=a[k][:], axis=mybir.AxisListType.X, op=ALU.max, negate=True)
 
         def exponents(g):
@@ -171,7 +181,7 @@ def tile_attend_gkl_w_kb_kernel(tc, xT, wT, y, wt, kb, xm, offs, out):
                     out=e[k][:], in_=a[k][:], func=ACT.Exp, bias=neg_max[:, k : k + 1], scale=1.0, accum_out=sums[g][:, t : t + 1]
                 )
 
-        def factor_on_vector(g, places):
+        def row_factor(g, places):
             nc.vector.reciprocal(out=inv[g][:, places], in_=sums[g][:, places])
             nc.vector.tensor_tensor(out=factor[g][:, places], in0=inv[g][:, places], in1=weights[:, g, places], op=ALU.mult)
 
@@ -194,12 +204,9 @@ def tile_attend_gkl_w_kb_kernel(tc, xT, wT, y, wt, kb, xm, offs, out):
                     op1=ALU.subtract,
                 )
 
-        def group_g(g, s0, copies, tag):
-            g_grouped[g, s0] = keep.tile([P, HALF, PACK], BF16, name=f"g_grouped{g}_{s0}", tag=tag, align_bytes=64)
-            width = HALF // len(copies)
-            for n, copy in enumerate(copies):
-                c0 = n * width
-                interleave(copy, g_grouped[g, s0][:, c0 : c0 + width, :], g_bf[g, s0][:, :, c0 : c0 + width])
+        def group_g(g, s0, copy):
+            g_grouped[g, s0] = keep.tile([P, HALF, PACK], BF16, name=f"g_grouped{g}_{s0}", align_bytes=64)
+            interleave(copy, g_grouped[g, s0][:], g_bf[g, s0][:])
 
         def quantize_g(g, s0):
             cols = slice(s0, s0 + HALF)
@@ -207,19 +214,15 @@ def tile_attend_gkl_w_kb_kernel(tc, xT, wT, y, wt, kb, xm, offs, out):
 
         m_codes = [keep.tile([P, SPANS * P], U32, name=f"m_codes{b}", align_bytes=64) for b in range(FEATURE_BLOCKS)]
         m_scales = [keep.tile([P, SPANS * P], U8, name=f"m_scales{b}", align_bytes=64) for b in range(FEATURE_BLOCKS)]
-
-        def on_gpsimd(out, in_):
-            nc.gpsimd.tensor_scalar(out=out, in0=in_, scalar1=1.0, scalar2=0.0, op0=ALU.mult, op1=ALU.add)
-
         m_bf = {}
 
-        def cast_xm(b, engine, tag):
-            m_bf[b] = keep.tile([P, SPANS * P, PACK], BF16, name=f"m_bf{b}", tag=tag, align_bytes=64)
-            dst, src = m_bf[b][:].rearrange("p (g c) j -> p g c j", g=SPANS), m_raw[b // 2][:, :, :, b % 2 * P : (b % 2 + 1) * P]
-            if engine is on_gpsimd:
-                on_gpsimd(dst, src.rearrange("p g j c -> p g c j"))
-            else:
-                engine(out=dst.rearrange("p g (c i) j -> p g c j i", i=4), in_=src.rearrange("p g j (c i) -> p g c j i", i=4))
+        def cast_xm(b, copy, grouped):
+            m_bf[b] = grouped
+            src = m_raw[b // 2][:, :, :, b % 2 * P : (b % 2 + 1) * P]
+            copy(
+                out=grouped.rearrange("p (g c i) j -> p g c j i", g=SPANS, i=RUN),
+                in_=src.rearrange("p g j (c i) -> p g c j i", i=RUN),
+            )
 
         def quantize_xm(b, calls=1):
             width = SPANS * P // calls
@@ -227,94 +230,98 @@ def tile_attend_gkl_w_kb_kernel(tc, xT, wT, y, wt, kb, xm, offs, out):
                 cols = slice(n * width, (n + 1) * width)
                 quantize(m_codes[b][:, cols], m_scales[b][:, cols], m_bf[b][:, cols, :], E4)
 
-        dw_ps, dw_sb = {}, {}
+        staged = {}
+
+        def bank(columns):
+            return psum.tile([P, columns], F32, name="dw", tag="side")[:]
 
         def product(b, s0, s1, dw):
             for g in range(SPANS):
                 cols = slice(g * P, (g + 1) * P)
                 matmul(dw, m_codes[b][:, cols], m_scales[b][:, cols], g_codes[g][:, s0:s1], g_scales[g][:, s0:s1], E5, g == 0, g == SPANS - 1)
-            for s in range(s0, s1, HALF):
-                dw_ps[b, s] = dw[:, s - s0 : s - s0 + HALF]
 
-        def bank(columns):
-            return psum.tile([P, columns], F32, name="dw", tag="side")[:]
+        def stage(copy, dw, *halves):
+            b, s0 = halves[0]
+            copied = keep.tile([P, len(halves) * HALF], F32, name=f"staged{b}_{s0}", align_bytes=64)
+            copy(out=copied[:], in_=dw)
+            for n, half in enumerate(halves):
+                staged[half] = copied[:, n * HALF : (n + 1) * HALF]
 
-        def stage(b, s0, copy, tag, into=None):
-            dw_sb[b, s0] = into if into is not None else keep.tile([P, HALF], F32, name=f"dw_sb{b}_{s0}", tag=tag, align_bytes=64)[:]
-            copy(out=dw_sb[b, s0], in_=dw_ps[b, s0])
+        def half_product(b, s0, copy):
+            dw = bank(HALF)
+            product(b, s0, s0 + HALF, dw)
+            stage(copy, dw, (b, s0))
 
-        def scatter(b, s0, s1, engine):
-            window = windows[b]
-            places = window[:].indirect(offsets[:, s0 // PER_COLUMN : s1 // PER_COLUMN])
-            if engine is nc.vector:
-                nc.vector.tensor_copy(places, dw_sb[b, s0][:, 0 : s1 - s0])
-            else:
-                nc.scalar.activation(places, dw_sb[b, s0][:, 0 : s1 - s0], ACT.Copy)
-            if s1 == N:
-                nc.sync.dma_start(out=out[b * P : (b + 1) * P, :], in_=window[:])
+        def places(b, s0):
+            return windows[b][:].indirect(offsets[:, s0 // PER_COLUMN : (s0 + HALF) // PER_COLUMN])
 
-        for h in range(R // PIECE):
-            prepare_x(h, on_scalar if h < 2 else on_vector)
-        scores(0, PIECE, "side", (0, 1, 2), ())
-        scores(PIECE, SPAN, "scores", (0, 1, 2), ())
-        scores(0, SPAN, "scores", (3,), (3,))
-        scores(SPAN, R, "side", (0, 1, 2, 3), (0,))
+        def scatter_early(b):
+            nc.scalar.activation(places(b, EARLY), staged[b, EARLY], ACT.Copy)
+
+        def scatter_late_and_store(b):
+            nc.vector.tensor_copy(places(b, LATE), staged[b, LATE])
+            nc.sync.dma_start(out=out[b * P : (b + 1) * P, :], in_=windows[b][:])
+
+        for h in range(PIECES):
+            prepare_x(h, on_scalar if h < SPAN // PIECE else on_vector)
+
+        scores(0, PIECE, range(last_block), add_on_scalar, "side")
+        scores(PIECE, SPAN, range(last_block), add_on_scalar, "scores")
+        scores(0, SPAN, [last_block], add_on_vector, "scores")
+        scores(SPAN, R, [0], add_on_vector, "side")
+        scores(SPAN, R, range(1, SLOT_BLOCKS), add_on_scalar, "side")
 
         for k in range(TILES - 2):
             row_max(k)
         exponents(0)
-        weigh_targets_on_gpsimd(held, range(PACK))
-        factor_on_vector(0, slice(0, PACK))
+        weigh_targets_on_gpsimd(after_x, range(PACK))
+        row_factor(0, slice(0, PACK))
         weigh_targets_on_gpsimd(keep.tile([P, PACK, N], F32, name="wy_last"), range(PACK, TILES))
         for k in range(TILES - 2, TILES):
             row_max(k)
         exponents(1)
-        factor_on_vector(1, slice(0, PACK // 2))
-        factor_on_vector(1, slice(PACK // 2, PACK))
+        row_factor(1, slice(0, PACK // 2))
+        row_factor(1, slice(PACK // 2, PACK))
 
         for g in range(SPANS):
             gradient(g, EARLY)
-        group_g(0, EARLY, (on_scalar,), "g_grouped0")
-        cast_xm(0, on_scalar, "m_bf0")
+        group_g(0, EARLY, on_scalar)
+        cast_xm(0, on_scalar, keep.tile([P, SPANS * P, PACK], BF16, name="m_bf0", align_bytes=64)[:])
         quantize_xm(0, SPANS)
-        group_g(1, EARLY, (on_vector,), "g_grouped1")
+        group_g(1, EARLY, on_vector)
         for g in range(SPANS):
             quantize_g(g, EARLY)
-        product(0, EARLY, LATE, bank(HALF))
-        stage(0, EARLY, on_scalar, "dw_sb0")
+        half_product(0, EARLY, on_scalar)
 
         gradient(0, LATE)
-        group_g(0, LATE, (on_scalar,), "g_grouped0_late")
-        cast_xm(1, on_scalar, "m_bf1")
+        group_g(0, LATE, on_scalar)
+        cast_xm(1, on_scalar, keep.tile([P, SPANS * P, PACK], BF16, name="m_bf1", align_bytes=64)[:])
         gradient(1, LATE)
-        group_g(1, LATE, (on_vector,), "g_grouped1_late")
-        scatter(0, EARLY, LATE, nc.scalar)
+        group_g(1, LATE, on_vector)
+        scatter_early(0)
         quantize_xm(1)
-        product(1, EARLY, LATE, bank(HALF))
-        stage(1, EARLY, on_scalar, "dw_sb1")
+        half_product(1, EARLY, on_scalar)
         for g in range(SPANS):
             quantize_g(g, LATE)
-        late_bank = psum.tile([P, HALF], F32, name="late_bank", tag="scores")[:]
-        cast_xm(2, on_vector, "g_grouped1_late")
+
+        m_last = keep.tile([P, 2, SPANS * P, PACK], BF16, name="m_last", tag=f"g_grouped1_{LATE}", align_bytes=64)
+        cast_xm(2, on_vector, m_last[:, 0])
+        cast_xm(3, on_vector, m_last[:, 1])
+        half_product(0, LATE, on_vector)
         quantize_xm(2)
-        cast_xm(3, on_gpsimd, "g_grouped1_late")
-        product(0, LATE, N, late_bank)
-        stage(0, LATE, on_vector, "dw_sb0_late")
-        scatter(1, EARLY, LATE, nc.scalar)
-        scatter(0, LATE, N, nc.vector)
-        product(2, EARLY, LATE, bank(HALF))
-        stage(2, EARLY, on_scalar, "dw_sb2")
+        scatter_early(1)
+        scatter_late_and_store(0)
         quantize_xm(3)
-        product(1, LATE, N, late_bank)
-        stage(1, LATE, on_vector, "g_grouped1_late")
-        scatter(1, LATE, N, nc.vector)
-        scatter(2, EARLY, LATE, nc.scalar)
-        product(2, LATE, N, late_bank)
-        stage(2, LATE, on_scalar, "dw_sb2_late")
-        product(3, EARLY, LATE, bank(HALF))
-        stage(3, EARLY, on_scalar, "dw_sb3")
-        scatter(2, LATE, N, nc.vector)
-        scatter(3, EARLY, LATE, nc.scalar)
-        product(3, LATE, N, late_bank)
-        stage(3, LATE, on_scalar, "dw_sb3_late")
-        scatter(3, LATE, N, nc.vector)
+
+        pair = bank(N)
+        product(1, LATE, N, pair[:, 0:HALF])
+        product(2, EARLY, LATE, pair[:, HALF:N])
+        stage(on_scalar, pair, (1, LATE), (2, EARLY))
+        scatter_late_and_store(1)
+        scatter_early(2)
+        half_product(2, LATE, on_vector)
+        product(3, 0, N, pair)
+        stage(on_scalar, pair, (3, EARLY), (3, LATE))
+        scatter_late_and_store(2)
+        scatter_early(3)
+        scatter_late_and_store(3)

@@ -304,11 +304,18 @@ def tile_attend_gkl_w_kb_kernel(tc, xT, wT, y, wt, kb, xm, offs, out):
         for g in range(SPANS):
             quantize_g(g, LATE)
 
-        m_last = keep.tile([P, 2, SPANS * P, PACK], BF16, name="m_last", tag=f"g_grouped1_{LATE}", align_bytes=64)
-        cast_xm(2, on_vector, m_last[:, 0])
-        cast_xm(3, on_vector, m_last[:, 1])
+        cast_xm(2, on_vector, keep.tile([P, SPANS * P, PACK], BF16, name="m_bf2", tag=f"g_grouped1_{LATE}", align_bytes=64)[:])
         half_product(0, LATE, on_vector)
         quantize_xm(2)
+        m_bf[3] = keep.tile([P, SPANS * P, PACK], BF16, name="m_bf3", tag=f"g_grouped1_{LATE}", align_bytes=64)[:]
+        nc.gpsimd.tensor_scalar(
+            out=m_bf[3].rearrange("p (g c) j -> p g c j", g=SPANS),
+            in0=m_raw[1][:, :, :, P : 2 * P].rearrange("p g j c -> p g c j"),
+            scalar1=1.0,
+            scalar2=0.0,
+            op0=ALU.mult,
+            op1=ALU.add,
+        )
         scatter_early(1)
         scatter_late_and_store(0)
         quantize_xm(3)

@@ -31,6 +31,7 @@ HALF = N // 2
 EARLY, LATE = 0, HALF
 PER_COLUMN = 16
 PSUM_BUFS = 4
+PAIR = 2
 RUN = 4
 
 
@@ -127,7 +128,7 @@ def tile_attend_gkl_w_kb_kernel(tc, xT, wT, y, wt, kb, xm, offs, out):
             quantize(x_codes[:, rows], x_scales[:, rows], x_bf[h][:], E4)
 
         wy = {}
-        after_x = keep.tile([P, PACK + 1, N], F32, name="held", tag=f"x_bf{PIECES - 1}", align_bytes=64)
+        after_x = keep.tile([P, PACK, N], F32, name="held", tag=f"x_bf{PIECES - 1}", align_bytes=64)
 
         def weigh_targets_on_gpsimd(weighted, tiles):
             for n, k in enumerate(tiles):
@@ -140,7 +141,7 @@ def tile_attend_gkl_w_kb_kernel(tc, xT, wT, y, wt, kb, xm, offs, out):
         neg_max = keep.tile([P, TILES], F32, name="neg_max")
         sums = [keep.tile([P, PACK], F32, name=f"sums{g}") for g in range(SPANS)]
         inv = [keep.tile([P, PACK], F32, name=f"inv{g}") for g in range(SPANS)]
-        factor = [keep.tile([P, PACK], F32, name=f"factor{g}") for g in range(SPANS)]
+        factor = keep.tile([P, PACK], F32, name="factor")
         e = [keep.tile([P, N], F32, name=f"e{k}") for k in range(TILES)]
         last_block = SLOT_BLOCKS - 1
         by_slot = {
@@ -149,7 +150,7 @@ def tile_attend_gkl_w_kb_kernel(tc, xT, wT, y, wt, kb, xm, offs, out):
             for b in range(SLOT_BLOCKS)
             if (g, b) != (0, last_block)
         }
-        by_slot[0, last_block] = after_x[:, PACK, :].rearrange("p (t m) -> p t m", t=PACK)
+        by_slot[0, last_block] = keep.tile([P, PACK, P], F32, name="by_slot_held", tag=f"x_raw{PIECES - 1}")
         a = {}
 
         def add_on_scalar(sums_out, raw, bias):
@@ -181,32 +182,39 @@ def tile_attend_gkl_w_kb_kernel(tc, xT, wT, y, wt, kb, xm, offs, out):
                     out=e[k][:], in_=a[k][:], func=ACT.Exp, bias=neg_max[:, k : k + 1], scale=1.0, accum_out=sums[g][:, t : t + 1]
                 )
 
-        def row_factor(g, places):
-            nc.vector.reciprocal(out=inv[g][:, places], in_=sums[g][:, places])
-            nc.vector.tensor_tensor(out=factor[g][:, places], in0=inv[g][:, places], in1=weights[:, g, places], op=ALU.mult)
 
-        g_bf = {
-            (g, s0): keep.tile([P, PACK, HALF], BF16, name=f"g_bf{g}_{s0}", align_bytes=64)
-            for g in range(SPANS)
-            for s0 in (EARLY, LATE)
+        g_bf = {s0: keep.tile([P, PACK, HALF], BF16, name=f"g_bf{s0}", align_bytes=64) for s0 in (EARLY, LATE)}
+        g_grouped = {
+            (g, s0): keep.tile([P, HALF, PACK], BF16, name=f"g_grouped{g}_{s0}", align_bytes=64) for g in range(SPANS) for s0 in (EARLY, LATE)
         }
-        g_grouped = {}
+        wy_last = keep.tile([P, PACK, N], F32, name="wy_last")
+        scaled = keep.tile([P, PACK, N], F32, name="scaled", tag="w_raw2", align_bytes=64)
 
-        def gradient(g, s0):
+        def first_gradient(s0):
             slots = slice(s0, s0 + HALF)
             for t in range(PACK):
                 nc.vector.scalar_tensor_tensor(
-                    out=g_bf[g, s0][:, t, :],
-                    in0=e[g * PACK + t][:, slots],
-                    scalar=factor[g][:, t : t + 1],
-                    in1=wy[g * PACK + t][:, slots],
+                    out=g_bf[s0][:, t, :], in0=e[t][:, slots], scalar=factor[:, t : t + 1], in1=wy[t][:, slots], op0=ALU.mult, op1=ALU.subtract
+                )
+            interleave(on_scalar, g_grouped[0, s0][:], g_bf[s0][:])
+
+        def scale_last(s0):
+            slots = slice(s0, s0 + HALF)
+            for t in range(PACK):
+                nc.vector.tensor_scalar(
+                    out=scaled[:, t, slots],
+                    in0=e[PACK + t][:, slots],
+                    scalar1=inv[1][:, t : t + 1],
+                    scalar2=weights[:, 1, t : t + 1],
                     op0=ALU.mult,
-                    op1=ALU.subtract,
+                    op1=ALU.mult,
                 )
 
-        def group_g(g, s0, copy):
-            g_grouped[g, s0] = keep.tile([P, HALF, PACK], BF16, name=f"g_grouped{g}_{s0}", align_bytes=64)
-            interleave(copy, g_grouped[g, s0][:], g_bf[g, s0][:])
+        def last_gradient(s0):
+            first, second = (src[:, :, s0 : s0 + HALF].rearrange("p j (c i) -> p c j i", i=PAIR) for src in (scaled, wy_last))
+            nc.vector.tensor_tensor(
+                out=g_grouped[1, s0][:].rearrange("p (c i) j -> p c j i", i=PAIR), in0=first, in1=second, op=ALU.subtract
+            )
 
         def quantize_g(g, s0):
             cols = slice(s0, s0 + HALF)
@@ -275,29 +283,28 @@ def tile_attend_gkl_w_kb_kernel(tc, xT, wT, y, wt, kb, xm, offs, out):
             row_max(k)
         exponents(0)
         weigh_targets_on_gpsimd(after_x, range(PACK))
-        row_factor(0, slice(0, PACK))
-        weigh_targets_on_gpsimd(keep.tile([P, PACK, N], F32, name="wy_last"), range(PACK, TILES))
+        nc.vector.reciprocal(out=inv[0][:], in_=sums[0][:])
+        nc.gpsimd.tensor_tensor(out=factor[:], in0=inv[0][:], in1=weights[:, 0, :], op=ALU.mult)
+        weigh_targets_on_gpsimd(wy_last, range(PACK, TILES))
         for k in range(TILES - 2, TILES):
             row_max(k)
         exponents(1)
-        row_factor(1, slice(0, PACK // 2))
-        row_factor(1, slice(PACK // 2, PACK))
 
-        for g in range(SPANS):
-            gradient(g, EARLY)
-        group_g(0, EARLY, on_scalar)
+        first_gradient(EARLY)
+        for places_of_pair in (slice(0, PACK // 2), slice(PACK // 2, PACK)):
+            nc.vector.reciprocal(out=inv[1][:, places_of_pair], in_=sums[1][:, places_of_pair])
+        scale_last(EARLY)
+        last_gradient(EARLY)
         cast_xm(0, on_scalar, keep.tile([P, SPANS * P, PACK], BF16, name="m_bf0", align_bytes=64)[:])
         quantize_xm(0, SPANS)
-        group_g(1, EARLY, on_vector)
         for g in range(SPANS):
             quantize_g(g, EARLY)
         half_product(0, EARLY, on_scalar)
 
-        gradient(0, LATE)
-        group_g(0, LATE, on_scalar)
+        first_gradient(LATE)
         cast_xm(1, on_scalar, keep.tile([P, SPANS * P, PACK], BF16, name="m_bf1", align_bytes=64)[:])
-        gradient(1, LATE)
-        group_g(1, LATE, on_vector)
+        scale_last(LATE)
+        last_gradient(LATE)
         scatter_early(0)
         quantize_xm(1)
         half_product(1, EARLY, on_scalar)
@@ -324,9 +331,9 @@ def tile_attend_gkl_w_kb_kernel(tc, xT, wT, y, wt, kb, xm, offs, out):
         product(1, LATE, N, pair[:, 0:HALF])
         product(2, EARLY, LATE, pair[:, HALF:N])
         stage(on_scalar, pair, (1, LATE), (2, EARLY))
+        half_product(2, LATE, on_vector)
         scatter_late_and_store(1)
         scatter_early(2)
-        half_product(2, LATE, on_vector)
         product(3, 0, N, pair)
         stage(on_scalar, pair, (3, EARLY), (3, LATE))
         scatter_late_and_store(2)

@@ -277,7 +277,9 @@ def tile_attend_gkl_w_kb_kernel(tc, xT, wT, y, wt, kb, xm, offs, out):
         scores(PIECE, SPAN, range(last_block), add_on_scalar, "scores")
         scores(0, SPAN, [last_block], add_on_vector, "scores")
         scores(SPAN, R, [0], add_on_vector, "side")
-        scores(SPAN, R, range(1, SLOT_BLOCKS), add_on_scalar, "side")
+        scores(SPAN, R, [1], add_on_scalar, "side")
+        scores(SPAN, R, [2], add_on_vector, "side")
+        scores(SPAN, R, [3], add_on_scalar, "side")
 
         for k in range(TILES - 2):
             row_max(k)
@@ -306,15 +308,15 @@ def tile_attend_gkl_w_kb_kernel(tc, xT, wT, y, wt, kb, xm, offs, out):
         scale_last(LATE)
         last_gradient(LATE)
         scatter_early(0)
-        quantize_xm(1)
-        half_product(1, EARLY, on_scalar)
         for g in range(SPANS):
             quantize_g(g, LATE)
+        quantize_xm(1)
+        half_product(1, EARLY, on_scalar)
 
-        cast_xm(2, on_vector, keep.tile([P, SPANS * P, PACK], BF16, name="m_bf2", tag=f"g_grouped1_{LATE}", align_bytes=64)[:])
+        cast_xm(2, on_vector, keep.tile([P, SPANS * P, PACK], BF16, name="m_bf2", tag=f"g_grouped0_{LATE}", align_bytes=64)[:])
         half_product(0, LATE, on_vector)
         quantize_xm(2)
-        m_bf[3] = keep.tile([P, SPANS * P, PACK], BF16, name="m_bf3", tag=f"g_grouped1_{LATE}", align_bytes=64)[:]
+        m_bf[3] = keep.tile([P, SPANS * P, PACK], BF16, name="m_bf3", tag=f"g_grouped0_{LATE}", align_bytes=64)[:]
         nc.gpsimd.tensor_scalar(
             out=m_bf[3].rearrange("p (g c) j -> p g c j", g=SPANS),
             in0=m_raw[1][:, :, :, P : 2 * P].rearrange("p g j c -> p g c j"),

from contextlib import ExitStack

import concourse.mybir as mybir
from concourse.masks import make_identity

N, T, D, R = 512, 2048, 512, 1024
FLOPS = 2 * 2 * N * D * R

F32 = mybir.dt.float32
BF16 = mybir.dt.bfloat16
U32 = mybir.dt.uint32
I32 = mybir.dt.int32
U16 = mybir.dt.uint16
U8 = mybir.dt.uint8
E4 = mybir.dt.float8_e4m3fn_x4
E5 = mybir.dt.float8_e5m2_x4
ALU = mybir.AluOpType
ACT = mybir.ActivationFunctionType

P = 128
PACK = 4
SPAN = P * PACK
SPANS = R // SPAN
TILES = SPANS * PACK
PIECE = SPAN // 2
PIECES = R // PIECE
SLOT_BLOCKS = N // P
FEATURE_BLOCKS = D // P
BLOCK_PAIRS = FEATURE_BLOCKS // 2
HALF = N // 2
EARLY, LATE = 0, HALF
PER_COLUMN = 16
PSUM_BUFS = 4
PAIR = 2
RUN = 4


def interleave(copy, dst, src):
    copy(out=dst.rearrange("p (c i) j -> p c j i", i=RUN), in_=src.rearrange("p j (c i) -> p c j i", i=RUN))


def tile_attend_gkl_w_kb_kernel(tc, xT, wT, y, wt, kb, xm, offs, out):
    nc = tc.nc
    on_scalar, on_vector = nc.scalar.copy, nc.vector.tensor_copy
    with ExitStack() as ctx:
        keep = ctx.enter_context(tc.tile_pool(name="keep", bufs=1))
        psum = ctx.enter_context(tc.psum_pool(name="psum", bufs=PSUM_BUFS))

        offsets = keep.tile([P, N // PER_COLUMN], U16, name="offsets")
        w_raw = [keep.tile([P, T], F32, name=f"w_raw{j}", align_bytes=64) for j in range(PACK)]
        x_raw = [keep.tile([P, PACK, PIECE], F32, name=f"x_raw{h}")[:] for h in range(PIECES)]
        y_raw = [keep.tile([P, 2, N], F32, name=f"y_raw{u}", align_bytes=64) for u in range(TILES // 2)]
        m_raw = [keep.tile([P, SPANS, PACK, 2 * P], F32, name=f"m_raw{u}", tag=f"w_raw{u}", align_bytes=64) for u in range(BLOCK_PAIRS)]
        kb_row = keep.tile([P, T], F32, name="kb_row")
        weights = keep.tile([P, SPANS, 2 * PACK], F32, name="weights")[:, :, 0:PACK]
        w_rows = wT.rearrange("(p j) c -> p j c", j=PACK)
        x_rows = xT[0].rearrange("(p j) r -> p j r", j=PACK)

        nc.vector.memset(kb_row[:].bitcast(I32), 0)
        nc.sync.dma_start(out=w_raw[0][:], in_=w_rows[:, 0, :])
        nc.sync.dma_start(offsets[:], offs)
        nc.sync.dma_start(out=w_raw[1][:], in_=w_rows[:, 1, :])
        nc.sync.dma_start(out=kb_row[0:1, :], in_=kb[0:1, :])
        for j in range(2, PACK):
            nc.sync.dma_start(out=w_raw[j][:], in_=w_rows[:, j, :])
        for h in range(PIECES):
            nc.sync.dma_start(out=x_raw[h], in_=x_rows[:, :, h * PIECE : (h + 1) * PIECE])
        nc.sync.dma_start(out=weights, in_=wt[0].rearrange("(g p t) o -> p g (t o)", g=SPANS, t=PACK))
        y_rows = y[0].rearrange("(g p t) i -> p g t i", g=SPANS, t=PACK)
        for u in range(TILES // 2):
            g, t = divmod(2 * u, PACK)
            nc.sync.dma_start(out=y_raw[u][:], in_=y_rows[:, g, t : t + 2, :])
        m_rows = xm[0].rearrange("(g p t) d -> p g t d", g=SPANS, t=PACK)
        for u in range(BLOCK_PAIRS):
            for g in range(SPANS):
                nc.sync.dma_start(out=m_raw[u][:, g], in_=m_rows[:, g, :, 2 * u * P : 2 * (u + 1) * P])

        ident = keep.tile([P, P], F32, name="ident")
        make_identity(nc, ident[:])
        windows = [keep.tile([P, T], F32, name=f"window{w}") for w in range(FEATURE_BLOCKS)]
        nc.vector.memset(windows[0][:].bitcast(I32), 0)
        g_codes = [keep.tile([P, N], U32, name=f"g_codes{g}", align_bytes=64) for g in range(SPANS)]
        g_scales = [keep.tile([P, N], U8, name=f"g_scales{g}", align_bytes=64) for g in range(SPANS)]
        for window in windows[1:]:
            nc.gpsimd.memset(window[:].bitcast(I32), 0)

        def quantize(codes, scales, grouped, fmt):
            nc.vector.quantize_mx(out=codes.bitcast(fmt), scales=scales, in_=grouped.rearrange("p c j -> p (c j)"))

        def matmul(acc, lhs_codes, lhs_scales, rhs_codes, rhs_scales, rhs_fmt, start, stop):
            nc.tensor.matmul_mx(
                out=acc,
                lhsT=lhs_codes.bitcast(E4),
                lhsT_scale=lhs_scales,
                rhs=rhs_codes.bitcast(rhs_fmt),
                rhs_scale=rhs_scales,
                start=start,
                stop=stop,
            )

        w_bf = keep.tile([P, N, PACK], BF16, name="w_bf", align_bytes=64)
        w_codes = keep.tile([P, N], U32, name="w_codes", align_bytes=64)
        w_scales = keep.tile([P, N], U8, name="w_scales", align_bytes=64)
        w_pair = keep.tile([P, 2, N], F32, name="w_pair")
        for j in range(2):
            nc.vector.tensor_copy(w_pair[:, j, :], w_raw[j][:].indirect(offsets[:]))
        nc.scalar.copy(out=w_bf[:, :, 0:2], in_=w_pair[:].rearrange("p j c -> p c j"))

        kb_picked = keep.tile([P, N], F32, name="kb_picked")
        nc.vector.tensor_copy(kb_picked[:], kb_row[:].indirect(offsets[:]))
        kb_turned = psum.tile([P, SLOT_BLOCKS, P], F32, name="kb_turned", tag="side")
        for b in range(SLOT_BLOCKS):
            nc.tensor.transpose(kb_turned[:, b, :], kb_picked[:, b * P : (b + 1) * P], ident[:])
        kb_col = keep.tile([P, SLOT_BLOCKS], F32, name="kb_col")
        nc.scalar.copy(out=kb_col[:], in_=kb_turned[:, :, 0])

        for j in range(2, PACK):
            nc.vector.tensor_copy(w_bf[:, :, j], w_raw[j][:].indirect(offsets[:]))
        quantize(w_codes[:], w_scales[:], w_bf[:], E4)

        x_bf = [keep.tile([P, PIECE, PACK], BF16, name=f"x_bf{h}", align_bytes=64) for h in range(PIECES)]
        x_codes = keep.tile([P, R], U32, name="x_codes", align_bytes=64)
        x_scales = keep.tile([P, R], U8, name="x_scales", align_bytes=64)

        def prepare_x(h, copy):
            interleave(copy, x_bf[h][:], x_raw[h])
            rows = slice(h * PIECE, (h + 1) * PIECE)
            quantize(x_codes[:, rows], x_scales[:, rows], x_bf[h][:], E4)

        wy = {}
        after_x = keep.tile([P, PACK, N], F32, name="held", tag=f"x_bf{PIECES - 1}", align_bytes=64)

        def weigh_targets_on_gpsimd(weighted, tiles):
            for n, k in enumerate(tiles):
                g, t = divmod(k, PACK)
                wy[k] = weighted[:, n, :]
                nc.gpsimd.tensor_scalar(
                    out=wy[k], in0=y_raw[k // 2][:, k % 2, :], scalar1=weights[:, g, t : t + 1], scalar2=0.0, op0=ALU.mult, op1=ALU.add
                )

        neg_max = keep.tile([P, TILES], F32, name="neg_max")
        sums = [keep.tile([P, PACK], F32, name=f"sums{g}") for g in range(SPANS)]
        inv = [keep.tile([P, PACK], F32, name=f"inv{g}") for g in range(SPANS)]
        factor = keep.tile([P, PACK], F32, name="factor")
        e = [keep.tile([P, N], F32, name=f"e{k}") for k in range(TILES)]
        last_block = SLOT_BLOCKS - 1
        by_slot = {
            (g, b): keep.tile([P, PACK, P], F32, name=f"by_slot{g}_{b}")
            for g in range(SPANS)
            for b in range(SLOT_BLOCKS)
            if (g, b) != (0, last_block)
        }
        by_slot[0, last_block] = keep.tile([P, PACK, P], F32, name="by_slot_held", tag=f"x_raw{PIECES - 1}")
        a = {}

        def add_on_scalar(sums_out, raw, bias):
            nc.scalar.activation(out=sums_out, in_=raw, func=ACT.Identity, bias=bias, scale=1.0)

        def add_on_vector(sums_out, raw, bias):
            nc.vector.tensor_scalar(out=sums_out, in0=raw, scalar1=bias, scalar2=None, op0=ALU.add)

        def scores(r0, r1, blocks, add, tag):
            g = r0 // SPAN
            m = slice((r0 - g * SPAN) // PACK, (r1 - g * SPAN) // PACK)
            for b in blocks:
                slots = slice(b * P, (b + 1) * P)
                raw = psum.tile([P, r1 - r0], F32, name="raw", tag=tag)
                matmul(raw[:], w_codes[:, slots], w_scales[:, slots], x_codes[:, r0:r1], x_scales[:, r0:r1], E4, True, True)
                add(by_slot[g, b][:, :, m], raw[:].rearrange("p (m t) -> p t m", t=PACK), kb_col[:, b : b + 1])

        def row_max(k):
            g, t = divmod(k, PACK)
            a[k] = psum.tile([P, N], F32, name="turned", tag=("scores", "side")[g])
            for b in range(SLOT_BLOCKS):
                nc.tensor.transpose(a[k][:, b * P : (b + 1) * P], by_slot[g, b][:, t, :], ident[:])
            nc.vector.tensor_reduce(out=neg_max[:, k : k + 1], in_=a[k][:], axis=mybir.AxisListType.X, op=ALU.max, negate=True)

        def exponents(g):
            for t in range(PACK):
                k = g * PACK + t
                nc.scalar.activation(
                    out=e[k][:], in_=a[k][:], func=ACT.Exp, bias=neg_max[:, k : k + 1], scale=1.0, accum_out=sums[g][:, t : t + 1]
                )


        g_bf = {s0: keep.tile([P, PACK, HALF], BF16, name=f"g_bf{s0}", align_bytes=64) for s0 in (EARLY, LATE)}
        g_grouped = {
            (g, s0): keep.tile([P, HALF, PACK], BF16, name=f"g_grouped{g}_{s0}", align_bytes=64) for g in range(SPANS) for s0 in (EARLY, LATE)
        }
        wy_last = keep.tile([P, PACK, N], F32, name="wy_last")
        scaled = keep.tile([P, PACK, N], F32, name="scaled", tag="w_raw2", align_bytes=64)

        def first_gradient(s0):
            slots = slice(s0, s0 + HALF)
            for t in range(PACK):
                nc.vector.scalar_tensor_tensor(
                    out=g_bf[s0][:, t, :], in0=e[t][:, slots], scalar=factor[:, t : t + 1], in1=wy[t][:, slots], op0=ALU.mult, op1=ALU.subtract
                )
            interleave(on_scalar, g_grouped[0, s0][:], g_bf[s0][:])

        def scale_last(s0):
            slots = slice(s0, s0 + HALF)
            for t in range(PACK):
                nc.vector.tensor_scalar(
                    out=scaled[:, t, slots],
                    in0=e[PACK + t][:, slots],
                    scalar1=inv[1][:, t : t + 1],
                    scalar2=weights[:, 1, t : t + 1],
                    op0=ALU.mult,
                    op1=ALU.mult,
                )

        def last_gradient(s0):
            first, second = (src[:, :, s0 : s0 + HALF].rearrange("p j (c i) -> p c j i", i=PAIR) for src in (scaled, wy_last))
            nc.vector.tensor_tensor(
                out=g_grouped[1, s0][:].rearrange("p (c i) j -> p c j i", i=PAIR), in0=first, in1=second, op=ALU.subtract
            )

        def quantize_g(g, s0):
            cols = slice(s0, s0 + HALF)
            quantize(g_codes[g][:, cols], g_scales[g][:, cols], g_grouped[g, s0][:], E5)

        m_codes = [keep.tile([P, SPANS * P], U32, name=f"m_codes{b}", align_bytes=64) for b in range(FEATURE_BLOCKS)]
        m_scales = [keep.tile([P, SPANS * P], U8, name=f"m_scales{b}", align_bytes=64) for b in range(FEATURE_BLOCKS)]
        m_bf = {}

        def cast_xm(b, copy, grouped):
            m_bf[b] = grouped
            src = m_raw[b // 2][:, :, :, b % 2 * P : (b % 2 + 1) * P]
            copy(
                out=grouped.rearrange("p (g c i) j -> p g c j i", g=SPANS, i=RUN),
                in_=src.rearrange("p g j (c i) -> p g c j i", i=RUN),
            )

        def quantize_xm(b, calls=1):
            width = SPANS * P // calls
            for n in range(calls):
                cols = slice(n * width, (n + 1) * width)
                quantize(m_codes[b][:, cols], m_scales[b][:, cols], m_bf[b][:, cols, :], E4)

        staged = {}

        def bank(columns):
            return psum.tile([P, columns], F32, name="dw", tag="side")[:]

        def product(b, s0, s1, dw):
            for g in range(SPANS):
                cols = slice(g * P, (g + 1) * P)
                matmul(dw, m_codes[b][:, cols], m_scales[b][:, cols], g_codes[g][:, s0:s1], g_scales[g][:, s0:s1], E5, g == 0, g == SPANS - 1)

        def stage(copy, dw, *halves):
            b, s0 = halves[0]
            copied = keep.tile([P, len(halves) * HALF], F32, name=f"staged{b}_{s0}", align_bytes=64)
            copy(out=copied[:], in_=dw)
            for n, half in enumerate(halves):
                staged[half] = copied[:, n * HALF : (n + 1) * HALF]

        def half_product(b, s0, copy):
            dw = bank(HALF)
            product(b, s0, s0 + HALF, dw)
            stage(copy, dw, (b, s0))

        def places(b, s0):
            return windows[b][:].indirect(offsets[:, s0 // PER_COLUMN : (s0 + HALF) // PER_COLUMN])

        def scatter_early(b):
            nc.scalar.activation(places(b, EARLY), staged[b, EARLY], ACT.Copy)

        def scatter_late_and_store(b):
            nc.vector.tensor_copy(places(b, LATE), staged[b, LATE])
            nc.sync.dma_start(out=out[b * P : (b + 1) * P, :], in_=windows[b][:])

        for h in range(PIECES):
            prepare_x(h, on_scalar if h < SPAN // PIECE else on_vector)

        scores(0, PIECE, range(last_block), add_on_scalar, "side")
        scores(PIECE, SPAN, range(last_block), add_on_scalar, "scores")
        scores(0, SPAN, [last_block], add_on_vector, "scores")
        scores(SPAN, R, [0], add_on_vector, "side")
        scores(SPAN, R, [1], add_on_scalar, "side")
        scores(SPAN, R, [2], add_on_vector, "side")
        scores(SPAN, R, [3], add_on_scalar, "side")

        for k in range(TILES - 2):
            row_max(k)
        exponents(0)
        weigh_targets_on_gpsimd(after_x, range(PACK))
        nc.vector.reciprocal(out=inv[0][:], in_=sums[0][:])
        nc.gpsimd.tensor_tensor(out=factor[:], in0=inv[0][:], in1=weights[:, 0, :], op=ALU.mult)
        weigh_targets_on_gpsimd(wy_last, range(PACK, TILES))
        for k in range(TILES - 2, TILES):
            row_max(k)
        exponents(1)

        first_gradient(EARLY)
        for places_of_pair in (slice(0, PACK // 2), slice(PACK // 2, PACK)):
            nc.vector.reciprocal(out=inv[1][:, places_of_pair], in_=sums[1][:, places_of_pair])
        scale_last(EARLY)
        last_gradient(EARLY)
        cast_xm(0, on_scalar, keep.tile([P, SPANS * P, PACK], BF16, name="m_bf0", align_bytes=64)[:])
        quantize_xm(0, SPANS)
        for g in range(SPANS):
            quantize_g(g, EARLY)
        half_product(0, EARLY, on_scalar)

        first_gradient(LATE)
        cast_xm(1, on_scalar, keep.tile([P, SPANS * P, PACK], BF16, name="m_bf1", align_bytes=64)[:])
        scale_last(LATE)
        last_gradient(LATE)
        scatter_early(0)
        for g in range(SPANS):
            quantize_g(g, LATE)
        quantize_xm(1)
        half_product(1, EARLY, on_scalar)

        cast_xm(2, on_vector, keep.tile([P, SPANS * P, PACK], BF16, name="m_bf2", tag=f"g_grouped0_{LATE}", align_bytes=64)[:])
        half_product(0, LATE, on_vector)
        quantize_xm(2)
        m_bf[3] = keep.tile([P, SPANS * P, PACK], BF16, name="m_bf3", tag=f"g_grouped0_{LATE}", align_bytes=64)[:]
        nc.gpsimd.tensor_scalar(
            out=m_bf[3].rearrange("p (g c) j -> p g c j", g=SPANS),
            in0=m_raw[1][:, :, :, P : 2 * P].rearrange("p g j c -> p g c j"),
            scalar1=1.0,
            scalar2=0.0,
            op0=ALU.mult,
            op1=ALU.add,
        )
        scatter_early(1)
        scatter_late_and_store(0)
        quantize_xm(3)

        pair = bank(N)
        product(1, LATE, N, pair[:, 0:HALF])
        product(2, EARLY, LATE, pair[:, HALF:N])
        stage(on_scalar, pair, (1, LATE), (2, EARLY))
        half_product(2, LATE, on_vector)
        scatter_late_and_store(1)
        scatter_early(2)
        product(3, 0, N, pair)
        stage(on_scalar, pair, (3, EARLY), (3, LATE))
        scatter_late_and_store(2)
        scatter_early(3)
        scatter_late_and_store(3)
